import numpy as np
import ml_dtypes


def mxq(x, axis, fmt="e4m3"):
    dtype, down = {"e4m3": (ml_dtypes.float8_e4m3fn, 7), "e5m2": (ml_dtypes.float8_e5m2, 14)}[fmt]
    v = np.moveaxis(np.asarray(x, np.float32).astype(ml_dtypes.bfloat16).astype(np.float64), axis, -1)
    blocks = v.reshape(v.shape[:-1] + (-1, 32))
    amax = np.abs(blocks).max(-1, keepdims=True)
    byte = np.maximum(np.where(amax > 0, np.frexp(amax)[1] - 1 + 127, 0) - down, 1)
    scale = np.exp2(byte - 127.0)
    codes = (blocks / scale).astype(np.float32).astype(dtype).astype(np.float64)
    return np.moveaxis((codes * scale).reshape(v.shape), -1, axis)


WIDE = False


def mx_kscale(k):
    if not WIDE:
        return np.ones(k)
    levels = np.array([10, -10, 5, -5, 0])
    if k % 512:
        return np.exp2(np.random.permutation(np.resize(levels, k // 32))).repeat(32)
    a = np.empty((k // 512, 16))
    for p in range(k // 512):
        a[p, :8] = np.random.permutation(np.resize(levels, 8))
        for g in range(8):
            far = levels[np.abs(levels - a[p, g]) >= 10]
            a[p, g + 8] = far[np.random.randint(len(far))]
    return np.exp2(a.ravel()).repeat(32)


def f64(x):
    return np.asarray(x).astype(np.float64)


def striped(idx):
    return np.tile(idx.reshape(-1, 16).T, (8, 1)).astype(np.uint16)


def unstriped(offs):
    return offs[:16].T.reshape(-1).astype(np.int64)


E2M1 = np.array([0.0, 0.5, 1.0, 1.5, 2.0, 3.0, 4.0, 6.0, -0.0, -0.5, -1.0, -1.5, -2.0, -3.0, -4.0, -6.0])


def pack_weight(w, fmt):
    k, n = w.shape
    w = f64(np.asarray(w, np.float32).astype(ml_dtypes.bfloat16)).reshape(k // 32, 32, n)
    amax = np.abs(w).max(1)
    if fmt == "e4m3":
        byte = np.frexp(amax)[1] - 1 + 127 - 7
    else:
        mant, ex = np.frexp(amax / 6.0)
        byte = np.where(mant > 0.5, ex, ex - 1) + 127
    byte = np.clip(np.where(amax > 0, byte, 1), 1, 254)
    scaled = (w * np.exp2(127.0 - byte)[:, None, :]).reshape(k, n).astype(np.float32)
    by_word = np.ascontiguousarray(scaled.reshape(k // 512, 128, 4, n).transpose(0, 1, 3, 2))
    if fmt == "e4m3":
        words = by_word.astype(ml_dtypes.float8_e4m3fn).view(np.uint8)
    else:
        c = by_word.astype(ml_dtypes.float4_e2m1fn).view(np.uint8) & 0xF
        words = (c[..., 0::2] | (c[..., 1::2] << 4)).reshape(k // 512, 128, 2 * n)
    return np.ascontiguousarray(words), np.ascontiguousarray(byte.astype(np.uint8).reshape(k // 512, 16, n))


def unpack_weight(words, scales, fmt):
    g, _, n = scales.shape
    words = np.ascontiguousarray(words).reshape(g, 128, n, -1)
    if fmt == "e4m3":
        vals = words.view(ml_dtypes.float8_e4m3fn).astype(np.float64)
    else:
        nib = np.empty((g, 128, n, 4), np.uint8)
        nib[..., 0::2] = words & 0xF
        nib[..., 1::2] = words >> 4
        vals = E2M1[nib]
    vals = vals * np.repeat(np.exp2(scales.astype(np.float64) - 127.0), 8, axis=1)[..., None]
    return vals.transpose(0, 1, 3, 2).reshape(g * 512, n)


def gelu(v):
    return 0.5 * v * (1.0 + np.tanh(np.sqrt(2.0 / np.pi) * (v + 0.044715 * v**3)))


K, T, T2, S, H, N = 512, 2048, 2048, 1024, 1024, 512

def setup_inputs():
    n = np.random.standard_normal
    s = mx_kscale(K)[:, None]
    u = mx_kscale(H)[:, None]
    tab_words, tab_scales = pack_weight(n((K, T)) * s, "e4m3")
    w1_words, w1_scales = pack_weight(n((K, H)) / np.sqrt(K) / s * u.T, "e2m1")
    w4_words, w4_scales = pack_weight(n((H, N)) / np.sqrt(2 * H) / u, "e4m3")
    perm = np.random.permutation(T2)
    return {
        "tab_words": tab_words, "tab_scales": tab_scales,
        "offs": striped(np.random.permutation(T)[:S]),
        "xT": (np.round(16 * n((K, T2))) / 16 * s).astype(np.float32),
        "offs2": striped(perm[:S]),
        "offs3": striped(perm[-S:]),
        "w1_words": w1_words, "w1_scales": w1_scales,
        "w2": (n((K, H)) / np.sqrt(2 * K) / s * u.T).astype(np.float32),
        "gain": (np.exp(0.3 * n(H)) / u[:, 0]).astype(np.float32),
        "w3": (n((H, N)) / np.sqrt(H) / u).astype(np.float32),
        "w4_words": w4_words, "w4_scales": w4_scales,
    }

def reference(tab_words, tab_scales, offs, xT, offs2, offs3, w1_words, w1_scales,
              w2, gain, w3, w4_words, w4_scales):
    v = unpack_weight(tab_words, tab_scales, "e4m3")[:, unstriped(offs)]
    w1 = unpack_weight(w1_words, w1_scales, "e2m1")
    w4 = unpack_weight(w4_words, w4_scales, "e4m3")
    x = f64(xT)[:, unstriped(offs2)] - f64(xT)[:, unstriped(offs3)]
    a = w1.T @ v
    b = mxq(f64(w2), 0, "e4m3").T @ mxq(x, 0, "e4m3")
    h = a * b * f64(gain)[:, None]
    d = a - b
    y = mxq(f64(w3), 0, "e4m3").T @ mxq(h, 0, "e4m3") + w4.T @ mxq(d, 0, "e4m3")
    return 0.5 * y * (1 + np.tanh(0.7978845608 * (y + 0.044715 * y ** 3)))

@@ -1,0 +1,264 @@
+from contextlib import ExitStack
+
+import concourse.mybir as mybir
+
+K, T, S, H, N = 512, 2048, 1024, 1024, 512
+FLOPS = 2 * S * (2 * K * H + 2 * H * N)
+
+F32 = mybir.dt.float32
+BF16 = mybir.dt.bfloat16
+I32 = mybir.dt.int32
+U32 = mybir.dt.uint32
+U16 = mybir.dt.uint16
+U8 = mybir.dt.uint8
+FP8X4 = mybir.dt.float8_e4m3fn_x4
+FP4X4 = mybir.dt.float4_e2m1fn_x4
+ALU = mybir.AluOpType
+ACT = mybir.ActivationFunctionType
+
+P = 128
+PACK = 4
+PASS = P * PACK
+R_PASSES = H // PASS
+HALF = S // 2
+SUB = 128
+CHUNKS = (256, 256, 256, 128, 128)
+ALIGN = 64
+
+
+def tile_list_photo_redshift_features_kernel(
+    tc, tab_words, tab_scales, offs, xT, offs2, offs3, w1_words, w1_scales, w2, gain, w3, w4_words, w4_scales, out
+):
+    nc = tc.nc
+    with ExitStack() as ctx:
+        keep = ctx.enter_context(tc.tile_pool(name="keep", bufs=1))
+        ring = ctx.enter_context(tc.tile_pool(name="ring", bufs=2))
+        psum = ctx.enter_context(tc.psum_pool(name="psum", bufs=1))
+
+        def kept(name, shape, dtype, tag=None):
+            return keep.tile(shape, dtype, name=name, tag=tag or name, align_bytes=ALIGN)
+
+        def load_scale_rows(queue, plane, rows):
+            for q in range(4):
+                queue.dma_start(out=plane[32 * q : 32 * q + 4].bitcast(I32), in_=rows[4 * q : 4 * q + 4].bitcast(I32))
+
+        idx1 = kept("idx1", [P, S // 16], U16)
+        idx2 = kept("idx2", [P, S // 16], U16)
+        idx3 = kept("idx3", [P, S // 16], U16)
+        tab_s = kept("tab_s", [P, T], U8)
+        tab_w = kept("tab_w", [P, T], I32, tag="slot_s")
+        w1_s = kept("w1_s", [P, H], U8)
+        w1_w = kept("w1_w", [P, 2 * H], U8)
+        w4_s = kept("w4_s", [P, R_PASSES, N], U8)
+        w4_w = kept("w4_w", [P, R_PASSES, N], I32)
+        gains = kept("gains", [P, R_PASSES, PACK], F32)
+        planes = [kept("plane%d" % i, [P, T], F32) for i in range(PACK)]
+        x_rows = xT.rearrange("(p i) t -> i p t", i=PACK)
+
+        nc.vector.memset(tab_s[:].bitcast(I32), 0)
+        nc.vector.memset(w1_s[:].bitcast(I32), 0)
+        nc.gpsimd.memset(w4_s[:].rearrange("p a c -> p (a c)").bitcast(I32), 0)
+
+        nc.scalar.dma_start(out=gains[:], in_=gain.rearrange("(g p t) -> p g t", g=R_PASSES, t=PACK))
+        nc.sync.dma_start(out=w1_w[:].bitcast(I32), in_=w1_words[0].bitcast(I32))
+        nc.sync.dma_start(idx1[:], offs)
+        load_scale_rows(nc.sync, tab_s, tab_scales[0])
+        nc.sync.dma_start(out=tab_w[:], in_=tab_words[0].rearrange("p t i -> p (t i)").bitcast(I32))
+        nc.sync.dma_start(out=planes[0][:], in_=x_rows[0])
+        load_scale_rows(nc.sync, w1_s, w1_scales[0])
+        nc.sync.dma_start(idx3[:], offs3)
+
+        v_w = kept("v_w", [P, S], U32)
+        v_s = kept("v_s", [P, S], U8)
+        nc.vector.tensor_copy(v_s[:], tab_s[:].indirect(idx1[:]))
+        nc.vector.tensor_copy(v_w[:], tab_w[:].bitcast(U32).indirect(idx1[:]))
+
+        w2_raw = [kept("w2_raw%d" % g, [P, PACK, PASS], F32) for g in range(R_PASSES)]
+        w3_raw = [kept("w3_raw%d" % g, [P, PACK, N], F32, tag=("slot_r", "slot_s")[g]) for g in range(R_PASSES)]
+        for g in range(R_PASSES):
+            nc.sync.dma_start(
+                out=w2_raw[g][:], in_=w2[:, g * PASS : (g + 1) * PASS].rearrange("(p i) r -> p i r", i=PACK)
+            )
+            if g == 0:
+                nc.sync.dma_start(idx2[:], offs2)
+            nc.sync.dma_start(out=planes[1 + g][:], in_=x_rows[1 + g])
+        nc.sync.dma_start(out=w3_raw[0][:], in_=w3[0:PASS, :].rearrange("(p i) n -> p i n", i=PACK))
+        nc.sync.dma_start(out=planes[3][:], in_=x_rows[3])
+        nc.sync.dma_start(out=w3_raw[1][:], in_=w3[PASS : 2 * PASS, :].rearrange("(p i) n -> p i n", i=PACK))
+        nc.sync.dma_start(out=w4_w[:], in_=w4_words.rearrange("a p c i -> p a (c i)").bitcast(I32))
+        load_scale_rows(nc.sync, w4_s, w4_scales.rearrange("a q c -> q a c"))
+
+        w1_wo = kept("w1_wo", [P, 2 * H], U8)
+        w1_so = kept("w1_so", [P, H], U8)
+        nc.vector.tensor_copy(
+            w1_wo[:].bitcast(U16).rearrange("p (g t m) -> p g t m", g=R_PASSES, t=PACK),
+            w1_w[:].bitcast(U16).rearrange("p (g m t) -> p g t m", g=R_PASSES, t=PACK),
+        )
+        nc.vector.tensor_copy(
+            w1_so[:].rearrange("p (g t m) -> p g t m", g=R_PASSES, t=PACK),
+            w1_s[:].rearrange("p (g m t) -> p g t m", g=R_PASSES, t=PACK),
+        )
+
+        a_plain, a_gained = {}, {}
+
+        def template_product(half, g):
+            plain = kept("a_plain%d%d" % (half, g), [P, PACK, HALF], F32)
+            gained = kept("a_gained%d%d" % (half, g), [P, PACK, HALF], F32)
+            cols = slice(half * HALF, (half + 1) * HALF)
+            for t in range(PACK):
+                r0 = g * PASS + t * P
+                bank = psum.tile([P, HALF], F32, name="a_bank", tag="a_bank", bufs=2)
+                nc.tensor.matmul_mx(
+                    out=bank[:],
+                    lhsT=w1_wo[:, 2 * r0 : 2 * (r0 + P)].bitcast(FP4X4),
+                    lhsT_scale=w1_so[:, r0 : r0 + P],
+                    rhs=v_w[:, cols].bitcast(FP8X4),
+                    rhs_scale=v_s[:, cols],
+                    start=True,
+                    stop=True,
+                )
+                nc.scalar.copy(plain[:, t, :], bank[:])
+                nc.scalar.activation(gained[:, t, :], bank[:], ACT.Copy, scale=gains[:, g, t : t + 1])
+            a_plain[half, g], a_gained[half, g] = plain, gained
+
+        def quantize(name, grouped, width):
+            codes = kept(name + "_w", [P, width], U32)
+            scales = kept(name + "_s", [P, width], U8)
+            nc.vector.quantize_mx(
+                out=codes[:].bitcast(FP8X4), scales=scales[:], in_=grouped[:].rearrange("p c i -> p (c i)")
+            )
+            return codes, scales
+
+        def interleave(grouped, rows):
+            nc.scalar.copy(
+                grouped[:].rearrange("p (c e) i -> p c i e", e=2), rows[:].rearrange("p i (c e) -> p c i e", e=2)
+            )
+
+        colours = [kept("colour%d" % half, [P, PACK, HALF], F32) for half in range(2)]
+
+        def gather_plane(i):
+            picked = []
+            for half in range(2):
+                second = ring.tile([P, HALF], F32, name="second", tag="second", bufs=3)
+                cols = slice(half * HALF // 16, (half + 1) * HALF // 16)
+                nc.vector.tensor_copy(second[:], planes[i][:].indirect(idx3[:, cols]))
+                picked.append((second, cols))
+            for half, (second, cols) in enumerate(picked):
+                nc.vector.tensor_tensor(
+                    colours[half][:, i, :], planes[i][:].indirect(idx2[:, cols]), second[:], ALU.subtract
+                )
+
+        def round_w2(g):
+            grouped = ring.tile([P, PASS, PACK], BF16, name="w_grouped", tag="w_grouped", align_bytes=ALIGN)
+            nc.scalar.copy(
+                grouped[:].rearrange("p (t m) i -> p m t i", t=PACK),
+                w2_raw[g][:].rearrange("p i (m t) -> p m t i", t=PACK),
+            )
+            return quantize("w2q%d" % g, grouped, PASS)
+
+        def round_w3(g):
+            grouped = ring.tile([P, N, PACK], BF16, name="w_grouped", tag="w_grouped", align_bytes=ALIGN)
+            interleave(grouped, w3_raw[g])
+            return quantize("w3q%d" % g, grouped, N)
+
+        def round_x(half):
+            grouped = kept("x_grouped%d" % half, [P, HALF, PACK], BF16, tag=("slot_r", "slot_s")[half])
+            interleave(grouped, colours[half])
+            return quantize("xq%d" % half, grouped, HALF)
+
+        gather_plane(0)
+        template_product(0, 0)
+        w2q = [round_w2(0)]
+        gather_plane(1)
+        template_product(0, 1)
+        w2q.append(round_w2(1))
+        gather_plane(2)
+        gather_plane(3)
+        w3q = [round_w3(0)]
+        xq = [round_x(0)]
+        w3q.append(round_w3(1))
+        xq.append(round_x(1))
+
+        def meet(j0, width, g):
+            half, c0 = divmod(j0, HALF)
+            grouped = ring.tile([P, 2 * width, PACK], BF16, name="hd", tag="hd", bufs=3, align_bytes=ALIGN)
+            for s0 in range(0, width, SUB):
+                cols = slice(c0 + s0, c0 + s0 + SUB)
+                bank = psum.tile([P, PACK, SUB], F32, name="b_bank", tag="b_bank", bufs=3)
+                for t in range(PACK):
+                    nc.tensor.matmul_mx(
+                        out=bank[:, t, :],
+                        lhsT=w2q[g][0][:, t * P : (t + 1) * P].bitcast(FP8X4),
+                        lhsT_scale=w2q[g][1][:, t * P : (t + 1) * P],
+                        rhs=xq[half][0][:, cols].bitcast(FP8X4),
+                        rhs_scale=xq[half][1][:, cols],
+                        start=True,
+                        stop=True,
+                    )
+                b = bank[:].rearrange("p t (c e) -> p c t e", e=2)
+                nc.vector.tensor_tensor(
+                    grouped[:, s0 : s0 + SUB, :].rearrange("p (c e) t -> p c t e", e=2),
+                    a_gained[half, g][:, :, cols].rearrange("p t (c e) -> p c t e", e=2),
+                    b,
+                    ALU.mult,
+                )
+                nc.vector.tensor_tensor(
+                    grouped[:, width + s0 : width + s0 + SUB, :].rearrange("p (c e) t -> p c t e", e=2),
+                    a_plain[half, g][:, :, cols].rearrange("p t (c e) -> p c t e", e=2),
+                    b,
+                    ALU.subtract,
+                )
+            return grouped
+
+        y_banks = {}
+
+        def second_stage(j0, width, g, grouped):
+            codes = ring.tile([P, 2 * width], U32, name="hd_w", tag="hd_w", bufs=3, align_bytes=ALIGN)
+            scales = ring.tile([P, 2 * width], U8, name="hd_s", tag="hd_s", bufs=3, align_bytes=ALIGN)
+            nc.vector.quantize_mx(
+                out=codes[:].bitcast(FP8X4), scales=scales[:], in_=grouped[:].rearrange("p c t -> p (c t)")
+            )
+            tiles_a_bank = 512 // width
+            for n0 in range(0, N // P, tiles_a_bank):
+                if g == 0:
+                    y_banks[j0, n0] = psum.tile([P, tiles_a_bank, width], F32, name="y_bank", tag="y_bank", bufs=3)
+                bank = y_banks[j0, n0]
+                for n in range(tiles_a_bank):
+                    rows = slice((n0 + n) * P, (n0 + n + 1) * P)
+                    nc.tensor.matmul_mx(
+                        out=bank[:, n, :],
+                        lhsT=w3q[g][0][:, rows].bitcast(FP8X4),
+                        lhsT_scale=w3q[g][1][:, rows],
+                        rhs=codes[:, 0:width].bitcast(FP8X4),
+                        rhs_scale=scales[:, 0:width],
+                        start=(g == 0 and n == 0),
+                        stop=False,
+                    )
+                    nc.tensor.matmul_mx(
+                        out=bank[:, n, :],
+                        lhsT=w4_w[:, g, rows].bitcast(FP8X4),
+                        lhsT_scale=w4_s[:, g, rows],
+                        rhs=codes[:, width : 2 * width].bitcast(FP8X4),
+                        rhs_scale=scales[:, width : 2 * width],
+                        start=False,
+                        stop=(g == R_PASSES - 1 and n == tiles_a_bank - 1),
+                    )
+                if g == R_PASSES - 1:
+                    result = ring.tile([P, tiles_a_bank, width], F32, name="result", tag="result", bufs=3)
+                    nc.scalar.activation(result[:], bank[:], ACT.Gelu_apprx_tanh)
+                    nc.sync.dma_start(
+                        out=out[n0 * P : (n0 + tiles_a_bank) * P, j0 : j0 + width].rearrange("(n p) j -> p n j", p=P),
+                        in_=result[:],
+                    )
+
+        starts = [sum(CHUNKS[:c]) for c in range(len(CHUNKS))]
+        steps = [(j0, width, g) for j0, width in zip(starts, CHUNKS) for g in range(R_PASSES)]
+        waiting = None
+        for number, step in enumerate(steps):
+            if number < R_PASSES:
+                template_product(1, number)
+            grouped = meet(*step)
+            if waiting is not None:
+                second_stage(*waiting)
+            waiting = step + (grouped,)
+        second_stage(*waiting)

@@ -23,6 +23,8 @@ R_PASSES = H // PASS
 HALF = S // 2
 SUB = 128
 CHUNKS = (256, 256, 256, 128, 128)
+QUARTER = S // 4
+SUMMED_FROM = (S - SUB, S - 2 * SUB)
 ALIGN = 64
 
 
@@ -66,7 +68,12 @@ def tile_list_photo_redshift_features_kernel(
         nc.sync.dma_start(out=tab_w[:], in_=tab_words[0].rearrange("p t i -> p (t i)").bitcast(I32))
         nc.sync.dma_start(out=planes[0][:], in_=x_rows[0])
         load_scale_rows(nc.sync, w1_s, w1_scales[0])
-        nc.sync.dma_start(idx3[:], offs3)
+        nc.sync.dma_start(idx2[:], offs2)
+
+        warm = kept("warm", [P, R_PASSES, PACK], F32)
+        nc.scalar.activation(warm[:], gains[:], ACT.Gelu_apprx_tanh)
+        minus_gains = kept("minus_gains", [P, R_PASSES, PACK], F32)
+        nc.scalar.activation(minus_gains[:], gains[:], ACT.Copy, scale=-1.0)
 
         v_w = kept("v_w", [P, S], U32)
         v_s = kept("v_s", [P, S], U8)
@@ -80,7 +87,7 @@ def tile_list_photo_redshift_features_kernel(
                 out=w2_raw[g][:], in_=w2[:, g * PASS : (g + 1) * PASS].rearrange("(p i) r -> p i r", i=PACK)
             )
             if g == 0:
-                nc.sync.dma_start(idx2[:], offs2)
+                nc.sync.dma_start(idx3[:], offs3)
             nc.sync.dma_start(out=planes[1 + g][:], in_=x_rows[1 + g])
         nc.sync.dma_start(out=w3_raw[0][:], in_=w3[0:PASS, :].rearrange("(p i) n -> p i n", i=PACK))
         nc.sync.dma_start(out=planes[3][:], in_=x_rows[3])
@@ -105,6 +112,7 @@ def tile_list_photo_redshift_features_kernel(
             plain = kept("a_plain%d%d" % (half, g), [P, PACK, HALF], F32)
             gained = kept("a_gained%d%d" % (half, g), [P, PACK, HALF], F32)
             cols = slice(half * HALF, (half + 1) * HALF)
+            needed = min(HALF, SUMMED_FROM[g] - half * HALF)
             for t in range(PACK):
                 r0 = g * PASS + t * P
                 bank = psum.tile([P, HALF], F32, name="a_bank", tag="a_bank", bufs=2)
@@ -117,8 +125,8 @@ def tile_list_photo_redshift_features_kernel(
                     start=True,
                     stop=True,
                 )
-                nc.scalar.copy(plain[:, t, :], bank[:])
-                nc.scalar.activation(gained[:, t, :], bank[:], ACT.Copy, scale=gains[:, g, t : t + 1])
+                nc.scalar.activation(gained[:, t, :], bank[:], ACT.Copy, scale=minus_gains[:, g, t : t + 1])
+                nc.scalar.copy(plain[:, t, 0:needed], bank[:, 0:needed])
             a_plain[half, g], a_gained[half, g] = plain, gained
 
         def quantize(name, grouped, width):
@@ -131,22 +139,28 @@ def tile_list_photo_redshift_features_kernel(
 
         def interleave(grouped, rows):
             nc.scalar.copy(
-                grouped[:].rearrange("p (c e) i -> p c i e", e=2), rows[:].rearrange("p i (c e) -> p c i e", e=2)
+                grouped.rearrange("p (c e) i -> p c i e", e=2), rows.rearrange("p i (c e) -> p c i e", e=2)
             )
 
         colours = [kept("colour%d" % half, [P, PACK, HALF], F32) for half in range(2)]
 
-        def gather_plane(i):
-            picked = []
-            for half in range(2):
-                second = ring.tile([P, HALF], F32, name="second", tag="second", bufs=3)
-                cols = slice(half * HALF // 16, (half + 1) * HALF // 16)
-                nc.vector.tensor_copy(second[:], planes[i][:].indirect(idx3[:, cols]))
-                picked.append((second, cols))
-            for half, (second, cols) in enumerate(picked):
+        def gather_plane(i, width):
+            def pick(j0):
+                first = ring.tile([P, width], F32, name="first", tag="first", bufs=3)
+                nc.vector.tensor_copy(first[:], planes[i][:].indirect(idx2[:, j0 // 16 : (j0 + width) // 16]))
+                return first
+
+            picked = pick(0)
+            for j0 in range(0, S, width):
+                ahead = pick(j0 + width) if j0 + width < S else None
+                half, c0 = divmod(j0, HALF)
                 nc.vector.tensor_tensor(
-                    colours[half][:, i, :], planes[i][:].indirect(idx2[:, cols]), second[:], ALU.subtract
+                    colours[half][:, i, c0 : c0 + width],
+                    planes[i][:].indirect(idx3[:, j0 // 16 : (j0 + width) // 16]),
+                    picked[:],
+                    ALU.subtract,
                 )
+                picked = ahead
 
         def round_w2(g):
             grouped = ring.tile([P, PASS, PACK], BF16, name="w_grouped", tag="w_grouped", align_bytes=ALIGN)
@@ -158,43 +172,70 @@ def tile_list_photo_redshift_features_kernel(
 
         def round_w3(g):
             grouped = ring.tile([P, N, PACK], BF16, name="w_grouped", tag="w_grouped", align_bytes=ALIGN)
-            interleave(grouped, w3_raw[g])
+            interleave(grouped[:], w3_raw[g][:])
             return quantize("w3q%d" % g, grouped, N)
 
-        def round_x(half):
-            grouped = kept("x_grouped%d" % half, [P, HALF, PACK], BF16, tag=("slot_r", "slot_s")[half])
-            interleave(grouped, colours[half])
-            return quantize("xq%d" % half, grouped, HALF)
+        def round_x(quarter):
+            half, c0 = divmod(quarter * QUARTER, HALF)
+            tag = ("slot_r", "x_grouped1", "slot_s", "x_grouped3")[quarter]
+            grouped = kept("x_grouped%d" % quarter, [P, QUARTER, PACK], BF16, tag=tag)
+            interleave(grouped[:], colours[half][:, :, c0 : c0 + QUARTER])
+            return quantize("xq%d" % quarter, grouped, QUARTER)
 
-        gather_plane(0)
+        gather_plane(0, HALF)
         template_product(0, 0)
         w2q = [round_w2(0)]
-        gather_plane(1)
+        gather_plane(1, HALF)
         template_product(0, 1)
         w2q.append(round_w2(1))
-        gather_plane(2)
-        gather_plane(3)
+        gather_plane(2, HALF)
+        gather_plane(3, QUARTER)
         w3q = [round_w3(0)]
-        xq = [round_x(0)]
+        xq = [round_x(0), round_x(1)]
         w3q.append(round_w3(1))
-        xq.append(round_x(1))
+        xq.extend([round_x(2), round_x(3)])
+
+        def colour_pass(bank, j, g, t, start):
+            quarter, c0 = divmod(j, QUARTER)
+            nc.tensor.matmul_mx(
+                out=bank[:, t, :],
+                lhsT=w2q[g][0][:, t * P : (t + 1) * P].bitcast(FP8X4),
+                lhsT_scale=w2q[g][1][:, t * P : (t + 1) * P],
+                rhs=xq[quarter][0][:, c0 : c0 + SUB].bitcast(FP8X4),
+                rhs_scale=xq[quarter][1][:, c0 : c0 + SUB],
+                start=start,
+                stop=True,
+            )
+
+        def residual_in_psum(j0, g):
+            bank = psum.tile([P, PACK, SUB], F32, name="a_bank", tag="a_bank", bufs=2)
+            for t in range(PACK):
+                r0 = g * PASS + t * P
+                nc.tensor.matmul_mx(
+                    out=bank[:, t, :],
+                    lhsT=w1_wo[:, 2 * r0 : 2 * (r0 + P)].bitcast(FP4X4),
+                    lhsT_scale=w1_so[:, r0 : r0 + P],
+                    rhs=v_w[:, j0 : j0 + SUB].bitcast(FP8X4),
+                    rhs_scale=v_s[:, j0 : j0 + SUB],
+                    start=True,
+                    stop=False,
+                )
+                colour_pass(bank, j0, g, t, False)
+            grouped = kept("d_grouped%d_%d" % (j0, g), [P, SUB, PACK], BF16)
+            interleave(grouped[:], bank[:])
+            return quantize("dq%d_%d" % (j0, g), grouped, SUB)
 
         def meet(j0, width, g):
             half, c0 = divmod(j0, HALF)
-            grouped = ring.tile([P, 2 * width, PACK], BF16, name="hd", tag="hd", bufs=3, align_bytes=ALIGN)
+            summed = j0 >= SUMMED_FROM[g]
+            grouped = ring.tile(
+                [P, width if summed else 2 * width, PACK], BF16, name="hd", tag="hd", bufs=3, align_bytes=ALIGN
+            )
             for s0 in range(0, width, SUB):
                 cols = slice(c0 + s0, c0 + s0 + SUB)
                 bank = psum.tile([P, PACK, SUB], F32, name="b_bank", tag="b_bank", bufs=3)
                 for t in range(PACK):
-                    nc.tensor.matmul_mx(
-                        out=bank[:, t, :],
-                        lhsT=w2q[g][0][:, t * P : (t + 1) * P].bitcast(FP8X4),
-                        lhsT_scale=w2q[g][1][:, t * P : (t + 1) * P],
-                        rhs=xq[half][0][:, cols].bitcast(FP8X4),
-                        rhs_scale=xq[half][1][:, cols],
-                        start=True,
-                        stop=True,
-                    )
+                    colour_pass(bank, j0 + s0, g, t, True)
                 b = bank[:].rearrange("p t (c e) -> p c t e", e=2)
                 nc.vector.tensor_tensor(
                     grouped[:, s0 : s0 + SUB, :].rearrange("p (c e) t -> p c t e", e=2),
@@ -202,48 +243,36 @@ def tile_list_photo_redshift_features_kernel(
                     b,
                     ALU.mult,
                 )
-                nc.vector.tensor_tensor(
-                    grouped[:, width + s0 : width + s0 + SUB, :].rearrange("p (c e) t -> p c t e", e=2),
-                    a_plain[half, g][:, :, cols].rearrange("p t (c e) -> p c t e", e=2),
-                    b,
-                    ALU.subtract,
-                )
+                if not summed:
+                    nc.vector.tensor_tensor(
+                        grouped[:, width + s0 : width + s0 + SUB, :].rearrange("p (c e) t -> p c t e", e=2),
+                        a_plain[half, g][:, :, cols].rearrange("p t (c e) -> p c t e", e=2),
+                        b,
+                        ALU.add,
+                    )
             return grouped
 
         y_banks = {}
 
-        def second_stage(j0, width, g, grouped):
-            codes = ring.tile([P, 2 * width], U32, name="hd_w", tag="hd_w", bufs=3, align_bytes=ALIGN)
-            scales = ring.tile([P, 2 * width], U8, name="hd_s", tag="hd_s", bufs=3, align_bytes=ALIGN)
-            nc.vector.quantize_mx(
-                out=codes[:].bitcast(FP8X4), scales=scales[:], in_=grouped[:].rearrange("p c t -> p (c t)")
-            )
-            tiles_a_bank = 512 // width
+        def y_passes(j0, width, weights, operand, last):
+            tiles_a_bank = 2 if j0 + width == S else 512 // width
             for n0 in range(0, N // P, tiles_a_bank):
-                if g == 0:
+                first = (j0, n0) not in y_banks
+                if first:
                     y_banks[j0, n0] = psum.tile([P, tiles_a_bank, width], F32, name="y_bank", tag="y_bank", bufs=3)
                 bank = y_banks[j0, n0]
                 for n in range(tiles_a_bank):
                     rows = slice((n0 + n) * P, (n0 + n + 1) * P)
                     nc.tensor.matmul_mx(
                         out=bank[:, n, :],
-                        lhsT=w3q[g][0][:, rows].bitcast(FP8X4),
-                        lhsT_scale=w3q[g][1][:, rows],
-                        rhs=codes[:, 0:width].bitcast(FP8X4),
-                        rhs_scale=scales[:, 0:width],
-                        start=(g == 0 and n == 0),
-                        stop=False,
+                        lhsT=weights[0][:, rows].bitcast(FP8X4),
+                        lhsT_scale=weights[1][:, rows],
+                        rhs=operand[0].bitcast(FP8X4),
+                        rhs_scale=operand[1],
+                        start=(first and n == 0),
+                        stop=(last and n == tiles_a_bank - 1),
                     )
-                    nc.tensor.matmul_mx(
-                        out=bank[:, n, :],
-                        lhsT=w4_w[:, g, rows].bitcast(FP8X4),
-                        lhsT_scale=w4_s[:, g, rows],
-                        rhs=codes[:, width : 2 * width].bitcast(FP8X4),
-                        rhs_scale=scales[:, width : 2 * width],
-                        start=False,
-                        stop=(g == R_PASSES - 1 and n == tiles_a_bank - 1),
-                    )
-                if g == R_PASSES - 1:
+                if last:
                     result = ring.tile([P, tiles_a_bank, width], F32, name="result", tag="result", bufs=3)
                     nc.scalar.activation(result[:], bank[:], ACT.Gelu_apprx_tanh)
                     nc.sync.dma_start(
@@ -251,12 +280,34 @@ def tile_list_photo_redshift_features_kernel(
                         in_=result[:],
                     )
 
+        def second_stage(j0, width, g, grouped):
+            if g == 0:
+                for gs in range(R_PASSES):
+                    if j0 >= SUMMED_FROM[gs]:
+                        d_codes, d_scales = residuals[j0, gs]
+                        y_passes(j0, width, (w4_w[:, gs, :], w4_s[:, gs, :]), (d_codes[:], d_scales[:]), False)
+            summed = j0 >= SUMMED_FROM[g]
+            columns = width if summed else 2 * width
+            codes = ring.tile([P, columns], U32, name="hd_w", tag="hd_w", bufs=3, align_bytes=ALIGN)
+            scales = ring.tile([P, columns], U8, name="hd_s", tag="hd_s", bufs=3, align_bytes=ALIGN)
+            nc.vector.quantize_mx(
+                out=codes[:].bitcast(FP8X4), scales=scales[:], in_=grouped[:].rearrange("p c t -> p (c t)")
+            )
+            if not summed:
+                d_op = (codes[:, width:columns], scales[:, width:columns])
+                y_passes(j0, width, (w4_w[:, g, :], w4_s[:, g, :]), d_op, False)
+            y_passes(j0, width, w3q[g], (codes[:, 0:width], scales[:, 0:width]), g == R_PASSES - 1)
+
         starts = [sum(CHUNKS[:c]) for c in range(len(CHUNKS))]
         steps = [(j0, width, g) for j0, width in zip(starts, CHUNKS) for g in range(R_PASSES)]
         waiting = None
+        residuals = {}
         for number, step in enumerate(steps):
             if number < R_PASSES:
                 template_product(1, number)
+            for j0, width, g in steps[number + 1 : number + 3]:
+                if j0 >= SUMMED_FROM[g] and (j0, g) not in residuals:
+                    residuals[j0, g] = residual_in_psum(j0, g)
             grouped = meet(*step)
             if waiting is not None:
                 second_stage(*waiting)

@@ -142,7 +142,7 @@ def tile_list_photo_redshift_features_kernel(
                 grouped.rearrange("p (c e) i -> p c i e", e=2), rows.rearrange("p i (c e) -> p c i e", e=2)
             )
 
-        colours = [kept("colour%d" % half, [P, PACK, HALF], F32) for half in range(2)]
+        colours = kept("colours", [P, PACK, S], F32)
 
         def gather_plane(i, width):
             def pick(j0):
@@ -153,9 +153,8 @@ def tile_list_photo_redshift_features_kernel(
             picked = pick(0)
             for j0 in range(0, S, width):
                 ahead = pick(j0 + width) if j0 + width < S else None
-                half, c0 = divmod(j0, HALF)
                 nc.vector.tensor_tensor(
-                    colours[half][:, i, c0 : c0 + width],
+                    colours[:, i, j0 : j0 + width],
                     planes[i][:].indirect(idx3[:, j0 // 16 : (j0 + width) // 16]),
                     picked[:],
                     ALU.subtract,
@@ -176,10 +175,9 @@ def tile_list_photo_redshift_features_kernel(
             return quantize("w3q%d" % g, grouped, N)
 
         def round_x(quarter):
-            half, c0 = divmod(quarter * QUARTER, HALF)
             tag = ("slot_r", "x_grouped1", "slot_s", "x_grouped3")[quarter]
             grouped = kept("x_grouped%d" % quarter, [P, QUARTER, PACK], BF16, tag=tag)
-            interleave(grouped[:], colours[half][:, :, c0 : c0 + QUARTER])
+            interleave(grouped[:], colours[:, :, quarter * QUARTER : (quarter + 1) * QUARTER])
             return quantize("xq%d" % quarter, grouped, QUARTER)
 
         gather_plane(0, HALF)
@@ -259,7 +257,8 @@ def tile_list_photo_redshift_features_kernel(
             for n0 in range(0, N // P, tiles_a_bank):
                 first = (j0, n0) not in y_banks
                 if first:
-                    y_banks[j0, n0] = psum.tile([P, tiles_a_bank, width], F32, name="y_bank", tag="y_bank", bufs=3)
+                    tag, bufs = ("a_bank", 2) if j0 + width == S else ("y_bank", 3)
+                    y_banks[j0, n0] = psum.tile([P, tiles_a_bank, width], F32, name="y_bank", tag=tag, bufs=bufs)
                 bank = y_banks[j0, n0]
                 for n in range(tiles_a_bank):
                     rows = slice((n0 + n) * P, (n0 + n + 1) * P)
@@ -273,7 +272,7 @@ def tile_list_photo_redshift_features_kernel(
                         stop=(last and n == tiles_a_bank - 1),
                     )
                 if last:
-                    result = ring.tile([P, tiles_a_bank, width], F32, name="result", tag="result", bufs=3)
+                    result = ring.tile([P, tiles_a_bank, width], F32, name="result", tag="result", bufs=5)
                     nc.scalar.activation(result[:], bank[:], ACT.Gelu_apprx_tanh)
                     nc.sync.dma_start(
                         out=out[n0 * P : (n0 + tiles_a_bank) * P, j0 : j0 + width].rearrange("(n p) j -> p n j", p=P),

@@ -22,7 +22,8 @@ PASS = P * PACK
 R_PASSES = H // PASS
 HALF = S // 2
 SUB = 128
-CHUNKS = (256, 256, 256, 128, 128)
+WIDE = 2 * SUB
+WIDE_END = S - 2 * SUB
 QUARTER = S // 4
 SUMMED_FROM = (S - SUB, S - 2 * SUB)
 ALIGN = 64
@@ -49,7 +50,7 @@ def tile_list_photo_redshift_features_kernel(
         idx3 = kept("idx3", [P, S // 16], U16)
         tab_s = kept("tab_s", [P, T], U8)
         tab_w = kept("tab_w", [P, T], I32, tag="slot_s")
-        w1_s = kept("w1_s", [P, H], U8)
+        w1_s = kept("w1_s", [P, H], U8, tag="slot_v")
         w1_w = kept("w1_w", [P, 2 * H], U8)
         w4_s = kept("w4_s", [P, R_PASSES, N], U8)
         w4_w = kept("w4_w", [P, R_PASSES, N], I32)
@@ -66,74 +67,90 @@ def tile_list_photo_redshift_features_kernel(
         nc.sync.dma_start(idx1[:], offs)
         load_scale_rows(nc.sync, tab_s, tab_scales[0])
         nc.sync.dma_start(out=tab_w[:], in_=tab_words[0].rearrange("p t i -> p (t i)").bitcast(I32))
-        nc.sync.dma_start(out=planes[0][:], in_=x_rows[0])
         load_scale_rows(nc.sync, w1_s, w1_scales[0])
+        nc.sync.dma_start(out=planes[0][:], in_=x_rows[0])
         nc.sync.dma_start(idx2[:], offs2)
+        nc.sync.dma_start(idx3[:], offs3)
 
-        warm = kept("warm", [P, R_PASSES, PACK], F32)
-        nc.scalar.activation(warm[:], gains[:], ACT.Gelu_apprx_tanh)
         minus_gains = kept("minus_gains", [P, R_PASSES, PACK], F32)
         nc.scalar.activation(minus_gains[:], gains[:], ACT.Copy, scale=-1.0)
 
-        v_w = kept("v_w", [P, S], U32)
         v_s = kept("v_s", [P, S], U8)
         nc.vector.tensor_copy(v_s[:], tab_s[:].indirect(idx1[:]))
-        nc.vector.tensor_copy(v_w[:], tab_w[:].bitcast(U32).indirect(idx1[:]))
-
-        w2_raw = [kept("w2_raw%d" % g, [P, PACK, PASS], F32) for g in range(R_PASSES)]
-        w3_raw = [kept("w3_raw%d" % g, [P, PACK, N], F32, tag=("slot_r", "slot_s")[g]) for g in range(R_PASSES)]
-        for g in range(R_PASSES):
-            nc.sync.dma_start(
-                out=w2_raw[g][:], in_=w2[:, g * PASS : (g + 1) * PASS].rearrange("(p i) r -> p i r", i=PACK)
-            )
-            if g == 0:
-                nc.sync.dma_start(idx3[:], offs3)
-            nc.sync.dma_start(out=planes[1 + g][:], in_=x_rows[1 + g])
-        nc.sync.dma_start(out=w3_raw[0][:], in_=w3[0:PASS, :].rearrange("(p i) n -> p i n", i=PACK))
-        nc.sync.dma_start(out=planes[3][:], in_=x_rows[3])
-        nc.sync.dma_start(out=w3_raw[1][:], in_=w3[PASS : 2 * PASS, :].rearrange("(p i) n -> p i n", i=PACK))
-        nc.sync.dma_start(out=w4_w[:], in_=w4_words.rearrange("a p c i -> p a (c i)").bitcast(I32))
-        load_scale_rows(nc.sync, w4_s, w4_scales.rearrange("a q c -> q a c"))
-
         w1_wo = kept("w1_wo", [P, 2 * H], U8)
         w1_so = kept("w1_so", [P, H], U8)
         nc.vector.tensor_copy(
             w1_wo[:].bitcast(U16).rearrange("p (g t m) -> p g t m", g=R_PASSES, t=PACK),
             w1_w[:].bitcast(U16).rearrange("p (g m t) -> p g t m", g=R_PASSES, t=PACK),
         )
+        v_w = [kept("v_w0", [P, HALF], U32)]
+        nc.vector.tensor_copy(v_w[0][:], tab_w[:].bitcast(U32).indirect(idx1[:, 0 : HALF // 16]))
         nc.vector.tensor_copy(
             w1_so[:].rearrange("p (g t m) -> p g t m", g=R_PASSES, t=PACK),
             w1_s[:].rearrange("p (g m t) -> p g t m", g=R_PASSES, t=PACK),
         )
+        v_w.append(kept("v_w1", [P, HALF], U32, tag="slot_v"))
+        nc.vector.tensor_copy(v_w[1][:], tab_w[:].bitcast(U32).indirect(idx1[:, HALF // 16 : S // 16]))
+
+        w2_raw = [kept("w2_raw%d" % g, [P, PACK, PASS], F32) for g in range(R_PASSES)]
+        w3_raw = [kept("w3_raw%d" % g, [P, PACK, N], F32, tag=("w3_raw0", "slot_s")[g]) for g in range(R_PASSES)]
+        for g in range(R_PASSES):
+            nc.sync.dma_start(
+                out=w2_raw[g][:], in_=w2[:, g * PASS : (g + 1) * PASS].rearrange("(p i) r -> p i r", i=PACK)
+            )
+            nc.sync.dma_start(out=planes[1 + g][:], in_=x_rows[1 + g])
+        nc.sync.dma_start(out=planes[3][:], in_=x_rows[3])
+        for g in range(R_PASSES):
+            nc.sync.dma_start(
+                out=w3_raw[g][:], in_=w3[g * PASS : (g + 1) * PASS, :].rearrange("(p i) n -> p i n", i=PACK)
+            )
+        nc.sync.dma_start(out=w4_w[:], in_=w4_words.rearrange("a p c i -> p a (c i)").bitcast(I32))
+        load_scale_rows(nc.sync, w4_s, w4_scales.rearrange("a q c -> q a c"))
+
+        def on_gpsimd(j):
+            return j < WIDE_END and j % WIDE == 0
 
         a_plain, a_gained = {}, {}
 
-        def template_product(half, g):
-            plain = kept("a_plain%d%d" % (half, g), [P, PACK, HALF], F32)
-            gained = kept("a_gained%d%d" % (half, g), [P, PACK, HALF], F32)
-            cols = slice(half * HALF, (half + 1) * HALF)
-            needed = min(HALF, SUMMED_FROM[g] - half * HALF)
-            for t in range(PACK):
-                r0 = g * PASS + t * P
-                bank = psum.tile([P, HALF], F32, name="a_bank", tag="a_bank", bufs=2)
-                nc.tensor.matmul_mx(
-                    out=bank[:],
-                    lhsT=w1_wo[:, 2 * r0 : 2 * (r0 + P)].bitcast(FP4X4),
-                    lhsT_scale=w1_so[:, r0 : r0 + P],
-                    rhs=v_w[:, cols].bitcast(FP8X4),
-                    rhs_scale=v_s[:, cols],
-                    start=True,
-                    stop=True,
-                )
-                nc.scalar.activation(gained[:, t, :], bank[:], ACT.Copy, scale=minus_gains[:, g, t : t + 1])
-                nc.scalar.copy(plain[:, t, 0:needed], bank[:, 0:needed])
-            a_plain[half, g], a_gained[half, g] = plain, gained
+        def template_pass(bank, j0, width, g, t, stop):
+            r0 = g * PASS + t * P
+            half, c0 = divmod(j0, HALF)
+            nc.tensor.matmul_mx(
+                out=bank,
+                lhsT=w1_wo[:, 2 * r0 : 2 * (r0 + P)].bitcast(FP4X4),
+                lhsT_scale=w1_so[:, r0 : r0 + P],
+                rhs=v_w[half][:, c0 : c0 + width].bitcast(FP8X4),
+                rhs_scale=v_s[:, j0 : j0 + width],
+                start=True,
+                stop=stop,
+            )
 
-        def quantize(name, grouped, width):
-            codes = kept(name + "_w", [P, width], U32)
+        def template_product(half, g):
+            needed = min(HALF, SUMMED_FROM[g] - half * HALF)
+            blocks = [j for j in range(half * HALF, (half + 1) * HALF, SUB) if not on_gpsimd(j)]
+            plain = kept("a_plain%d%d" % (half, g), [P, PACK, needed], F32)
+            gained = kept("a_gained%d%d" % (half, g), [P, PACK, len(blocks), SUB], F32)
+            first, step = blocks[0] % HALF // SUB, (blocks[1] - blocks[0]) // SUB
+            for t in range(PACK):
+                bank = psum.tile([P, HALF], F32, name="sum_bank", tag="sum_bank", bufs=4)
+                template_pass(bank[:], half * HALF, HALF, g, t, True)
+                nc.scalar.copy(plain[:, t, :], bank[:, 0:needed])
+                nc.scalar.activation(
+                    gained[:, t, :, :],
+                    bank[:].rearrange("p (b c) -> p b c", c=SUB)[:, first : HALF // SUB : step, :],
+                    ACT.Copy,
+                    scale=minus_gains[:, g, t : t + 1],
+                )
+            for j in range(half * HALF, half * HALF + needed, SUB):
+                a_plain[j, g] = plain[:, :, j % HALF : j % HALF + SUB]
+            for n, j in enumerate(blocks):
+                a_gained[j, g] = gained[:, :, n, :]
+
+        def quantize(name, grouped, width, tag=None):
+            codes = kept(name + "_w", [P, width], U32, tag=tag)
             scales = kept(name + "_s", [P, width], U8)
             nc.vector.quantize_mx(
-                out=codes[:].bitcast(FP8X4), scales=scales[:], in_=grouped[:].rearrange("p c i -> p (c i)")
+                out=codes[:].bitcast(FP8X4), scales=scales[:], in_=grouped.rearrange("p c i -> p (c i)")
             )
             return codes, scales
 
@@ -144,54 +161,71 @@ def tile_list_photo_redshift_features_kernel(
 
         colours = kept("colours", [P, PACK, S], F32)
 
-        def gather_plane(i, width):
-            def pick(j0):
-                first = ring.tile([P, width], F32, name="first", tag="first", bufs=3)
-                nc.vector.tensor_copy(first[:], planes[i][:].indirect(idx2[:, j0 // 16 : (j0 + width) // 16]))
-                return first
+        def pick(i, j0, width, first):
+            nc.vector.tensor_copy(first[:], planes[i][:].indirect(idx2[:, j0 // 16 : (j0 + width) // 16]))
+            return first
 
-            picked = pick(0)
-            for j0 in range(0, S, width):
-                ahead = pick(j0 + width) if j0 + width < S else None
-                nc.vector.tensor_tensor(
-                    colours[:, i, j0 : j0 + width],
-                    planes[i][:].indirect(idx3[:, j0 // 16 : (j0 + width) // 16]),
-                    picked[:],
-                    ALU.subtract,
-                )
-                picked = ahead
+        def subtract(i, j0, width, first):
+            nc.vector.tensor_tensor(
+                colours[:, i, j0 : j0 + width],
+                planes[i][:].indirect(idx3[:, j0 // 16 : (j0 + width) // 16]),
+                first[:],
+                ALU.subtract,
+            )
+
+        def gather_plane(i):
+            firsts = [
+                pick(i, j0, HALF, ring.tile([P, HALF], F32, name="first", tag="first", bufs=3)) for j0 in (0, HALF)
+            ]
+            for n, first in enumerate(firsts):
+                subtract(i, n * HALF, HALF, first)
 
         def round_w2(g):
-            grouped = ring.tile([P, PASS, PACK], BF16, name="w_grouped", tag="w_grouped", align_bytes=ALIGN)
+            grouped = kept("w2_grouped%d" % g, [P, PASS, PACK], BF16)
             nc.scalar.copy(
                 grouped[:].rearrange("p (t m) i -> p m t i", t=PACK),
                 w2_raw[g][:].rearrange("p i (m t) -> p m t i", t=PACK),
             )
-            return quantize("w2q%d" % g, grouped, PASS)
+            return grouped
 
-        def round_w3(g):
-            grouped = ring.tile([P, N, PACK], BF16, name="w_grouped", tag="w_grouped", align_bytes=ALIGN)
-            interleave(grouped[:], w3_raw[g][:])
-            return quantize("w3q%d" % g, grouped, N)
+        w3_grouped = [kept("w3_grouped%d" % g, [P, N, PACK], BF16, tag="w2_grouped%d" % g) for g in range(R_PASSES)]
+
+        def round_w3(g, part):
+            cols = slice(part * N // 2, (part + 1) * N // 2)
+            interleave(w3_grouped[g][:, cols, :], w3_raw[g][:, :, cols])
+
+        x_grouped = [kept("x_grouped%d" % q, [P, QUARTER, PACK], BF16) for q in range(4)]
 
         def round_x(quarter):
-            tag = ("slot_r", "x_grouped1", "slot_s", "x_grouped3")[quarter]
-            grouped = kept("x_grouped%d" % quarter, [P, QUARTER, PACK], BF16, tag=tag)
-            interleave(grouped[:], colours[:, :, quarter * QUARTER : (quarter + 1) * QUARTER])
-            return quantize("xq%d" % quarter, grouped, QUARTER)
+            interleave(x_grouped[quarter][:], colours[:, :, quarter * QUARTER : (quarter + 1) * QUARTER])
 
-        gather_plane(0, HALF)
+        def quantize_x(quarter):
+            return quantize("xq%d" % quarter, x_grouped[quarter][:], QUARTER)
+
+        gather_plane(0)
         template_product(0, 0)
-        w2q = [round_w2(0)]
-        gather_plane(1, HALF)
+        w2_grouped = [round_w2(0)]
+        gather_plane(1)
         template_product(0, 1)
-        w2q.append(round_w2(1))
-        gather_plane(2, HALF)
-        gather_plane(3, QUARTER)
-        w3q = [round_w3(0)]
-        xq = [round_x(0), round_x(1)]
-        w3q.append(round_w3(1))
-        xq.extend([round_x(2), round_x(3)])
+        w2_grouped.append(round_w2(1))
+        gather_plane(2)
+        w2q = [quantize("w2q0", w2_grouped[0][:], PASS, tag="plane2")]
+        last = PACK - 1
+        firsts = [pick(last, q * QUARTER, QUARTER, kept("last_first%d" % q, [P, QUARTER], F32)) for q in range(2)]
+        subtract(last, 0, QUARTER, firsts[0])
+        firsts.append(pick(last, 2 * QUARTER, QUARTER, kept("last_first2", [P, QUARTER], F32)))
+        subtract(last, QUARTER, QUARTER, firsts[1])
+        w2q.append(quantize("w2q1", w2_grouped[1][:], PASS, tag="last_first1"))
+        subtract(last, 2 * QUARTER, QUARTER, firsts[2])
+        template_product(1, 0)
+        template_product(1, 1)
+        round_x(0)
+        xq = [quantize_x(0)]
+        firsts.append(pick(last, 3 * QUARTER, QUARTER, kept("last_first3", [P, QUARTER], F32, tag="x_grouped0")))
+        subtract(last, 3 * QUARTER, QUARTER, firsts[3])
+        round_x(1)
+        xq.append(quantize_x(1))
+        w3q = []
 
         def colour_pass(bank, j, g, t, start):
             quarter, c0 = divmod(j, QUARTER)
@@ -205,65 +239,77 @@ def tile_list_photo_redshift_features_kernel(
                 stop=True,
             )
 
-        def residual_in_psum(j0, g):
-            bank = psum.tile([P, PACK, SUB], F32, name="a_bank", tag="a_bank", bufs=2)
-            for t in range(PACK):
-                r0 = g * PASS + t * P
-                nc.tensor.matmul_mx(
-                    out=bank[:, t, :],
-                    lhsT=w1_wo[:, 2 * r0 : 2 * (r0 + P)].bitcast(FP4X4),
-                    lhsT_scale=w1_so[:, r0 : r0 + P],
-                    rhs=v_w[:, j0 : j0 + SUB].bitcast(FP8X4),
-                    rhs_scale=v_s[:, j0 : j0 + SUB],
-                    start=True,
-                    stop=False,
-                )
-                colour_pass(bank, j0, g, t, False)
-            grouped = kept("d_grouped%d_%d" % (j0, g), [P, SUB, PACK], BF16)
-            interleave(grouped[:], bank[:])
-            return quantize("dq%d_%d" % (j0, g), grouped, SUB)
+        def block_bank():
+            return psum.tile([P, PACK, SUB], F32, name="block_bank", tag="block_bank", bufs=4)
 
-        def meet(j0, width, g):
-            half, c0 = divmod(j0, HALF)
-            summed = j0 >= SUMMED_FROM[g]
-            grouped = ring.tile(
-                [P, width if summed else 2 * width, PACK], BF16, name="hd", tag="hd", bufs=3, align_bytes=ALIGN
-            )
+        def residual_in_psum(j0, g, grouped):
+            bank = block_bank()
+            for t in range(PACK):
+                template_pass(bank[:, t, :], j0, SUB, g, t, False)
+                colour_pass(bank, j0, g, t, False)
+            interleave(grouped, bank[:])
+
+        def paired(ap):
+            return ap.rearrange("p t (c e) -> p c t e", e=2)
+
+        def join(grouped, a, bank, op):
+            nc.vector.tensor_tensor(grouped.rearrange("p (c e) t -> p c t e", e=2), paired(a), paired(bank[:]), op)
+
+        starts = list(range(0, WIDE_END, WIDE)) + list(range(WIDE_END, S, SUB))
+        steps = [(j0, WIDE if j0 < WIDE_END else SUB, g) for j0 in starts for g in range(R_PASSES)]
+        wide_steps = R_PASSES * WIDE_END // WIDE
+        h_tiles, d_tiles = {}, {}
+
+        def h_tile(s):
+            if s not in h_tiles:
+                if s <= wide_steps:
+                    h_tiles[s] = ring.tile([P, WIDE, PACK], BF16, name="h_pair", tag="h_pair", bufs=2, align_bytes=ALIGN)
+                else:
+                    h_tiles[s] = kept("h_last%d" % s, [P, SUB, PACK], BF16)
+            return h_tiles[s]
+
+        def d_tile(s):
+            if s not in d_tiles:
+                d_tiles[s] = ring.tile([P, WIDE, PACK], BF16, name="d_pair", tag="d_pair", bufs=3, align_bytes=ALIGN)
+            return d_tiles[s]
+
+        def meet(s):
+            j0, width, g = steps[s]
             for s0 in range(0, width, SUB):
-                cols = slice(c0 + s0, c0 + s0 + SUB)
-                bank = psum.tile([P, PACK, SUB], F32, name="b_bank", tag="b_bank", bufs=3)
+                j = j0 + s0
+                bank = block_bank()
                 for t in range(PACK):
-                    colour_pass(bank, j0 + s0, g, t, True)
-                b = bank[:].rearrange("p t (c e) -> p c t e", e=2)
-                nc.vector.tensor_tensor(
-                    grouped[:, s0 : s0 + SUB, :].rearrange("p (c e) t -> p c t e", e=2),
-                    a_gained[half, g][:, :, cols].rearrange("p t (c e) -> p c t e", e=2),
-                    b,
-                    ALU.mult,
-                )
-                if not summed:
-                    nc.vector.tensor_tensor(
-                        grouped[:, width + s0 : width + s0 + SUB, :].rearrange("p (c e) t -> p c t e", e=2),
-                        a_plain[half, g][:, :, cols].rearrange("p t (c e) -> p c t e", e=2),
-                        b,
-                        ALU.add,
+                    colour_pass(bank, j, g, t, True)
+                if not on_gpsimd(j):
+                    join(h_tile(s)[:, 0:SUB, :], a_gained[j, g], bank, ALU.mult)
+                if j < SUMMED_FROM[g]:
+                    join(d_tile(s)[:, s0 : s0 + SUB, :], a_plain[j, g], bank, ALU.add)
+                if on_gpsimd(j):
+                    gained = ring.tile([P, PACK, SUB], F32, name="b_gained", tag="b_gained", bufs=3)
+                    for t in range(PACK):
+                        nc.scalar.activation(
+                            gained[:, t, :], bank[:, t, :], ACT.Copy, scale=minus_gains[:, g, t : t + 1]
+                        )
+                    nc.gpsimd.tensor_tensor(
+                        h_tile(s + 1)[:, SUB:WIDE, :],
+                        a_plain[j, g].rearrange("p t c -> p c t"),
+                        gained[:].rearrange("p t c -> p c t"),
+                        ALU.mult,
                     )
-            return grouped
 
         y_banks = {}
 
-        def y_passes(j0, width, weights, operand, last):
+        def y_passes(j0, width, c0, columns, weights, operand, last):
             tiles_a_bank = 2 if j0 + width == S else 512 // width
             for n0 in range(0, N // P, tiles_a_bank):
                 first = (j0, n0) not in y_banks
                 if first:
-                    tag, bufs = ("a_bank", 2) if j0 + width == S else ("y_bank", 3)
-                    y_banks[j0, n0] = psum.tile([P, tiles_a_bank, width], F32, name="y_bank", tag=tag, bufs=bufs)
+                    y_banks[j0, n0] = psum.tile([P, tiles_a_bank, width], F32, name="y_bank", tag="sum_bank", bufs=4)
                 bank = y_banks[j0, n0]
                 for n in range(tiles_a_bank):
                     rows = slice((n0 + n) * P, (n0 + n + 1) * P)
                     nc.tensor.matmul_mx(
-                        out=bank[:, n, :],
+                        out=bank[:, n, c0 : c0 + columns],
                         lhsT=weights[0][:, rows].bitcast(FP8X4),
                         lhsT_scale=weights[1][:, rows],
                         rhs=operand[0].bitcast(FP8X4),
@@ -279,36 +325,61 @@ def tile_list_photo_redshift_features_kernel(
                         in_=result[:],
                     )
 
-        def second_stage(j0, width, g, grouped):
-            if g == 0:
-                for gs in range(R_PASSES):
-                    if j0 >= SUMMED_FROM[gs]:
-                        d_codes, d_scales = residuals[j0, gs]
-                        y_passes(j0, width, (w4_w[:, gs, :], w4_s[:, gs, :]), (d_codes[:], d_scales[:]), False)
-            summed = j0 >= SUMMED_FROM[g]
-            columns = width if summed else 2 * width
-            codes = ring.tile([P, columns], U32, name="hd_w", tag="hd_w", bufs=3, align_bytes=ALIGN)
-            scales = ring.tile([P, columns], U8, name="hd_s", tag="hd_s", bufs=3, align_bytes=ALIGN)
-            nc.vector.quantize_mx(
-                out=codes[:].bitcast(FP8X4), scales=scales[:], in_=grouped[:].rearrange("p c t -> p (c t)")
-            )
-            if not summed:
-                d_op = (codes[:, width:columns], scales[:, width:columns])
-                y_passes(j0, width, (w4_w[:, g, :], w4_s[:, g, :]), d_op, False)
-            y_passes(j0, width, w3q[g], (codes[:, 0:width], scales[:, 0:width]), g == R_PASSES - 1)
+        def columns_of(quantized, c0, columns):
+            return quantized[0][:, c0 : c0 + columns], quantized[1][:, c0 : c0 + columns]
 
-        starts = [sum(CHUNKS[:c]) for c in range(len(CHUNKS))]
-        steps = [(j0, width, g) for j0, width in zip(starts, CHUNKS) for g in range(R_PASSES)]
-        waiting = None
-        residuals = {}
-        for number, step in enumerate(steps):
-            if number < R_PASSES:
-                template_product(1, number)
-            for j0, width, g in steps[number + 1 : number + 3]:
-                if j0 >= SUMMED_FROM[g] and (j0, g) not in residuals:
-                    residuals[j0, g] = residual_in_psum(j0, g)
-            grouped = meet(*step)
-            if waiting is not None:
-                second_stage(*waiting)
-            waiting = step + (grouped,)
-        second_stage(*waiting)
+        def w4(g):
+            return w4_w[:, g, :], w4_s[:, g, :]
+
+        d_last = kept("d_last", [P, WIDE, PACK], BF16)
+
+        def second_stage(s):
+            j0, width, g = steps[s]
+            both = None
+            if s < wide_steps or s == wide_steps:
+                both = quantize("dq%d" % s, d_tile(s)[:], WIDE)
+            elif s == wide_steps + 2:
+                both = quantize("dq%d" % s, d_last[:], WIDE)
+            held = 0 < s <= wide_steps
+            columns = WIDE if held else SUB
+            hq = quantize("hq%d" % s, h_tile(s)[:, 0:columns, :], columns)
+            if held:
+                pj0, pwidth, pg = steps[s - 1]
+                if pg == R_PASSES - 1:
+                    y_passes(pj0, pwidth, 0, SUB, w3q[pg], columns_of(hq, SUB, SUB), True)
+            if s < wide_steps:
+                y_passes(j0, width, 0, WIDE, w4(g), columns_of(both, 0, WIDE), False)
+            elif both is not None:
+                for gs in range(R_PASSES):
+                    y_passes(j0, width, 0, SUB, w4(gs), columns_of(both, gs * SUB, SUB), False)
+            if held and pg != R_PASSES - 1:
+                y_passes(pj0, pwidth, 0, SUB, w3q[pg], columns_of(hq, SUB, SUB), False)
+            closes = s >= wide_steps and g == R_PASSES - 1
+            y_passes(j0, width, width - SUB, SUB, w3q[g], columns_of(hq, 0, SUB), closes)
+
+        h_tile(0)
+        for s in range(len(steps)):
+            if s < 2:
+                round_w3(0, s)
+            if s == 2:
+                round_w3(1, 0)
+                round_w3(1, 1)
+            if s == 3:
+                round_x(2)
+            if s == 4:
+                round_x(3)
+            meet(s)
+            if s in (1, 2):
+                w3q.append(quantize("w3q%d" % (s - 1), w3_grouped[s - 1][:], N))
+            if s == 3:
+                xq.append(quantize_x(2))
+            if s == 4:
+                xq.append(quantize_x(3))
+            if s == 5:
+                residual_in_psum(WIDE_END, 1, d_tile(wide_steps)[:, SUB:WIDE, :])
+            if s == 6:
+                for gs in range(R_PASSES):
+                    residual_in_psum(S - SUB, gs, d_last[:, gs * SUB : (gs + 1) * SUB, :])
+            if s > 0:
+                second_stage(s - 1)
+        second_stage(len(steps) - 1)

@@ -291,9 +291,9 @@ def tile_list_photo_redshift_features_kernel(
                             gained[:, t, :], bank[:, t, :], ACT.Copy, scale=minus_gains[:, g, t : t + 1]
                         )
                     nc.gpsimd.tensor_tensor(
-                        h_tile(s + 1)[:, SUB:WIDE, :],
-                        a_plain[j, g].rearrange("p t c -> p c t"),
-                        gained[:].rearrange("p t c -> p c t"),
+                        h_tile(s + 1)[:, SUB:WIDE, :].rearrange("p (c e) t -> p c t e", e=2),
+                        paired(a_plain[j, g]),
+                        paired(gained[:]),
                         ALU.mult,
                     )
 

@@ -335,14 +335,14 @@ def tile_list_photo_redshift_features_kernel(
 
         def second_stage(s):
             j0, width, g = steps[s]
-            both = None
-            if s < wide_steps or s == wide_steps:
-                both = quantize("dq%d" % s, d_tile(s)[:], WIDE)
-            elif s == wide_steps + 2:
-                both = quantize("dq%d" % s, d_last[:], WIDE)
             held = 0 < s <= wide_steps
             columns = WIDE if held else SUB
             hq = quantize("hq%d" % s, h_tile(s)[:, 0:columns, :], columns)
+            both = None
+            if s <= wide_steps:
+                both = quantize("dq%d" % s, d_tile(s)[:], WIDE)
+            elif s == wide_steps + 2:
+                both = quantize("dq%d" % s, d_last[:], WIDE)
             if held:
                 pj0, pwidth, pg = steps[s - 1]
                 if pg == R_PASSES - 1:
@@ -380,6 +380,9 @@ def tile_list_photo_redshift_features_kernel(
             if s == 6:
                 for gs in range(R_PASSES):
                     residual_in_psum(S - SUB, gs, d_last[:, gs * SUB : (gs + 1) * SUB, :])
-            if s > 0:
+            if 0 < s < wide_steps:
                 second_stage(s - 1)
+            if s > wide_steps:
+                second_stage(s - 2)
+        second_stage(len(steps) - 2)
         second_stage(len(steps) - 1)

@@ -72,6 +72,8 @@ def tile_list_photo_redshift_features_kernel(
         nc.sync.dma_start(idx2[:], offs2)
         nc.sync.dma_start(idx3[:], offs3)
 
+        warm = kept("warm", [P, R_PASSES, PACK], F32)
+        nc.scalar.activation(warm[:], gains[:], ACT.Gelu_apprx_tanh)
         minus_gains = kept("minus_gains", [P, R_PASSES, PACK], F32)
         nc.scalar.activation(minus_gains[:], gains[:], ACT.Copy, scale=-1.0)
 
@@ -107,8 +109,8 @@ def tile_list_photo_redshift_features_kernel(
         nc.sync.dma_start(out=w4_w[:], in_=w4_words.rearrange("a p c i -> p a (c i)").bitcast(I32))
         load_scale_rows(nc.sync, w4_s, w4_scales.rearrange("a q c -> q a c"))
 
-        def on_gpsimd(j):
-            return j < WIDE_END and j % WIDE == 0
+        def on_gpsimd(j, g):
+            return j % WIDE == 0 and j < SUMMED_FROM[g]
 
         a_plain, a_gained = {}, {}
 
@@ -125,13 +127,22 @@ def tile_list_photo_redshift_features_kernel(
                 stop=stop,
             )
 
-        def template_product(half, g):
+        a_tiles = {}
+
+        def template_product(half, g, slices=range(PACK)):
             needed = min(HALF, SUMMED_FROM[g] - half * HALF)
-            blocks = [j for j in range(half * HALF, (half + 1) * HALF, SUB) if not on_gpsimd(j)]
-            plain = kept("a_plain%d%d" % (half, g), [P, PACK, needed], F32)
-            gained = kept("a_gained%d%d" % (half, g), [P, PACK, len(blocks), SUB], F32)
+            blocks = [j for j in range(half * HALF, (half + 1) * HALF, SUB) if not on_gpsimd(j, g)]
+            if (half, g) not in a_tiles:
+                plain = kept("a_plain%d%d" % (half, g), [P, PACK, needed], F32)
+                gained = kept("a_gained%d%d" % (half, g), [P, PACK, len(blocks), SUB], F32)
+                a_tiles[half, g] = plain, gained
+                for j in range(half * HALF, half * HALF + needed, SUB):
+                    a_plain[j, g] = plain[:, :, j % HALF : j % HALF + SUB]
+                for n, j in enumerate(blocks):
+                    a_gained[j, g] = gained[:, :, n, :]
+            plain, gained = a_tiles[half, g]
             first, step = blocks[0] % HALF // SUB, (blocks[1] - blocks[0]) // SUB
-            for t in range(PACK):
+            for t in slices:
                 bank = psum.tile([P, HALF], F32, name="sum_bank", tag="sum_bank", bufs=4)
                 template_pass(bank[:], half * HALF, HALF, g, t, True)
                 nc.scalar.copy(plain[:, t, :], bank[:, 0:needed])
@@ -141,10 +152,6 @@ def tile_list_photo_redshift_features_kernel(
                     ACT.Copy,
                     scale=minus_gains[:, g, t : t + 1],
                 )
-            for j in range(half * HALF, half * HALF + needed, SUB):
-                a_plain[j, g] = plain[:, :, j % HALF : j % HALF + SUB]
-            for n, j in enumerate(blocks):
-                a_gained[j, g] = gained[:, :, n, :]
 
         def quantize(name, grouped, width, tag=None):
             codes = kept(name + "_w", [P, width], U32, tag=tag)
@@ -218,13 +225,12 @@ def tile_list_photo_redshift_features_kernel(
         w2q.append(quantize("w2q1", w2_grouped[1][:], PASS, tag="last_first1"))
         subtract(last, 2 * QUARTER, QUARTER, firsts[2])
         template_product(1, 0)
-        template_product(1, 1)
+        template_product(1, 1, range(0, 2))
         round_x(0)
-        xq = [quantize_x(0)]
-        firsts.append(pick(last, 3 * QUARTER, QUARTER, kept("last_first3", [P, QUARTER], F32, tag="x_grouped0")))
-        subtract(last, 3 * QUARTER, QUARTER, firsts[3])
         round_x(1)
-        xq.append(quantize_x(1))
+        xq = [quantize_x(0), quantize_x(1)]
+        firsts.append(pick(last, 3 * QUARTER, QUARTER, kept("last_first3", [P, QUARTER], F32, tag="x_grouped1")))
+        subtract(last, 3 * QUARTER, QUARTER, firsts[3])
         w3q = []
 
         def colour_pass(bank, j, g, t, start):
@@ -243,7 +249,7 @@ def tile_list_photo_redshift_features_kernel(
             return psum.tile([P, PACK, SUB], F32, name="block_bank", tag="block_bank", bufs=4)
 
         def residual_in_psum(j0, g, grouped):
-            bank = block_bank()
+            bank = psum.tile([P, PACK, SUB], F32, name="d_bank", tag="sum_bank", bufs=4)
             for t in range(PACK):
                 template_pass(bank[:, t, :], j0, SUB, g, t, False)
                 colour_pass(bank, j0, g, t, False)
@@ -261,46 +267,61 @@ def tile_list_photo_redshift_features_kernel(
         h_tiles, d_tiles = {}, {}
 
         def h_tile(s):
+            if s in (wide_steps, wide_steps + 1):
+                if wide_steps not in h_tiles:
+                    h_tiles[wide_steps] = kept("h_both", [P, R_PASSES, SUB, PACK], BF16, tag="h_odd")
+                return h_tiles[wide_steps][:, s - wide_steps, :, :]
             if s not in h_tiles:
-                if s <= wide_steps:
-                    h_tiles[s] = ring.tile([P, WIDE, PACK], BF16, name="h_pair", tag="h_pair", bufs=2, align_bytes=ALIGN)
-                else:
-                    h_tiles[s] = kept("h_last%d" % s, [P, SUB, PACK], BF16)
-            return h_tiles[s]
+                tag = ("x_grouped1", "h_odd")[s % 2] if s < wide_steps else None
+                h_tiles[s] = kept("h_grouped%d" % s, [P, steps[s][1], PACK], BF16, tag=tag)
+            return h_tiles[s][:]
+
+        d_first = kept("d_first", [P, R_PASSES, WIDE, PACK], BF16, tag="plane3")
 
         def d_tile(s):
+            if s < R_PASSES:
+                return d_first[:, s, :, :]
             if s not in d_tiles:
-                d_tiles[s] = ring.tile([P, WIDE, PACK], BF16, name="d_pair", tag="d_pair", bufs=3, align_bytes=ALIGN)
-            return d_tiles[s]
+                d_tiles[s] = kept("d_grouped%d" % s, [P, WIDE, PACK], BF16, tag="d_grouped%d" % (s % 3 if s < wide_steps else s))
+            return d_tiles[s][:]
 
-        def meet(s):
+        def in_fours(ap):
+            return ap.rearrange("p t (c e) -> p c t e", e=4)
+
+        banks = {}
+
+        def colour_product(s):
             j0, width, g = steps[s]
-            for s0 in range(0, width, SUB):
-                j = j0 + s0
-                bank = block_bank()
+            for j in range(j0, j0 + width, SUB):
+                banks[j, g] = block_bank()
                 for t in range(PACK):
-                    colour_pass(bank, j, g, t, True)
-                if not on_gpsimd(j):
-                    join(h_tile(s)[:, 0:SUB, :], a_gained[j, g], bank, ALU.mult)
-                if j < SUMMED_FROM[g]:
-                    join(d_tile(s)[:, s0 : s0 + SUB, :], a_plain[j, g], bank, ALU.add)
-                if on_gpsimd(j):
-                    gained = ring.tile([P, PACK, SUB], F32, name="b_gained", tag="b_gained", bufs=3)
+                    colour_pass(banks[j, g], j, g, t, True)
+                if on_gpsimd(j, g):
+                    gained = kept("b_gained%d" % s, [P, PACK, SUB], F32)
                     for t in range(PACK):
                         nc.scalar.activation(
-                            gained[:, t, :], bank[:, t, :], ACT.Copy, scale=minus_gains[:, g, t : t + 1]
+                            gained[:, t, :], banks[j, g][:, t, :], ACT.Copy, scale=minus_gains[:, g, t : t + 1]
                         )
                     nc.gpsimd.tensor_tensor(
-                        h_tile(s + 1)[:, SUB:WIDE, :].rearrange("p (c e) t -> p c t e", e=2),
-                        paired(a_plain[j, g]),
-                        paired(gained[:]),
+                        h_tile(s)[:, 0:SUB, :].rearrange("p (c e) t -> p c t e", e=4),
+                        in_fours(a_plain[j, g]),
+                        in_fours(gained[:]),
                         ALU.mult,
                     )
 
+        def meet(s):
+            j0, width, g = steps[s]
+            for j in reversed(range(j0, j0 + width, SUB)):
+                cols = slice(j - j0, j - j0 + SUB)
+                if j < SUMMED_FROM[g]:
+                    join(d_tile(s)[:, cols, :], a_plain[j, g], banks[j, g], ALU.add)
+                if not on_gpsimd(j, g):
+                    join(h_tile(s)[:, cols, :], a_gained[j, g], banks[j, g], ALU.mult)
+
         y_banks = {}
 
-        def y_passes(j0, width, c0, columns, weights, operand, last):
-            tiles_a_bank = 2 if j0 + width == S else 512 // width
+        def y_passes(j0, width, weights, operand, last):
+            tiles_a_bank = 512 // width
             for n0 in range(0, N // P, tiles_a_bank):
                 first = (j0, n0) not in y_banks
                 if first:
@@ -309,7 +330,7 @@ def tile_list_photo_redshift_features_kernel(
                 for n in range(tiles_a_bank):
                     rows = slice((n0 + n) * P, (n0 + n + 1) * P)
                     nc.tensor.matmul_mx(
-                        out=bank[:, n, c0 : c0 + columns],
+                        out=bank[:, n, :],
                         lhsT=weights[0][:, rows].bitcast(FP8X4),
                         lhsT_scale=weights[1][:, rows],
                         rhs=operand[0].bitcast(FP8X4),
@@ -318,12 +339,14 @@ def tile_list_photo_redshift_features_kernel(
                         stop=(last and n == tiles_a_bank - 1),
                     )
                 if last:
-                    result = ring.tile([P, tiles_a_bank, width], F32, name="result", tag="result", bufs=5)
-                    nc.scalar.activation(result[:], bank[:], ACT.Gelu_apprx_tanh)
-                    nc.sync.dma_start(
-                        out=out[n0 * P : (n0 + tiles_a_bank) * P, j0 : j0 + width].rearrange("(n p) j -> p n j", p=P),
-                        in_=result[:],
-                    )
+                    tiles = 2 if j0 + width == S else tiles_a_bank
+                    for n in range(0, tiles_a_bank, tiles):
+                        result = ring.tile([P, tiles, width], F32, name="result", tag="result", bufs=5)
+                        nc.scalar.activation(result[:], bank[:, n : n + tiles, :], ACT.Gelu_apprx_tanh)
+                        rows = slice((n0 + n) * P, (n0 + n + tiles) * P)
+                        nc.sync.dma_start(
+                            out=out[rows, j0 : j0 + width].rearrange("(n p) j -> p n j", p=P), in_=result[:]
+                        )
 
         def columns_of(quantized, c0, columns):
             return quantized[0][:, c0 : c0 + columns], quantized[1][:, c0 : c0 + columns]
@@ -333,56 +356,68 @@ def tile_list_photo_redshift_features_kernel(
 
         d_last = kept("d_last", [P, WIDE, PACK], BF16)
 
+        waiting = []
+
+        def h_passes(before):
+            for job in list(waiting):
+                j0, width, g, operand = job
+                if g < len(w3q) and j0 < before:
+                    y_passes(j0, width, w3q[g], operand, g == R_PASSES - 1)
+                    waiting.remove(job)
+
         def second_stage(s):
             j0, width, g = steps[s]
-            held = 0 < s <= wide_steps
-            columns = WIDE if held else SUB
-            hq = quantize("hq%d" % s, h_tile(s)[:, 0:columns, :], columns)
-            both = None
-            if s <= wide_steps:
-                both = quantize("dq%d" % s, d_tile(s)[:], WIDE)
-            elif s == wide_steps + 2:
-                both = quantize("dq%d" % s, d_last[:], WIDE)
-            if held:
-                pj0, pwidth, pg = steps[s - 1]
-                if pg == R_PASSES - 1:
-                    y_passes(pj0, pwidth, 0, SUB, w3q[pg], columns_of(hq, SUB, SUB), True)
+            hq = quantize("hq%d" % s, h_tile(s), width, tag=("b_gained%d" % (s + 1) if s + 1 < wide_steps else None))
+            waiting.append((j0, width, g, columns_of(hq, 0, width)))
             if s < wide_steps:
-                y_passes(j0, width, 0, WIDE, w4(g), columns_of(both, 0, WIDE), False)
-            elif both is not None:
-                for gs in range(R_PASSES):
-                    y_passes(j0, width, 0, SUB, w4(gs), columns_of(both, gs * SUB, SUB), False)
-            if held and pg != R_PASSES - 1:
-                y_passes(pj0, pwidth, 0, SUB, w3q[pg], columns_of(hq, SUB, SUB), False)
-            closes = s >= wide_steps and g == R_PASSES - 1
-            y_passes(j0, width, width - SUB, SUB, w3q[g], columns_of(hq, 0, SUB), closes)
+                dq = quantize("dq%d" % s, d_tile(s), WIDE)
+                h_passes(j0)
+                y_passes(j0, width, w4(g), columns_of(dq, 0, WIDE), False)
+            h_passes(S)
 
-        h_tile(0)
-        for s in range(len(steps)):
-            if s < 2:
-                round_w3(0, s)
+        def both_passes(name, grouped, j0, weights, closes):
+            both = quantize(name, grouped, WIDE, tag=("b_gained6" if name == "dq_end" else None))
+            for g in range(R_PASSES):
+                y_passes(j0, SUB, weights(g), columns_of(both, g * SUB, SUB), closes and g == R_PASSES - 1)
+
+        colour_product(0)
+        colour_product(1)
+        for s in range(wide_steps):
+            meet(s)
+            if s == 0:
+                round_w3(0, 0)
+            if s == 1:
+                round_w3(0, 1)
+                round_x(2)
+                w3q.append(quantize("w3q0", w3_grouped[0][:], N))
             if s == 2:
                 round_w3(1, 0)
-                round_w3(1, 1)
-            if s == 3:
-                round_x(2)
-            if s == 4:
                 round_x(3)
-            meet(s)
-            if s in (1, 2):
-                w3q.append(quantize("w3q%d" % (s - 1), w3_grouped[s - 1][:], N))
-            if s == 3:
+                round_w3(1, 1)
                 xq.append(quantize_x(2))
-            if s == 4:
+                template_product(1, 1, range(2, PACK))
+            if s == 3:
                 xq.append(quantize_x(3))
-            if s == 5:
-                residual_in_psum(WIDE_END, 1, d_tile(wide_steps)[:, SUB:WIDE, :])
-            if s == 6:
+                w3q.append(quantize("w3q1", w3_grouped[1][:], N))
+            if s + 2 <= wide_steps:
+                colour_product(s + 2)
+            if s + 1 == wide_steps:
+                for later in range(wide_steps + 1, len(steps)):
+                    colour_product(later)
+            if s == 4:
                 for gs in range(R_PASSES):
                     residual_in_psum(S - SUB, gs, d_last[:, gs * SUB : (gs + 1) * SUB, :])
-            if 0 < s < wide_steps:
+            if s > 0:
                 second_stage(s - 1)
-            if s > wide_steps:
-                second_stage(s - 2)
-        second_stage(len(steps) - 2)
-        second_stage(len(steps) - 1)
+            if s == 4:
+                residual_in_psum(WIDE_END, 1, d_tile(wide_steps)[:, SUB:WIDE, :])
+        both_passes("dq_last", d_last[:], S - SUB, w4, False)
+        second_stage(wide_steps - 1)
+        for s in range(wide_steps, wide_steps + 3):
+            meet(s)
+        both_passes("dq_end", d_tile(wide_steps), WIDE_END, w4, False)
+        h_end = h_tiles[wide_steps][:].rearrange("p g c t -> p (g c) t")
+        both_passes("hq_end", h_end, WIDE_END, lambda g: w3q[g], True)
+        meet(wide_steps + 3)
+        second_stage(wide_steps + 2)
+        second_stage(wide_steps + 3)

@@ -19,13 +19,18 @@ ACT = mybir.ActivationFunctionType
 P = 128
 PACK = 4
 PASS = P * PACK
+BANK = 512
+LIST_ROWS = 16
 R_PASSES = H // PASS
 HALF = S // 2
-SUB = 128
-WIDE = 2 * SUB
-WIDE_END = S - 2 * SUB
 QUARTER = S // 4
-SUMMED_FROM = (S - SUB, S - 2 * SUB)
+BLOCK = BANK // PACK
+WIDE = 2 * BLOCK
+WIDE_END = S - 2 * BLOCK
+SUMMED_FROM = (S - BLOCK, S - 2 * BLOCK)
+EARLY_SLICES = 2
+SUM_BANKS = 4
+BLOCK_BANKS = 4
 ALIGN = 64
 
 
@@ -41,22 +46,25 @@ def tile_list_photo_redshift_features_kernel(
         def kept(name, shape, dtype, tag=None):
             return keep.tile(shape, dtype, name=name, tag=tag or name, align_bytes=ALIGN)
 
-        def load_scale_rows(queue, plane, rows):
+        def load_scale_rows(tile, rows):
             for q in range(4):
-                queue.dma_start(out=plane[32 * q : 32 * q + 4].bitcast(I32), in_=rows[4 * q : 4 * q + 4].bitcast(I32))
+                nc.sync.dma_start(out=tile[32 * q : 32 * q + 4].bitcast(I32), in_=rows[4 * q : 4 * q + 4].bitcast(I32))
 
-        idx1 = kept("idx1", [P, S // 16], U16)
-        idx2 = kept("idx2", [P, S // 16], U16)
-        idx3 = kept("idx3", [P, S // 16], U16)
+        idx1 = kept("idx1", [P, S // LIST_ROWS], U16)
+        idx2 = kept("idx2", [P, S // LIST_ROWS], U16)
+        idx3 = kept("idx3", [P, S // LIST_ROWS], U16)
         tab_s = kept("tab_s", [P, T], U8)
-        tab_w = kept("tab_w", [P, T], I32, tag="slot_s")
-        w1_s = kept("w1_s", [P, H], U8, tag="slot_v")
+        tab_w = kept("tab_w", [P, T], I32)
+        w1_s = kept("w1_s", [P, H], U8)
         w1_w = kept("w1_w", [P, 2 * H], U8)
         w4_s = kept("w4_s", [P, R_PASSES, N], U8)
         w4_w = kept("w4_w", [P, R_PASSES, N], I32)
         gains = kept("gains", [P, R_PASSES, PACK], F32)
         planes = [kept("plane%d" % i, [P, T], F32) for i in range(PACK)]
         x_rows = xT.rearrange("(p i) t -> i p t", i=PACK)
+
+        def entries(idx, j0, width):
+            return idx[:, j0 // LIST_ROWS : (j0 + width) // LIST_ROWS]
 
         nc.vector.memset(tab_s[:].bitcast(I32), 0)
         nc.vector.memset(w1_s[:].bitcast(I32), 0)
@@ -65,15 +73,13 @@ def tile_list_photo_redshift_features_kernel(
         nc.scalar.dma_start(out=gains[:], in_=gain.rearrange("(g p t) -> p g t", g=R_PASSES, t=PACK))
         nc.sync.dma_start(out=w1_w[:].bitcast(I32), in_=w1_words[0].bitcast(I32))
         nc.sync.dma_start(idx1[:], offs)
-        load_scale_rows(nc.sync, tab_s, tab_scales[0])
+        load_scale_rows(tab_s, tab_scales[0])
         nc.sync.dma_start(out=tab_w[:], in_=tab_words[0].rearrange("p t i -> p (t i)").bitcast(I32))
-        load_scale_rows(nc.sync, w1_s, w1_scales[0])
+        load_scale_rows(w1_s, w1_scales[0])
         nc.sync.dma_start(out=planes[0][:], in_=x_rows[0])
         nc.sync.dma_start(idx2[:], offs2)
         nc.sync.dma_start(idx3[:], offs3)
 
-        warm = kept("warm", [P, R_PASSES, PACK], F32)
-        nc.scalar.activation(warm[:], gains[:], ACT.Gelu_apprx_tanh)
         minus_gains = kept("minus_gains", [P, R_PASSES, PACK], F32)
         nc.scalar.activation(minus_gains[:], gains[:], ACT.Copy, scale=-1.0)
 
@@ -86,33 +92,34 @@ def tile_list_photo_redshift_features_kernel(
             w1_w[:].bitcast(U16).rearrange("p (g m t) -> p g t m", g=R_PASSES, t=PACK),
         )
         v_w = [kept("v_w0", [P, HALF], U32)]
-        nc.vector.tensor_copy(v_w[0][:], tab_w[:].bitcast(U32).indirect(idx1[:, 0 : HALF // 16]))
+        nc.vector.tensor_copy(v_w[0][:], tab_w[:].bitcast(U32).indirect(entries(idx1, 0, HALF)))
         nc.vector.tensor_copy(
             w1_so[:].rearrange("p (g t m) -> p g t m", g=R_PASSES, t=PACK),
             w1_s[:].rearrange("p (g m t) -> p g t m", g=R_PASSES, t=PACK),
         )
-        v_w.append(kept("v_w1", [P, HALF], U32, tag="slot_v"))
-        nc.vector.tensor_copy(v_w[1][:], tab_w[:].bitcast(U32).indirect(idx1[:, HALF // 16 : S // 16]))
+        v_w.append(kept("v_w1", [P, HALF], U32, tag="w1_s"))
+        nc.vector.tensor_copy(v_w[1][:], tab_w[:].bitcast(U32).indirect(entries(idx1, HALF, HALF)))
 
         w2_raw = [kept("w2_raw%d" % g, [P, PACK, PASS], F32) for g in range(R_PASSES)]
-        w3_raw = [kept("w3_raw%d" % g, [P, PACK, N], F32, tag=("w3_raw0", "slot_s")[g]) for g in range(R_PASSES)]
+        w3_raw = [kept("w3_raw%d" % g, [P, PACK, N], F32, tag=("w3_raw0", "tab_w")[g]) for g in range(R_PASSES)]
         for g in range(R_PASSES):
             nc.sync.dma_start(
                 out=w2_raw[g][:], in_=w2[:, g * PASS : (g + 1) * PASS].rearrange("(p i) r -> p i r", i=PACK)
             )
             nc.sync.dma_start(out=planes[1 + g][:], in_=x_rows[1 + g])
-        nc.sync.dma_start(out=planes[3][:], in_=x_rows[3])
+        nc.sync.dma_start(out=planes[PACK - 1][:], in_=x_rows[PACK - 1])
         for g in range(R_PASSES):
             nc.sync.dma_start(
                 out=w3_raw[g][:], in_=w3[g * PASS : (g + 1) * PASS, :].rearrange("(p i) n -> p i n", i=PACK)
             )
         nc.sync.dma_start(out=w4_w[:], in_=w4_words.rearrange("a p c i -> p a (c i)").bitcast(I32))
-        load_scale_rows(nc.sync, w4_s, w4_scales.rearrange("a q c -> q a c"))
+        load_scale_rows(w4_s, w4_scales.rearrange("a q c -> q a c"))
 
         def on_gpsimd(j, g):
             return j % WIDE == 0 and j < SUMMED_FROM[g]
 
-        a_plain, a_gained = {}, {}
+        def sum_bank(shape):
+            return psum.tile(shape, F32, name="sum_bank", tag="sum_bank", bufs=SUM_BANKS)
 
         def template_pass(bank, j0, width, g, t, stop):
             r0 = g * PASS + t * P
@@ -127,28 +134,28 @@ def tile_list_photo_redshift_features_kernel(
                 stop=stop,
             )
 
-        a_tiles = {}
+        a_tiles, a_plain, a_gained = {}, {}, {}
 
         def template_product(half, g, slices=range(PACK)):
             needed = min(HALF, SUMMED_FROM[g] - half * HALF)
-            blocks = [j for j in range(half * HALF, (half + 1) * HALF, SUB) if not on_gpsimd(j, g)]
+            blocks = [j for j in range(half * HALF, (half + 1) * HALF, BLOCK) if not on_gpsimd(j, g)]
             if (half, g) not in a_tiles:
                 plain = kept("a_plain%d%d" % (half, g), [P, PACK, needed], F32)
-                gained = kept("a_gained%d%d" % (half, g), [P, PACK, len(blocks), SUB], F32)
+                gained = kept("a_gained%d%d" % (half, g), [P, PACK, len(blocks), BLOCK], F32)
                 a_tiles[half, g] = plain, gained
-                for j in range(half * HALF, half * HALF + needed, SUB):
-                    a_plain[j, g] = plain[:, :, j % HALF : j % HALF + SUB]
+                for j in range(half * HALF, half * HALF + needed, BLOCK):
+                    a_plain[j, g] = plain[:, :, j % HALF : j % HALF + BLOCK]
                 for n, j in enumerate(blocks):
                     a_gained[j, g] = gained[:, :, n, :]
             plain, gained = a_tiles[half, g]
-            first, step = blocks[0] % HALF // SUB, (blocks[1] - blocks[0]) // SUB
+            first, stride = blocks[0] % HALF // BLOCK, (blocks[1] - blocks[0]) // BLOCK
             for t in slices:
-                bank = psum.tile([P, HALF], F32, name="sum_bank", tag="sum_bank", bufs=4)
+                bank = sum_bank([P, HALF])
                 template_pass(bank[:], half * HALF, HALF, g, t, True)
                 nc.scalar.copy(plain[:, t, :], bank[:, 0:needed])
                 nc.scalar.activation(
                     gained[:, t, :, :],
-                    bank[:].rearrange("p (b c) -> p b c", c=SUB)[:, first : HALF // SUB : step, :],
+                    bank[:].rearrange("p (b c) -> p b c", c=BLOCK)[:, first : HALF // BLOCK : stride, :],
                     ACT.Copy,
                     scale=minus_gains[:, g, t : t + 1],
                 )
@@ -161,31 +168,32 @@ def tile_list_photo_redshift_features_kernel(
             )
             return codes, scales
 
+        def runs_in(rows, run):
+            return rows.rearrange("p t (c e) -> p c t e", e=run)
+
+        def runs_out(grouped, run):
+            return grouped.rearrange("p (c e) t -> p c t e", e=run)
+
         def interleave(grouped, rows):
-            nc.scalar.copy(
-                grouped.rearrange("p (c e) i -> p c i e", e=2), rows.rearrange("p i (c e) -> p c i e", e=2)
-            )
+            nc.scalar.copy(runs_out(grouped, 2), runs_in(rows, 2))
 
         colours = kept("colours", [P, PACK, S], F32)
 
-        def pick(i, j0, width, first):
-            nc.vector.tensor_copy(first[:], planes[i][:].indirect(idx2[:, j0 // 16 : (j0 + width) // 16]))
-            return first
+        def pick(i, j0, width, picked):
+            nc.vector.tensor_copy(picked[:], planes[i][:].indirect(entries(idx2, j0, width)))
+            return picked
 
-        def subtract(i, j0, width, first):
+        def subtract(i, j0, width, picked):
             nc.vector.tensor_tensor(
-                colours[:, i, j0 : j0 + width],
-                planes[i][:].indirect(idx3[:, j0 // 16 : (j0 + width) // 16]),
-                first[:],
-                ALU.subtract,
+                colours[:, i, j0 : j0 + width], planes[i][:].indirect(entries(idx3, j0, width)), picked[:], ALU.subtract
             )
 
         def gather_plane(i):
-            firsts = [
-                pick(i, j0, HALF, ring.tile([P, HALF], F32, name="first", tag="first", bufs=3)) for j0 in (0, HALF)
+            picks = [
+                pick(i, j0, HALF, ring.tile([P, HALF], F32, name="picked", tag="picked", bufs=3)) for j0 in (0, HALF)
             ]
-            for n, first in enumerate(firsts):
-                subtract(i, n * HALF, HALF, first)
+            for n, picked in enumerate(picks):
+                subtract(i, n * HALF, HALF, picked)
 
         def round_w2(g):
             grouped = kept("w2_grouped%d" % g, [P, PASS, PACK], BF16)
@@ -201,7 +209,7 @@ def tile_list_photo_redshift_features_kernel(
             cols = slice(part * N // 2, (part + 1) * N // 2)
             interleave(w3_grouped[g][:, cols, :], w3_raw[g][:, :, cols])
 
-        x_grouped = [kept("x_grouped%d" % q, [P, QUARTER, PACK], BF16) for q in range(4)]
+        x_grouped = [kept("x_grouped%d" % q, [P, QUARTER, PACK], BF16) for q in range(S // QUARTER)]
 
         def round_x(quarter):
             interleave(x_grouped[quarter][:], colours[:, :, quarter * QUARTER : (quarter + 1) * QUARTER])
@@ -218,20 +226,24 @@ def tile_list_photo_redshift_features_kernel(
         gather_plane(2)
         w2q = [quantize("w2q0", w2_grouped[0][:], PASS, tag="plane2")]
         last = PACK - 1
-        firsts = [pick(last, q * QUARTER, QUARTER, kept("last_first%d" % q, [P, QUARTER], F32)) for q in range(2)]
-        subtract(last, 0, QUARTER, firsts[0])
-        firsts.append(pick(last, 2 * QUARTER, QUARTER, kept("last_first2", [P, QUARTER], F32)))
-        subtract(last, QUARTER, QUARTER, firsts[1])
-        w2q.append(quantize("w2q1", w2_grouped[1][:], PASS, tag="last_first1"))
-        subtract(last, 2 * QUARTER, QUARTER, firsts[2])
+        picks = [pick(last, q * QUARTER, QUARTER, kept("last_pick%d" % q, [P, QUARTER], F32)) for q in range(2)]
+        subtract(last, 0, QUARTER, picks[0])
+        picks.append(pick(last, 2 * QUARTER, QUARTER, kept("last_pick2", [P, QUARTER], F32)))
+        subtract(last, QUARTER, QUARTER, picks[1])
+        w2q.append(quantize("w2q1", w2_grouped[1][:], PASS, tag="last_pick1"))
+        subtract(last, 2 * QUARTER, QUARTER, picks[2])
         template_product(1, 0)
-        template_product(1, 1, range(0, 2))
+        template_product(1, 1, range(0, EARLY_SLICES))
         round_x(0)
         round_x(1)
         xq = [quantize_x(0), quantize_x(1)]
-        firsts.append(pick(last, 3 * QUARTER, QUARTER, kept("last_first3", [P, QUARTER], F32, tag="x_grouped1")))
-        subtract(last, 3 * QUARTER, QUARTER, firsts[3])
+        picks.append(pick(last, 3 * QUARTER, QUARTER, kept("last_pick3", [P, QUARTER], F32, tag="x_grouped1")))
+        subtract(last, 3 * QUARTER, QUARTER, picks[3])
         w3q = []
+
+        starts = list(range(0, WIDE_END, WIDE)) + list(range(WIDE_END, S, BLOCK))
+        steps = [(j0, WIDE if j0 < WIDE_END else BLOCK, g) for j0 in starts for g in range(R_PASSES)]
+        wide_steps = R_PASSES * WIDE_END // WIDE
 
         def colour_pass(bank, j, g, t, start):
             quarter, c0 = divmod(j, QUARTER)
@@ -239,37 +251,25 @@ def tile_list_photo_redshift_features_kernel(
                 out=bank[:, t, :],
                 lhsT=w2q[g][0][:, t * P : (t + 1) * P].bitcast(FP8X4),
                 lhsT_scale=w2q[g][1][:, t * P : (t + 1) * P],
-                rhs=xq[quarter][0][:, c0 : c0 + SUB].bitcast(FP8X4),
-                rhs_scale=xq[quarter][1][:, c0 : c0 + SUB],
+                rhs=xq[quarter][0][:, c0 : c0 + BLOCK].bitcast(FP8X4),
+                rhs_scale=xq[quarter][1][:, c0 : c0 + BLOCK],
                 start=start,
                 stop=True,
             )
 
-        def block_bank():
-            return psum.tile([P, PACK, SUB], F32, name="block_bank", tag="block_bank", bufs=4)
-
-        def residual_in_psum(j0, g, grouped):
-            bank = psum.tile([P, PACK, SUB], F32, name="d_bank", tag="sum_bank", bufs=4)
+        def residual_in_psum(j, g, grouped):
+            bank = sum_bank([P, PACK, BLOCK])
             for t in range(PACK):
-                template_pass(bank[:, t, :], j0, SUB, g, t, False)
-                colour_pass(bank, j0, g, t, False)
+                template_pass(bank[:, t, :], j, BLOCK, g, t, False)
+                colour_pass(bank, j, g, t, False)
             interleave(grouped, bank[:])
 
-        def paired(ap):
-            return ap.rearrange("p t (c e) -> p c t e", e=2)
-
-        def join(grouped, a, bank, op):
-            nc.vector.tensor_tensor(grouped.rearrange("p (c e) t -> p c t e", e=2), paired(a), paired(bank[:]), op)
-
-        starts = list(range(0, WIDE_END, WIDE)) + list(range(WIDE_END, S, SUB))
-        steps = [(j0, WIDE if j0 < WIDE_END else SUB, g) for j0 in starts for g in range(R_PASSES)]
-        wide_steps = R_PASSES * WIDE_END // WIDE
         h_tiles, d_tiles = {}, {}
 
         def h_tile(s):
             if s in (wide_steps, wide_steps + 1):
                 if wide_steps not in h_tiles:
-                    h_tiles[wide_steps] = kept("h_both", [P, R_PASSES, SUB, PACK], BF16, tag="h_odd")
+                    h_tiles[wide_steps] = kept("h_both", [P, R_PASSES, BLOCK, PACK], BF16, tag="h_odd")
                 return h_tiles[wide_steps][:, s - wide_steps, :, :]
             if s not in h_tiles:
                 tag = ("x_grouped1", "h_odd")[s % 2] if s < wide_steps else None
@@ -282,64 +282,66 @@ def tile_list_photo_redshift_features_kernel(
             if s < R_PASSES:
                 return d_first[:, s, :, :]
             if s not in d_tiles:
-                d_tiles[s] = kept("d_grouped%d" % s, [P, WIDE, PACK], BF16, tag="d_grouped%d" % (s % 3 if s < wide_steps else s))
+                tag = "d_grouped%d" % (s % 3 if s < wide_steps else s)
+                d_tiles[s] = kept("d_grouped%d" % s, [P, WIDE, PACK], BF16, tag=tag)
             return d_tiles[s][:]
 
-        def in_fours(ap):
-            return ap.rearrange("p t (c e) -> p c t e", e=4)
-
-        banks = {}
+        b_banks = {}
 
         def colour_product(s):
             j0, width, g = steps[s]
-            for j in range(j0, j0 + width, SUB):
-                banks[j, g] = block_bank()
+            for j in range(j0, j0 + width, BLOCK):
+                bank = psum.tile([P, PACK, BLOCK], F32, name="block_bank", tag="block_bank", bufs=BLOCK_BANKS)
+                b_banks[j, g] = bank
                 for t in range(PACK):
-                    colour_pass(banks[j, g], j, g, t, True)
+                    colour_pass(bank, j, g, t, True)
                 if on_gpsimd(j, g):
-                    gained = kept("b_gained%d" % s, [P, PACK, SUB], F32)
+                    gained = kept("b_gained%d" % s, [P, PACK, BLOCK], F32)
                     for t in range(PACK):
                         nc.scalar.activation(
-                            gained[:, t, :], banks[j, g][:, t, :], ACT.Copy, scale=minus_gains[:, g, t : t + 1]
+                            gained[:, t, :], bank[:, t, :], ACT.Copy, scale=minus_gains[:, g, t : t + 1]
                         )
                     nc.gpsimd.tensor_tensor(
-                        h_tile(s)[:, 0:SUB, :].rearrange("p (c e) t -> p c t e", e=4),
-                        in_fours(a_plain[j, g]),
-                        in_fours(gained[:]),
+                        runs_out(h_tile(s)[:, 0:BLOCK, :], 4),
+                        runs_in(a_plain[j, g], 4),
+                        runs_in(gained[:], 4),
                         ALU.mult,
                     )
 
+        def join(grouped, a, bank, op):
+            nc.vector.tensor_tensor(runs_out(grouped, 2), runs_in(a, 2), runs_in(bank[:], 2), op)
+
         def meet(s):
             j0, width, g = steps[s]
-            for j in reversed(range(j0, j0 + width, SUB)):
-                cols = slice(j - j0, j - j0 + SUB)
+            for j in reversed(range(j0, j0 + width, BLOCK)):
+                cols = slice(j - j0, j - j0 + BLOCK)
                 if j < SUMMED_FROM[g]:
-                    join(d_tile(s)[:, cols, :], a_plain[j, g], banks[j, g], ALU.add)
+                    join(d_tile(s)[:, cols, :], a_plain[j, g], b_banks[j, g], ALU.add)
                 if not on_gpsimd(j, g):
-                    join(h_tile(s)[:, cols, :], a_gained[j, g], banks[j, g], ALU.mult)
+                    join(h_tile(s)[:, cols, :], a_gained[j, g], b_banks[j, g], ALU.mult)
 
         y_banks = {}
 
-        def y_passes(j0, width, weights, operand, last):
-            tiles_a_bank = 512 // width
+        def y_passes(j0, width, weights, operand, closes):
+            tiles_a_bank = BANK // width
             for n0 in range(0, N // P, tiles_a_bank):
-                first = (j0, n0) not in y_banks
-                if first:
-                    y_banks[j0, n0] = psum.tile([P, tiles_a_bank, width], F32, name="y_bank", tag="sum_bank", bufs=4)
+                opens = (j0, n0) not in y_banks
+                if opens:
+                    y_banks[j0, n0] = sum_bank([P, tiles_a_bank, width])
                 bank = y_banks[j0, n0]
                 for n in range(tiles_a_bank):
-                    rows = slice((n0 + n) * P, (n0 + n + 1) * P)
+                    cols = slice((n0 + n) * P, (n0 + n + 1) * P)
                     nc.tensor.matmul_mx(
                         out=bank[:, n, :],
-                        lhsT=weights[0][:, rows].bitcast(FP8X4),
-                        lhsT_scale=weights[1][:, rows],
+                        lhsT=weights[0][:, cols].bitcast(FP8X4),
+                        lhsT_scale=weights[1][:, cols],
                         rhs=operand[0].bitcast(FP8X4),
                         rhs_scale=operand[1],
-                        start=(first and n == 0),
-                        stop=(last and n == tiles_a_bank - 1),
+                        start=(opens and n == 0),
+                        stop=(closes and n == tiles_a_bank - 1),
                     )
-                if last:
-                    tiles = 2 if j0 + width == S else tiles_a_bank
+                if closes:
+                    tiles = tiles_a_bank // 2 if j0 + width == S else tiles_a_bank
                     for n in range(0, tiles_a_bank, tiles):
                         result = ring.tile([P, tiles, width], F32, name="result", tag="result", bufs=5)
                         nc.scalar.activation(result[:], bank[:, n : n + tiles, :], ACT.Gelu_apprx_tanh)
@@ -351,34 +353,23 @@ def tile_list_photo_redshift_features_kernel(
         def columns_of(quantized, c0, columns):
             return quantized[0][:, c0 : c0 + columns], quantized[1][:, c0 : c0 + columns]
 
-        def w4(g):
-            return w4_w[:, g, :], w4_s[:, g, :]
-
-        d_last = kept("d_last", [P, WIDE, PACK], BF16)
-
-        waiting = []
-
-        def h_passes(before):
-            for job in list(waiting):
-                j0, width, g, operand = job
-                if g < len(w3q) and j0 < before:
-                    y_passes(j0, width, w3q[g], operand, g == R_PASSES - 1)
-                    waiting.remove(job)
+        w4q = [(w4_w[:, g, :], w4_s[:, g, :]) for g in range(R_PASSES)]
 
         def second_stage(s):
             j0, width, g = steps[s]
-            hq = quantize("hq%d" % s, h_tile(s), width, tag=("b_gained%d" % (s + 1) if s + 1 < wide_steps else None))
-            waiting.append((j0, width, g, columns_of(hq, 0, width)))
+            tag = "b_gained%d" % (s + 1) if s + 1 < wide_steps else None
+            hq = quantize("hq%d" % s, h_tile(s), width, tag=tag)
             if s < wide_steps:
                 dq = quantize("dq%d" % s, d_tile(s), WIDE)
-                h_passes(j0)
-                y_passes(j0, width, w4(g), columns_of(dq, 0, WIDE), False)
-            h_passes(S)
+                y_passes(j0, width, w4q[g], columns_of(dq, 0, WIDE), False)
+            y_passes(j0, width, w3q[g], columns_of(hq, 0, width), g == R_PASSES - 1)
 
-        def both_passes(name, grouped, j0, weights, closes):
-            both = quantize(name, grouped, WIDE, tag=("b_gained6" if name == "dq_end" else None))
+        def both_passes(name, grouped, j0, weights, closes, tag=None):
+            both = quantize(name, grouped, WIDE, tag=tag)
             for g in range(R_PASSES):
-                y_passes(j0, SUB, weights(g), columns_of(both, g * SUB, SUB), closes and g == R_PASSES - 1)
+                y_passes(j0, BLOCK, weights[g], columns_of(both, g * BLOCK, BLOCK), closes and g == R_PASSES - 1)
+
+        d_last = kept("d_last", [P, WIDE, PACK], BF16)
 
         colour_product(0)
         colour_product(1)
@@ -389,35 +380,35 @@ def tile_list_photo_redshift_features_kernel(
             if s == 1:
                 round_w3(0, 1)
                 round_x(2)
+                round_w3(1, 0)
                 w3q.append(quantize("w3q0", w3_grouped[0][:], N))
             if s == 2:
-                round_w3(1, 0)
-                round_x(3)
                 round_w3(1, 1)
+                round_x(3)
                 xq.append(quantize_x(2))
-                template_product(1, 1, range(2, PACK))
+                w3q.append(quantize("w3q1", w3_grouped[1][:], N))
+                template_product(1, 1, range(EARLY_SLICES, PACK))
             if s == 3:
                 xq.append(quantize_x(3))
-                w3q.append(quantize("w3q1", w3_grouped[1][:], N))
             if s + 2 <= wide_steps:
                 colour_product(s + 2)
             if s + 1 == wide_steps:
                 for later in range(wide_steps + 1, len(steps)):
                     colour_product(later)
-            if s == 4:
-                for gs in range(R_PASSES):
-                    residual_in_psum(S - SUB, gs, d_last[:, gs * SUB : (gs + 1) * SUB, :])
+            if s + 2 == wide_steps:
+                for g in range(R_PASSES):
+                    residual_in_psum(S - BLOCK, g, d_last[:, g * BLOCK : (g + 1) * BLOCK, :])
             if s > 0:
                 second_stage(s - 1)
-            if s == 4:
-                residual_in_psum(WIDE_END, 1, d_tile(wide_steps)[:, SUB:WIDE, :])
-        both_passes("dq_last", d_last[:], S - SUB, w4, False)
+            if s + 2 == wide_steps:
+                residual_in_psum(WIDE_END, R_PASSES - 1, d_tile(wide_steps)[:, BLOCK:WIDE, :])
+
+        both_passes("dq_last", d_last[:], S - BLOCK, w4q, False)
         second_stage(wide_steps - 1)
-        for s in range(wide_steps, wide_steps + 3):
+        for s in range(wide_steps, len(steps) - 1):
             meet(s)
-        both_passes("dq_end", d_tile(wide_steps), WIDE_END, w4, False)
-        h_end = h_tiles[wide_steps][:].rearrange("p g c t -> p (g c) t")
-        both_passes("hq_end", h_end, WIDE_END, lambda g: w3q[g], True)
-        meet(wide_steps + 3)
-        second_stage(wide_steps + 2)
-        second_stage(wide_steps + 3)
+        both_passes("dq_end", d_tile(wide_steps), WIDE_END, w4q, False, tag="b_gained%d" % wide_steps)
+        both_passes("hq_end", h_tiles[wide_steps][:].rearrange("p g c t -> p (g c) t"), WIDE_END, w3q, True)
+        meet(len(steps) - 1)
+        second_stage(len(steps) - 2)
+        second_stage(len(steps) - 1)

@@ -31,6 +31,7 @@ SUMMED_FROM = (S - BLOCK, S - 2 * BLOCK)
 EARLY_SLICES = 2
 SUM_BANKS = 4
 BLOCK_BANKS = 4
+RUN = 4
 ALIGN = 64
 
 
@@ -140,22 +141,24 @@ def tile_list_photo_redshift_features_kernel(
             needed = min(HALF, SUMMED_FROM[g] - half * HALF)
             blocks = [j for j in range(half * HALF, (half + 1) * HALF, BLOCK) if not on_gpsimd(j, g)]
             if (half, g) not in a_tiles:
-                plain = kept("a_plain%d%d" % (half, g), [P, PACK, needed], F32)
-                gained = kept("a_gained%d%d" % (half, g), [P, PACK, len(blocks), BLOCK], F32)
+                plain = kept("a_plain%d%d" % (half, g), [P, needed // RUN, PACK, RUN], F32)
+                gained = kept("a_gained%d%d" % (half, g), [P, len(blocks), BLOCK // RUN, PACK, RUN], F32)
                 a_tiles[half, g] = plain, gained
                 for j in range(half * HALF, half * HALF + needed, BLOCK):
-                    a_plain[j, g] = plain[:, :, j % HALF : j % HALF + BLOCK]
+                    a_plain[j, g] = plain[:, j % HALF // RUN : (j % HALF + BLOCK) // RUN, :, :]
                 for n, j in enumerate(blocks):
-                    a_gained[j, g] = gained[:, :, n, :]
+                    a_gained[j, g] = gained[:, n, :, :, :]
             plain, gained = a_tiles[half, g]
             first, stride = blocks[0] % HALF // BLOCK, (blocks[1] - blocks[0]) // BLOCK
             for t in slices:
                 bank = sum_bank([P, HALF])
                 template_pass(bank[:], half * HALF, HALF, g, t, True)
-                nc.scalar.copy(plain[:, t, :], bank[:, 0:needed])
+                nc.scalar.copy(plain[:, :, t, :], bank[:, 0:needed].rearrange("p (c e) -> p c e", e=RUN))
                 nc.scalar.activation(
-                    gained[:, t, :, :],
-                    bank[:].rearrange("p (b c) -> p b c", c=BLOCK)[:, first : HALF // BLOCK : stride, :],
+                    gained[:, :, :, t, :],
+                    bank[:].rearrange("p (b c e) -> p b c e", c=BLOCK // RUN, e=RUN)[
+                        :, first : HALF // BLOCK : stride, :, :
+                    ],
                     ACT.Copy,
                     scale=minus_gains[:, g, t : t + 1],
                 )
@@ -296,20 +299,23 @@ def tile_list_photo_redshift_features_kernel(
                 for t in range(PACK):
                     colour_pass(bank, j, g, t, True)
                 if on_gpsimd(j, g):
-                    gained = kept("b_gained%d" % s, [P, PACK, BLOCK], F32)
+                    gained = kept("b_gained%d" % s, [P, BLOCK // RUN, PACK, RUN], F32)
                     for t in range(PACK):
                         nc.scalar.activation(
-                            gained[:, t, :], bank[:, t, :], ACT.Copy, scale=minus_gains[:, g, t : t + 1]
+                            gained[:, :, t, :],
+                            bank[:, t, :].rearrange("p (c e) -> p c e", e=RUN),
+                            ACT.Copy,
+                            scale=minus_gains[:, g, t : t + 1],
                         )
                     nc.gpsimd.tensor_tensor(
-                        runs_out(h_tile(s)[:, 0:BLOCK, :], 4),
-                        runs_in(a_plain[j, g], 4),
-                        runs_in(gained[:], 4),
+                        runs_out(h_tile(s)[:, 0:BLOCK, :], RUN),
+                        a_plain[j, g],
+                        gained[:],
                         ALU.mult,
                     )
 
         def join(grouped, a, bank, op):
-            nc.vector.tensor_tensor(runs_out(grouped, 2), runs_in(a, 2), runs_in(bank[:], 2), op)
+            nc.vector.tensor_tensor(runs_out(grouped, RUN), a, runs_in(bank[:], RUN), op)
 
         def meet(s):
             j0, width, g = steps[s]

@@ -28,10 +28,13 @@ BLOCK = BANK // PACK
 WIDE = 2 * BLOCK
 WIDE_END = S - 2 * BLOCK
 SUMMED_FROM = (S - BLOCK, S - 2 * BLOCK)
-EARLY_SLICES = 2
+EARLY_SLICES = 0
 SUM_BANKS = 4
 BLOCK_BANKS = 4
 RUN = 4
+W2_ON_GPSIMD = 48
+REGION = 4096
+HEAD_AT = 4 * REGION
 ALIGN = 64
 
 
@@ -42,6 +45,7 @@ def tile_list_photo_redshift_features_kernel(
     with ExitStack() as ctx:
         keep = ctx.enter_context(tc.tile_pool(name="keep", bufs=1))
         ring = ctx.enter_context(tc.tile_pool(name="ring", bufs=2))
+        laid = ctx.enter_context(tc.tile_pool(name="laid", bufs=1))
         psum = ctx.enter_context(tc.psum_pool(name="psum", bufs=1))
 
         def kept(name, shape, dtype, tag=None):
@@ -51,23 +55,33 @@ def tile_list_photo_redshift_features_kernel(
             for q in range(4):
                 nc.sync.dma_start(out=tile[32 * q : 32 * q + 4].bitcast(I32), in_=rows[4 * q : 4 * q + 4].bitcast(I32))
 
+        def placed(name, shape, dtype, offset):
+            return laid.tile(shape, dtype, name=name, tag=name, align_bytes=ALIGN, offset=offset)
+
         idx1 = kept("idx1", [P, S // LIST_ROWS], U16)
         idx2 = kept("idx2", [P, S // LIST_ROWS], U16)
         idx3 = kept("idx3", [P, S // LIST_ROWS], U16)
         tab_s = kept("tab_s", [P, T], U8)
         tab_w = kept("tab_w", [P, T], I32)
-        w1_s = kept("w1_s", [P, H], U8)
+        w1_s = placed("w1_s", [P, H], U8, HEAD_AT - H // 2)
         w1_w = kept("w1_w", [P, 2 * H], U8)
         w4_s = kept("w4_s", [P, R_PASSES, N], U8)
         w4_w = kept("w4_w", [P, R_PASSES, N], I32)
         gains = kept("gains", [P, R_PASSES, PACK], F32)
         planes = [kept("plane%d" % i, [P, T], F32) for i in range(PACK)]
         x_rows = xT.rearrange("(p i) t -> i p t", i=PACK)
+        early = PACK * W2_ON_GPSIMD
+        w2_early = kept("w2_early", [P, PACK, early], F32, tag="colours0")
+        w2_raw = [placed("w2_raw0", [P, PACK, PASS - early], F32, 0), kept("w2_raw1", [P, PACK, PASS], F32)]
+        w3_raw = [kept("w3_raw%d" % g, [P, PACK, N], F32, tag=("w3_raw0", "tab_w")[g]) for g in range(R_PASSES)]
 
         def entries(idx, j0, width):
             return idx[:, j0 // LIST_ROWS : (j0 + width) // LIST_ROWS]
 
-        nc.vector.memset(tab_s[:].bitcast(I32), 0)
+        def load_w2(tile, r0, r1):
+            nc.sync.dma_start(out=tile[:], in_=w2[:, r0:r1].rearrange("(p i) r -> p i r", i=PACK))
+
+        nc.gpsimd.memset(tab_s[:].bitcast(I32), 0)
         nc.vector.memset(w1_s[:].bitcast(I32), 0)
         nc.gpsimd.memset(w4_s[:].rearrange("p a c -> p (a c)").bitcast(I32), 0)
 
@@ -77,46 +91,40 @@ def tile_list_photo_redshift_features_kernel(
         load_scale_rows(tab_s, tab_scales[0])
         nc.sync.dma_start(out=tab_w[:], in_=tab_words[0].rearrange("p t i -> p (t i)").bitcast(I32))
         load_scale_rows(w1_s, w1_scales[0])
+        load_w2(w2_early, 0, early)
         nc.sync.dma_start(out=planes[0][:], in_=x_rows[0])
         nc.sync.dma_start(idx2[:], offs2)
         nc.sync.dma_start(idx3[:], offs3)
+        for i in range(1, PACK):
+            nc.sync.dma_start(out=planes[i][:], in_=x_rows[i])
+        load_w2(w2_raw[0], early, PASS)
+        load_w2(w2_raw[1], PASS, H)
 
         minus_gains = kept("minus_gains", [P, R_PASSES, PACK], F32)
+        warm = kept("warm", [P, 1], F32)
+        nc.scalar.activation(warm[:], gains[:, 0, 0:1], ACT.Gelu_apprx_tanh)
         nc.scalar.activation(minus_gains[:], gains[:], ACT.Copy, scale=-1.0)
 
-        v_s = kept("v_s", [P, S], U8)
-        nc.vector.tensor_copy(v_s[:], tab_s[:].indirect(idx1[:]))
         w1_wo = kept("w1_wo", [P, 2 * H], U8)
         w1_so = kept("w1_so", [P, H], U8)
         nc.vector.tensor_copy(
             w1_wo[:].bitcast(U16).rearrange("p (g t m) -> p g t m", g=R_PASSES, t=PACK),
             w1_w[:].bitcast(U16).rearrange("p (g m t) -> p g t m", g=R_PASSES, t=PACK),
         )
+        v_s = kept("v_s", [P, S], U8)
+        nc.vector.tensor_copy(v_s[:], tab_s[:].indirect(idx1[:]))
         v_w = [kept("v_w0", [P, HALF], U32)]
         nc.vector.tensor_copy(v_w[0][:], tab_w[:].bitcast(U32).indirect(entries(idx1, 0, HALF)))
         nc.vector.tensor_copy(
             w1_so[:].rearrange("p (g t m) -> p g t m", g=R_PASSES, t=PACK),
             w1_s[:].rearrange("p (g m t) -> p g t m", g=R_PASSES, t=PACK),
         )
-        v_w.append(kept("v_w1", [P, HALF], U32, tag="w1_s"))
+        v_w.append(placed("v_w1", [P, HALF], U32, HEAD_AT))
         nc.vector.tensor_copy(v_w[1][:], tab_w[:].bitcast(U32).indirect(entries(idx1, HALF, HALF)))
 
-        w2_raw = [kept("w2_raw%d" % g, [P, PACK, PASS], F32) for g in range(R_PASSES)]
-        w3_raw = [kept("w3_raw%d" % g, [P, PACK, N], F32, tag=("w3_raw0", "tab_w")[g]) for g in range(R_PASSES)]
-        for g in range(R_PASSES):
-            nc.sync.dma_start(
-                out=w2_raw[g][:], in_=w2[:, g * PASS : (g + 1) * PASS].rearrange("(p i) r -> p i r", i=PACK)
-            )
-            nc.sync.dma_start(out=planes[1 + g][:], in_=x_rows[1 + g])
-        nc.sync.dma_start(out=planes[PACK - 1][:], in_=x_rows[PACK - 1])
-        for g in range(R_PASSES):
-            nc.sync.dma_start(
-                out=w3_raw[g][:], in_=w3[g * PASS : (g + 1) * PASS, :].rearrange("(p i) n -> p i n", i=PACK)
-            )
-        nc.sync.dma_start(out=w4_w[:], in_=w4_words.rearrange("a p c i -> p a (c i)").bitcast(I32))
-        load_scale_rows(w4_s, w4_scales.rearrange("a q c -> q a c"))
-
         def on_gpsimd(j, g):
+            if j < HALF:
+                return (j, g) != (HALF - BLOCK, R_PASSES - 1)
             return j % WIDE == 0 and j < SUMMED_FROM[g]
 
         def sum_bank(shape):
@@ -142,26 +150,30 @@ def tile_list_photo_redshift_features_kernel(
             blocks = [j for j in range(half * HALF, (half + 1) * HALF, BLOCK) if not on_gpsimd(j, g)]
             if (half, g) not in a_tiles:
                 plain = kept("a_plain%d%d" % (half, g), [P, needed // RUN, PACK, RUN], F32)
-                gained = kept("a_gained%d%d" % (half, g), [P, len(blocks), BLOCK // RUN, PACK, RUN], F32)
+                gained = None
+                if blocks:
+                    gained = kept("a_gained%d%d" % (half, g), [P, len(blocks), BLOCK // RUN, PACK, RUN], F32)
                 a_tiles[half, g] = plain, gained
                 for j in range(half * HALF, half * HALF + needed, BLOCK):
                     a_plain[j, g] = plain[:, j % HALF // RUN : (j % HALF + BLOCK) // RUN, :, :]
                 for n, j in enumerate(blocks):
                     a_gained[j, g] = gained[:, n, :, :, :]
             plain, gained = a_tiles[half, g]
-            first, stride = blocks[0] % HALF // BLOCK, (blocks[1] - blocks[0]) // BLOCK
             for t in slices:
                 bank = sum_bank([P, HALF])
                 template_pass(bank[:], half * HALF, HALF, g, t, True)
                 nc.scalar.copy(plain[:, :, t, :], bank[:, 0:needed].rearrange("p (c e) -> p c e", e=RUN))
-                nc.scalar.activation(
-                    gained[:, :, :, t, :],
-                    bank[:].rearrange("p (b c e) -> p b c e", c=BLOCK // RUN, e=RUN)[
-                        :, first : HALF // BLOCK : stride, :, :
-                    ],
-                    ACT.Copy,
-                    scale=minus_gains[:, g, t : t + 1],
-                )
+                if blocks:
+                    first = blocks[0] % HALF // BLOCK
+                    stride = (blocks[1] - blocks[0]) // BLOCK if len(blocks) > 1 else 1
+                    nc.scalar.activation(
+                        gained[:, :, :, t, :],
+                        bank[:].rearrange("p (b c e) -> p b c e", c=BLOCK // RUN, e=RUN)[
+                            :, first : HALF // BLOCK : stride, :, :
+                        ],
+                        ACT.Copy,
+                        scale=minus_gains[:, g, t : t + 1],
+                    )
 
         def quantize(name, grouped, width, tag=None):
             codes = kept(name + "_w", [P, width], U32, tag=tag)
@@ -180,73 +192,85 @@ def tile_list_photo_redshift_features_kernel(
         def interleave(grouped, rows):
             nc.scalar.copy(runs_out(grouped, 2), runs_in(rows, 2))
 
-        colours = kept("colours", [P, PACK, S], F32)
+        quarters = S // QUARTER
+        colours = [kept("colours%d" % q, [P, PACK, QUARTER], F32, tag="colours%d" % (q % 2)) for q in range(quarters)]
 
         def pick(i, j0, width, picked):
             nc.vector.tensor_copy(picked[:], planes[i][:].indirect(entries(idx2, j0, width)))
             return picked
 
-        def subtract(i, j0, width, picked):
+        def subtract(i, q, picked):
             nc.vector.tensor_tensor(
-                colours[:, i, j0 : j0 + width], planes[i][:].indirect(entries(idx3, j0, width)), picked[:], ALU.subtract
+                colours[q][:, i, :], planes[i][:].indirect(entries(idx3, q * QUARTER, QUARTER)), picked, ALU.subtract
             )
 
-        def gather_plane(i):
-            picks = [
-                pick(i, j0, HALF, ring.tile([P, HALF], F32, name="picked", tag="picked", bufs=3)) for j0 in (0, HALF)
-            ]
-            for n, picked in enumerate(picks):
-                subtract(i, n * HALF, HALF, picked)
+        def subtract_late(i, picked):
+            for n in range(2):
+                subtract(i, 2 + n, picked[:, n * QUARTER : (n + 1) * QUARTER])
 
-        def round_w2(g):
-            grouped = kept("w2_grouped%d" % g, [P, PASS, PACK], BF16)
+        w2_grouped = [placed("w2_grouped%d" % g, [P, PASS, PACK], BF16, REGION * (3 - 2 * g)) for g in range(R_PASSES)]
+        w3_grouped = [placed("w3_grouped%d" % g, [P, N, PACK], BF16, REGION * (2 + g)) for g in range(R_PASSES)]
+
+        def round_w2(g, m0=0):
             nc.scalar.copy(
-                grouped[:].rearrange("p (t m) i -> p m t i", t=PACK),
+                w2_grouped[g][:].rearrange("p (t m) i -> p m t i", t=PACK)[:, m0:P],
                 w2_raw[g][:].rearrange("p i (m t) -> p m t i", t=PACK),
             )
-            return grouped
 
-        w3_grouped = [kept("w3_grouped%d" % g, [P, N, PACK], BF16, tag="w2_grouped%d" % g) for g in range(R_PASSES)]
+        def round_on_gpsimd(grouped, rows):
+            nc.gpsimd.tensor_scalar(grouped, rows, 1.0, 0.0, ALU.mult, ALU.add)
 
         def round_w3(g, part):
             cols = slice(part * N // 2, (part + 1) * N // 2)
             interleave(w3_grouped[g][:, cols, :], w3_raw[g][:, :, cols])
 
-        x_grouped = [kept("x_grouped%d" % q, [P, QUARTER, PACK], BF16) for q in range(S // QUARTER)]
+        x_grouped = [kept("x_grouped%d" % q, [P, QUARTER, PACK], BF16) for q in range(quarters)]
+        x_grouped[1] = placed("x_grouped1", [P, QUARTER, PACK], BF16, REGION // 4)
 
-        def round_x(quarter):
-            interleave(x_grouped[quarter][:], colours[:, :, quarter * QUARTER : (quarter + 1) * QUARTER])
+        def round_x(q):
+            interleave(x_grouped[q][:], colours[q][:])
 
-        def quantize_x(quarter):
-            return quantize("xq%d" % quarter, x_grouped[quarter][:], QUARTER)
+        def quantize_x(q, tag=None):
+            return quantize("xq%d" % q, x_grouped[q][:], QUARTER, tag=tag)
 
-        gather_plane(0)
-        template_product(0, 0)
-        w2_grouped = [round_w2(0)]
-        gather_plane(1)
-        template_product(0, 1)
-        w2_grouped.append(round_w2(1))
-        gather_plane(2)
-        w2q = [quantize("w2q0", w2_grouped[0][:], PASS, tag="plane2")]
-        last = PACK - 1
-        picks = [pick(last, q * QUARTER, QUARTER, kept("last_pick%d" % q, [P, QUARTER], F32)) for q in range(2)]
-        subtract(last, 0, QUARTER, picks[0])
-        picks.append(pick(last, 2 * QUARTER, QUARTER, kept("last_pick2", [P, QUARTER], F32)))
-        subtract(last, QUARTER, QUARTER, picks[1])
-        w2q.append(quantize("w2q1", w2_grouped[1][:], PASS, tag="last_pick1"))
-        subtract(last, 2 * QUARTER, QUARTER, picks[2])
-        template_product(1, 0)
-        template_product(1, 1, range(0, EARLY_SLICES))
-        round_x(0)
+        round_on_gpsimd(
+            w2_grouped[0][:].rearrange("p (t m) i -> p m t i", t=PACK)[:, 0:W2_ON_GPSIMD],
+            w2_early[:].rearrange("p i (m t) -> p m t i", t=PACK),
+        )
+        w2q = []
+        for i in range(PACK):
+            picks = [
+                pick(i, q * QUARTER, QUARTER, kept("pick%d%d" % (i, q), [P, QUARTER], F32, tag="pick%d%d" % (i % 2, q)))
+                for q in range(2)
+            ]
+            for q in range(2):
+                subtract(i, q, picks[q][:])
+            if i == 0:
+                template_product(0, 0)
+                template_product(0, 1)
+                template_product(1, 0)
+                template_product(1, 1, range(0, EARLY_SLICES))
+        for g in range(R_PASSES):
+            nc.sync.dma_start(
+                out=w3_raw[g][:], in_=w3[g * PASS : (g + 1) * PASS, :].rearrange("(p i) n -> p i n", i=PACK)
+            )
+        nc.sync.dma_start(out=w4_w[:], in_=w4_words.rearrange("a p c i -> p a (c i)").bitcast(I32))
+        load_scale_rows(w4_s, w4_scales.rearrange("a q c -> q a c"))
+        picked = pick(0, HALF, HALF, kept("late_pick0", [P, HALF], F32, tag="pick10"))
+        round_on_gpsimd(x_grouped[0][:], colours[0][:].rearrange("p t c -> p c t"))
+        round_w2(0, W2_ON_GPSIMD)
         round_x(1)
-        xq = [quantize_x(0), quantize_x(1)]
-        picks.append(pick(last, 3 * QUARTER, QUARTER, kept("last_pick3", [P, QUARTER], F32, tag="x_grouped1")))
-        subtract(last, 3 * QUARTER, QUARTER, picks[3])
+        xq = [quantize_x(0)]
+        w2q.append(quantize("w2q0", w2_grouped[0][:], PASS, tag=None))
+        subtract(0, 2, picked[:, 0:QUARTER])
+        xq.append(quantize_x(1))
+        subtract(0, 3, picked[:, QUARTER:HALF])
         w3q = []
 
-        starts = list(range(0, WIDE_END, WIDE)) + list(range(WIDE_END, S, BLOCK))
-        steps = [(j0, WIDE if j0 < WIDE_END else BLOCK, g) for j0 in starts for g in range(R_PASSES)]
-        wide_steps = R_PASSES * WIDE_END // WIDE
+        steps = [(j0, WIDE, g) for g in range(R_PASSES) for j0 in (0, WIDE)]
+        steps += [(HALF, WIDE, g) for g in range(R_PASSES)]
+        wide_steps = len(steps)
+        steps += [(j0, BLOCK, g) for j0 in range(WIDE_END, S, BLOCK) for g in range(R_PASSES)]
 
         def colour_pass(bank, j, g, t, start):
             quarter, c0 = divmod(j, QUARTER)
@@ -267,29 +291,20 @@ def tile_list_photo_redshift_features_kernel(
                 colour_pass(bank, j, g, t, False)
             interleave(grouped, bank[:])
 
-        h_tiles, d_tiles = {}, {}
+        h_tiles = [placed("h%d" % s, [P, WIDE, PACK], BF16, REGION * min(s, 3)) for s in range(wide_steps + 1)]
+        h_last = [kept("h_last%d" % g, [P, BLOCK, PACK], BF16) for g in range(R_PASSES)]
+        d_tiles = [kept("d%d" % s, [P, WIDE, PACK], BF16, tag="d%d" % (s % 2)) for s in range(wide_steps)]
+        d_tiles.append(kept("d_end", [P, WIDE, PACK], BF16))
+        d_last = kept("d_last", [P, WIDE, PACK], BF16)
 
         def h_tile(s):
-            if s in (wide_steps, wide_steps + 1):
-                if wide_steps not in h_tiles:
-                    h_tiles[wide_steps] = kept("h_both", [P, R_PASSES, BLOCK, PACK], BF16, tag="h_odd")
-                return h_tiles[wide_steps][:, s - wide_steps, :, :]
-            if s not in h_tiles:
-                tag = ("x_grouped1", "h_odd")[s % 2] if s < wide_steps else None
-                h_tiles[s] = kept("h_grouped%d" % s, [P, steps[s][1], PACK], BF16, tag=tag)
-            return h_tiles[s][:]
+            if s < wide_steps:
+                return h_tiles[s][:]
+            if s < wide_steps + R_PASSES:
+                return h_tiles[wide_steps][:, (s - wide_steps) * BLOCK : (s - wide_steps + 1) * BLOCK, :]
+            return h_last[s - wide_steps - R_PASSES][:]
 
-        d_first = kept("d_first", [P, R_PASSES, WIDE, PACK], BF16, tag="plane3")
-
-        def d_tile(s):
-            if s < R_PASSES:
-                return d_first[:, s, :, :]
-            if s not in d_tiles:
-                tag = "d_grouped%d" % (s % 3 if s < wide_steps else s)
-                d_tiles[s] = kept("d_grouped%d" % s, [P, WIDE, PACK], BF16, tag=tag)
-            return d_tiles[s][:]
-
-        b_banks = {}
+        b_banks, b_gained = {}, {}
 
         def colour_product(s):
             j0, width, g = steps[s]
@@ -299,7 +314,8 @@ def tile_list_photo_redshift_features_kernel(
                 for t in range(PACK):
                     colour_pass(bank, j, g, t, True)
                 if on_gpsimd(j, g):
-                    gained = kept("b_gained%d" % s, [P, BLOCK // RUN, PACK, RUN], F32)
+                    gained = kept("b_gained%d_%d" % (s, j - j0), [P, BLOCK // RUN, PACK, RUN], F32)
+                    b_gained[j, g] = gained
                     for t in range(PACK):
                         nc.scalar.activation(
                             gained[:, :, t, :],
@@ -307,24 +323,31 @@ def tile_list_photo_redshift_features_kernel(
                             ACT.Copy,
                             scale=minus_gains[:, g, t : t + 1],
                         )
-                    nc.gpsimd.tensor_tensor(
-                        runs_out(h_tile(s)[:, 0:BLOCK, :], RUN),
-                        a_plain[j, g],
-                        gained[:],
-                        ALU.mult,
-                    )
+
+        def last_gained(s):
+            j0, width, g = steps[s]
+            return "b_gained%d_%d" % (s, max(j - j0 for j in range(j0, j0 + width, BLOCK) if on_gpsimd(j, g)))
 
         def join(grouped, a, bank, op):
             nc.vector.tensor_tensor(runs_out(grouped, RUN), a, runs_in(bank[:], RUN), op)
 
         def meet(s):
             j0, width, g = steps[s]
-            for j in reversed(range(j0, j0 + width, BLOCK)):
-                cols = slice(j - j0, j - j0 + BLOCK)
-                if j < SUMMED_FROM[g]:
-                    join(d_tile(s)[:, cols, :], a_plain[j, g], b_banks[j, g], ALU.add)
+            blocks = list(range(j0, j0 + width, BLOCK))
+            for j in blocks:
+                if on_gpsimd(j, g):
+                    nc.gpsimd.tensor_tensor(
+                        runs_out(h_tile(s)[:, j - j0 : j - j0 + BLOCK, :], RUN),
+                        a_plain[j, g],
+                        b_gained[j, g][:],
+                        ALU.mult,
+                    )
+            for j in blocks:
                 if not on_gpsimd(j, g):
-                    join(h_tile(s)[:, cols, :], a_gained[j, g], b_banks[j, g], ALU.mult)
+                    join(h_tile(s)[:, j - j0 : j - j0 + BLOCK, :], a_gained[j, g], b_banks[j, g], ALU.mult)
+            for j in blocks:
+                if j < SUMMED_FROM[g]:
+                    join(d_tiles[s][:, j - j0 : j - j0 + BLOCK, :], a_plain[j, g], b_banks[j, g], ALU.add)
 
         y_banks = {}
 
@@ -361,60 +384,88 @@ def tile_list_photo_redshift_features_kernel(
 
         w4q = [(w4_w[:, g, :], w4_s[:, g, :]) for g in range(R_PASSES)]
 
-        def second_stage(s):
+        hq = {}
+
+        def quantize_h(s, tag=None):
+            hq[s] = quantize("hq%d" % s, h_tile(s), steps[s][1], tag=tag)
+
+        def h_term(s):
             j0, width, g = steps[s]
-            tag = "b_gained%d" % (s + 1) if s + 1 < wide_steps else None
-            hq = quantize("hq%d" % s, h_tile(s), width, tag=tag)
-            if s < wide_steps:
-                dq = quantize("dq%d" % s, d_tile(s), WIDE)
-                y_passes(j0, width, w4q[g], columns_of(dq, 0, WIDE), False)
-            y_passes(j0, width, w3q[g], columns_of(hq, 0, width), g == R_PASSES - 1)
+            y_passes(j0, width, w3q[g], columns_of(hq[s], 0, width), g == R_PASSES - 1)
+
+        def d_term(s):
+            j0, width, g = steps[s]
+            y_passes(j0, width, w4q[g], columns_of(quantize("dq%d" % s, d_tiles[s][:], WIDE), 0, WIDE), False)
 
         def both_passes(name, grouped, j0, weights, closes, tag=None):
             both = quantize(name, grouped, WIDE, tag=tag)
             for g in range(R_PASSES):
                 y_passes(j0, BLOCK, weights[g], columns_of(both, g * BLOCK, BLOCK), closes and g == R_PASSES - 1)
 
-        d_last = kept("d_last", [P, WIDE, PACK], BF16)
-
         colour_product(0)
+        round_w2(1)
         colour_product(1)
         for s in range(wide_steps):
+            if s + 1 < PACK:
+                picked = pick(s + 1, HALF, HALF, placed("late_pick%d" % (s + 1), [P, HALF], F32, REGION * s + REGION // 2))
             meet(s)
+            if s + 1 < PACK:
+                subtract_late(s + 1, picked)
             if s == 0:
+                quantize_h(s)
+                w2q.append(quantize("w2q1", w2_grouped[1][:], PASS, tag=last_gained(s)))
                 round_w3(0, 0)
-            if s == 1:
                 round_w3(0, 1)
-                round_x(2)
+                colour_product(2)
+                d_term(s)
+            if s == 1:
+                quantize_h(s)
+                w3q.append(quantize("w3q0", w3_grouped[0][:], N, tag=last_gained(s)))
                 round_w3(1, 0)
-                w3q.append(quantize("w3q0", w3_grouped[0][:], N))
-            if s == 2:
                 round_w3(1, 1)
+                colour_product(3)
+                dq1 = quantize("dq1", d_tiles[s][:], WIDE)
+                h_term(0)
+            if s == 2:
+                round_x(2)
                 round_x(3)
+                quantize_h(s)
+                d_term(s)
+                w3q.append(quantize("w3q1", w3_grouped[1][:], N, tag=last_gained(s)))
                 xq.append(quantize_x(2))
-                w3q.append(quantize("w3q1", w3_grouped[1][:], N))
+                colour_product(4)
+                h_term(s)
                 template_product(1, 1, range(EARLY_SLICES, PACK))
+                y_passes(WIDE, WIDE, w4q[0], columns_of(dq1, 0, WIDE), False)
+                h_term(1)
             if s == 3:
-                xq.append(quantize_x(3))
-            if s + 2 <= wide_steps:
-                colour_product(s + 2)
-            if s + 1 == wide_steps:
-                for later in range(wide_steps + 1, len(steps)):
-                    colour_product(later)
-            if s + 2 == wide_steps:
+                xq.append(quantize_x(3, tag=last_gained(s)))
+                colour_product(5)
+                quantize_h(s)
                 for g in range(R_PASSES):
                     residual_in_psum(S - BLOCK, g, d_last[:, g * BLOCK : (g + 1) * BLOCK, :])
-            if s > 0:
-                second_stage(s - 1)
-            if s + 2 == wide_steps:
-                residual_in_psum(WIDE_END, R_PASSES - 1, d_tile(wide_steps)[:, BLOCK:WIDE, :])
+                d_term(s)
+                h_term(s)
+            if s == 4:
+                quantize_h(s)
+                colour_product(wide_steps)
+                colour_product(wide_steps + 1)
+                residual_in_psum(WIDE_END, R_PASSES - 1, d_tiles[wide_steps][:, BLOCK:WIDE, :])
+                d_term(s)
+                h_term(s)
+            if s == 5:
+                colour_product(wide_steps + 2)
+                colour_product(wide_steps + 3)
+                both_passes("dq_last", d_last[:], S - BLOCK, w4q, False, tag=last_gained(s))
+                quantize_h(s)
+                d_term(s)
+                h_term(s)
 
-        both_passes("dq_last", d_last[:], S - BLOCK, w4q, False)
-        second_stage(wide_steps - 1)
         for s in range(wide_steps, len(steps) - 1):
             meet(s)
-        both_passes("dq_end", d_tile(wide_steps), WIDE_END, w4q, False, tag="b_gained%d" % wide_steps)
-        both_passes("hq_end", h_tiles[wide_steps][:].rearrange("p g c t -> p (g c) t"), WIDE_END, w3q, True)
+        both_passes("dq_end", d_tiles[wide_steps][:], WIDE_END, w4q, False, tag=last_gained(wide_steps))
+        both_passes("hq_end", h_tiles[wide_steps][:], WIDE_END, w3q, True)
         meet(len(steps) - 1)
-        second_stage(len(steps) - 2)
-        second_stage(len(steps) - 1)
+        for s in range(len(steps) - R_PASSES, len(steps)):
+            quantize_h(s)
+            h_term(s)

@@ -28,7 +28,7 @@ BLOCK = BANK // PACK
 WIDE = 2 * BLOCK
 WIDE_END = S - 2 * BLOCK
 SUMMED_FROM = (S - BLOCK, S - 2 * BLOCK)
-EARLY_SLICES = 0
+EARLY_SLICES = 2
 SUM_BANKS = 4
 BLOCK_BANKS = 4
 RUN = 4
@@ -63,7 +63,7 @@ def tile_list_photo_redshift_features_kernel(
         idx3 = kept("idx3", [P, S // LIST_ROWS], U16)
         tab_s = kept("tab_s", [P, T], U8)
         tab_w = kept("tab_w", [P, T], I32)
-        w1_s = placed("w1_s", [P, H], U8, HEAD_AT - H // 2)
+        w1_s = placed("w1_s", [P, H], U8, HEAD_AT)
         w1_w = kept("w1_w", [P, 2 * H], U8)
         w4_s = kept("w4_s", [P, R_PASSES, N], U8)
         w4_w = kept("w4_w", [P, R_PASSES, N], I32)
@@ -71,7 +71,7 @@ def tile_list_photo_redshift_features_kernel(
         planes = [kept("plane%d" % i, [P, T], F32) for i in range(PACK)]
         x_rows = xT.rearrange("(p i) t -> i p t", i=PACK)
         early = PACK * W2_ON_GPSIMD
-        w2_early = kept("w2_early", [P, PACK, early], F32, tag="colours0")
+        w2_early = kept("w2_early", [P, PACK, early], F32)
         w2_raw = [placed("w2_raw0", [P, PACK, PASS - early], F32, 0), kept("w2_raw1", [P, PACK, PASS], F32)]
         w3_raw = [kept("w3_raw%d" % g, [P, PACK, N], F32, tag=("w3_raw0", "tab_w")[g]) for g in range(R_PASSES)]
 
@@ -91,10 +91,10 @@ def tile_list_photo_redshift_features_kernel(
         load_scale_rows(tab_s, tab_scales[0])
         nc.sync.dma_start(out=tab_w[:], in_=tab_words[0].rearrange("p t i -> p (t i)").bitcast(I32))
         load_scale_rows(w1_s, w1_scales[0])
-        load_w2(w2_early, 0, early)
         nc.sync.dma_start(out=planes[0][:], in_=x_rows[0])
         nc.sync.dma_start(idx2[:], offs2)
         nc.sync.dma_start(idx3[:], offs3)
+        load_w2(w2_early, 0, early)
         for i in range(1, PACK):
             nc.sync.dma_start(out=planes[i][:], in_=x_rows[i])
         load_w2(w2_raw[0], early, PASS)
@@ -233,19 +233,20 @@ def tile_list_photo_redshift_features_kernel(
         def quantize_x(q, tag=None):
             return quantize("xq%d" % q, x_grouped[q][:], QUARTER, tag=tag)
 
-        round_on_gpsimd(
-            w2_grouped[0][:].rearrange("p (t m) i -> p m t i", t=PACK)[:, 0:W2_ON_GPSIMD],
-            w2_early[:].rearrange("p i (m t) -> p m t i", t=PACK),
-        )
         w2q = []
         for i in range(PACK):
-            picks = [
-                pick(i, q * QUARTER, QUARTER, kept("pick%d%d" % (i, q), [P, QUARTER], F32, tag="pick%d%d" % (i % 2, q)))
-                for q in range(2)
-            ]
+            picks = [kept("pick%d%d" % (i, q), [P, QUARTER], F32, tag="pick%d%d" % (i % 2, q)) for q in range(2)]
+            if i == 0:
+                picks[0] = placed("first_pick", [P, QUARTER], F32, 3 * REGION)
+            for q in range(2):
+                pick(i, q * QUARTER, QUARTER, picks[q])
             for q in range(2):
                 subtract(i, q, picks[q][:])
             if i == 0:
+                round_on_gpsimd(
+                    w2_grouped[0][:].rearrange("p (t m) i -> p m t i", t=PACK)[:, 0:W2_ON_GPSIMD],
+                    w2_early[:].rearrange("p i (m t) -> p m t i", t=PACK),
+                )
                 template_product(0, 0)
                 template_product(0, 1)
                 template_product(1, 0)
@@ -294,8 +295,8 @@ def tile_list_photo_redshift_features_kernel(
         h_tiles = [placed("h%d" % s, [P, WIDE, PACK], BF16, REGION * min(s, 3)) for s in range(wide_steps + 1)]
         h_last = [kept("h_last%d" % g, [P, BLOCK, PACK], BF16) for g in range(R_PASSES)]
         d_tiles = [kept("d%d" % s, [P, WIDE, PACK], BF16, tag="d%d" % (s % 2)) for s in range(wide_steps)]
-        d_tiles.append(kept("d_end", [P, WIDE, PACK], BF16))
-        d_last = kept("d_last", [P, WIDE, PACK], BF16)
+        d_tiles.append(kept("d_end", [P, BLOCK, PACK], BF16))
+        d_last = kept("d_last", [P, 3 * BLOCK, PACK], BF16)
 
         def h_tile(s):
             if s < wide_steps:
@@ -308,25 +309,25 @@ def tile_list_photo_redshift_features_kernel(
 
         def colour_product(s):
             j0, width, g = steps[s]
+            theirs = [j for j in range(j0, j0 + width, BLOCK) if on_gpsimd(j, g)]
+            if theirs:
+                b_gained[s] = kept("b_gained%d" % s, [P, len(theirs), BLOCK // RUN, PACK, RUN], F32)
             for j in range(j0, j0 + width, BLOCK):
                 bank = psum.tile([P, PACK, BLOCK], F32, name="block_bank", tag="block_bank", bufs=BLOCK_BANKS)
                 b_banks[j, g] = bank
                 for t in range(PACK):
                     colour_pass(bank, j, g, t, True)
                 if on_gpsimd(j, g):
-                    gained = kept("b_gained%d_%d" % (s, j - j0), [P, BLOCK // RUN, PACK, RUN], F32)
-                    b_gained[j, g] = gained
                     for t in range(PACK):
                         nc.scalar.activation(
-                            gained[:, :, t, :],
+                            b_gained[s][:, (j - j0) // BLOCK, :, t, :],
                             bank[:, t, :].rearrange("p (c e) -> p c e", e=RUN),
                             ACT.Copy,
                             scale=minus_gains[:, g, t : t + 1],
                         )
 
         def last_gained(s):
-            j0, width, g = steps[s]
-            return "b_gained%d_%d" % (s, max(j - j0 for j in range(j0, j0 + width, BLOCK) if on_gpsimd(j, g)))
+            return "b_gained%d" % s
 
         def join(grouped, a, bank, op):
             nc.vector.tensor_tensor(runs_out(grouped, RUN), a, runs_in(bank[:], RUN), op)
@@ -334,14 +335,15 @@ def tile_list_photo_redshift_features_kernel(
         def meet(s):
             j0, width, g = steps[s]
             blocks = list(range(j0, j0 + width, BLOCK))
-            for j in blocks:
-                if on_gpsimd(j, g):
-                    nc.gpsimd.tensor_tensor(
-                        runs_out(h_tile(s)[:, j - j0 : j - j0 + BLOCK, :], RUN),
-                        a_plain[j, g],
-                        b_gained[j, g][:],
-                        ALU.mult,
-                    )
+            theirs = [j - j0 for j in blocks if on_gpsimd(j, g)]
+            columns = BLOCK if s == 0 else BLOCK * len(theirs)
+            for c0 in range(0, BLOCK * len(theirs), max(columns, 1)):
+                nc.gpsimd.tensor_tensor(
+                    runs_out(h_tile(s)[:, c0 : c0 + columns, :], RUN),
+                    a_tiles[j0 // HALF, g][0][:, (j0 % HALF + c0) // RUN : (j0 % HALF + c0 + columns) // RUN, :, :],
+                    b_gained[s][:].rearrange("p b c t e -> p (b c) t e")[:, c0 // RUN : (c0 + columns) // RUN, :, :],
+                    ALU.mult,
+                )
             for j in blocks:
                 if not on_gpsimd(j, g):
                     join(h_tile(s)[:, j - j0 : j - j0 + BLOCK, :], a_gained[j, g], b_banks[j, g], ALU.mult)
@@ -450,20 +452,24 @@ def tile_list_photo_redshift_features_kernel(
                 quantize_h(s)
                 colour_product(wide_steps)
                 colour_product(wide_steps + 1)
-                residual_in_psum(WIDE_END, R_PASSES - 1, d_tiles[wide_steps][:, BLOCK:WIDE, :])
+                residual_in_psum(WIDE_END, R_PASSES - 1, d_last[:, WIDE : WIDE + BLOCK, :])
                 d_term(s)
                 h_term(s)
             if s == 5:
                 colour_product(wide_steps + 2)
                 colour_product(wide_steps + 3)
-                both_passes("dq_last", d_last[:], S - BLOCK, w4q, False, tag=last_gained(s))
+                summed = quantize("dq_last", d_last[:], 3 * BLOCK, tag=last_gained(s))
                 quantize_h(s)
                 d_term(s)
                 h_term(s)
+                y_passes(WIDE_END, BLOCK, w4q[1], columns_of(summed, WIDE, BLOCK), False)
+                for g in range(R_PASSES):
+                    y_passes(S - BLOCK, BLOCK, w4q[g], columns_of(summed, g * BLOCK, BLOCK), False)
 
         for s in range(wide_steps, len(steps) - 1):
             meet(s)
-        both_passes("dq_end", d_tiles[wide_steps][:], WIDE_END, w4q, False, tag=last_gained(wide_steps))
+        d_end = quantize("dq_end", d_tiles[wide_steps][:], BLOCK, tag=last_gained(wide_steps))
+        y_passes(WIDE_END, BLOCK, w4q[0], columns_of(d_end, 0, BLOCK), False)
         both_passes("hq_end", h_tiles[wide_steps][:], WIDE_END, w3q, True)
         meet(len(steps) - 1)
         for s in range(len(steps) - R_PASSES, len(steps)):

@@ -32,6 +32,7 @@ EARLY_SLICES = 2
 SUM_BANKS = 4
 BLOCK_BANKS = 4
 RUN = 4
+SECOND_BLOCK = 64
 W2_ON_GPSIMD = 48
 REGION = 4096
 HEAD_AT = 4 * REGION
@@ -122,10 +123,10 @@ def tile_list_photo_redshift_features_kernel(
         v_w.append(placed("v_w1", [P, HALF], U32, HEAD_AT))
         nc.vector.tensor_copy(v_w[1][:], tab_w[:].bitcast(U32).indirect(entries(idx1, HALF, HALF)))
 
-        def on_gpsimd(j, g):
-            if j < HALF:
-                return (j, g) != (HALF - BLOCK, R_PASSES - 1)
-            return j % WIDE == 0 and j < SUMMED_FROM[g]
+        def gpsimd_columns(j, g):
+            if j < HALF and (j, g) != (HALF - BLOCK, R_PASSES - 1):
+                return BLOCK if j % WIDE == 0 else SECOND_BLOCK
+            return BLOCK if j % WIDE == 0 and j < SUMMED_FROM[g] else 0
 
         def sum_bank(shape):
             return psum.tile(shape, F32, name="sum_bank", tag="sum_bank", bufs=SUM_BANKS)
@@ -147,29 +148,33 @@ def tile_list_photo_redshift_features_kernel(
 
         def template_product(half, g, slices=range(PACK)):
             needed = min(HALF, SUMMED_FROM[g] - half * HALF)
-            blocks = [j for j in range(half * HALF, (half + 1) * HALF, BLOCK) if not on_gpsimd(j, g)]
             if (half, g) not in a_tiles:
                 plain = kept("a_plain%d%d" % (half, g), [P, needed // RUN, PACK, RUN], F32)
-                gained = None
-                if blocks:
-                    gained = kept("a_gained%d%d" % (half, g), [P, len(blocks), BLOCK // RUN, PACK, RUN], F32)
-                a_tiles[half, g] = plain, gained
                 for j in range(half * HALF, half * HALF + needed, BLOCK):
                     a_plain[j, g] = plain[:, j % HALF // RUN : (j % HALF + BLOCK) // RUN, :, :]
-                for n, j in enumerate(blocks):
-                    a_gained[j, g] = gained[:, n, :, :, :]
+                alike = {}
+                for j in range(half * HALF, (half + 1) * HALF, BLOCK):
+                    if gpsimd_columns(j, g) < BLOCK:
+                        alike.setdefault(gpsimd_columns(j, g), []).append(j)
+                gained = []
+                for c0, blocks in alike.items():
+                    tile = kept("a_gained%d%d_%d" % (half, g, c0), [P, len(blocks), (BLOCK - c0) // RUN, PACK, RUN], F32)
+                    gained.append((tile, c0, blocks))
+                    for n, j in enumerate(blocks):
+                        a_gained[j, g] = tile[:, n, :, :, :]
+                a_tiles[half, g] = plain, gained
             plain, gained = a_tiles[half, g]
             for t in slices:
                 bank = sum_bank([P, HALF])
                 template_pass(bank[:], half * HALF, HALF, g, t, True)
                 nc.scalar.copy(plain[:, :, t, :], bank[:, 0:needed].rearrange("p (c e) -> p c e", e=RUN))
-                if blocks:
+                for tile, c0, blocks in gained:
                     first = blocks[0] % HALF // BLOCK
                     stride = (blocks[1] - blocks[0]) // BLOCK if len(blocks) > 1 else 1
                     nc.scalar.activation(
-                        gained[:, :, :, t, :],
+                        tile[:, :, :, t, :],
                         bank[:].rearrange("p (b c e) -> p b c e", c=BLOCK // RUN, e=RUN)[
-                            :, first : HALF // BLOCK : stride, :, :
+                            :, first : first + stride * (len(blocks) - 1) + 1 : stride, c0 // RUN : BLOCK // RUN, :
                         ],
                         ACT.Copy,
                         scale=minus_gains[:, g, t : t + 1],
@@ -307,49 +312,59 @@ def tile_list_photo_redshift_features_kernel(
 
         b_banks, b_gained = {}, {}
 
+        def gpsimd_share(s):
+            j0, width, g = steps[s]
+            return sum(gpsimd_columns(j, g) for j in range(j0, j0 + width, BLOCK))
+
         def colour_product(s):
             j0, width, g = steps[s]
-            theirs = [j for j in range(j0, j0 + width, BLOCK) if on_gpsimd(j, g)]
-            if theirs:
-                b_gained[s] = kept("b_gained%d" % s, [P, len(theirs), BLOCK // RUN, PACK, RUN], F32)
+            if gpsimd_share(s):
+                b_gained[s] = kept("b_gained%d" % s, [P, gpsimd_share(s) // RUN, PACK, RUN], F32)
             for j in range(j0, j0 + width, BLOCK):
                 bank = psum.tile([P, PACK, BLOCK], F32, name="block_bank", tag="block_bank", bufs=BLOCK_BANKS)
                 b_banks[j, g] = bank
                 for t in range(PACK):
                     colour_pass(bank, j, g, t, True)
-                if on_gpsimd(j, g):
-                    for t in range(PACK):
-                        nc.scalar.activation(
-                            b_gained[s][:, (j - j0) // BLOCK, :, t, :],
-                            bank[:, t, :].rearrange("p (c e) -> p c e", e=RUN),
-                            ACT.Copy,
-                            scale=minus_gains[:, g, t : t + 1],
-                        )
+                columns = gpsimd_columns(j, g)
+                for t in range(PACK if columns else 0):
+                    nc.scalar.activation(
+                        b_gained[s][:, (j - j0) // RUN : (j - j0 + columns) // RUN, t, :],
+                        bank[:, t, 0:columns].rearrange("p (c e) -> p c e", e=RUN),
+                        ACT.Copy,
+                        scale=minus_gains[:, g, t : t + 1],
+                    )
 
         def last_gained(s):
             return "b_gained%d" % s
 
-        def join(grouped, a, bank, op):
-            nc.vector.tensor_tensor(runs_out(grouped, RUN), a, runs_in(bank[:], RUN), op)
+        def join(grouped, a, minus_b, op):
+            nc.vector.tensor_tensor(runs_out(grouped, RUN), a, runs_in(minus_b, RUN), op)
 
         def meet(s):
             j0, width, g = steps[s]
             blocks = list(range(j0, j0 + width, BLOCK))
-            theirs = [j - j0 for j in blocks if on_gpsimd(j, g)]
-            columns = BLOCK if s == 0 else BLOCK * len(theirs)
-            for c0 in range(0, BLOCK * len(theirs), max(columns, 1)):
+            share = gpsimd_share(s)
+            cuts = [0, BLOCK, share] if s == 0 else [0, share]
+            for c0, c1 in zip(cuts, cuts[1:]) if share else ():
+                a0 = j0 % HALF
                 nc.gpsimd.tensor_tensor(
-                    runs_out(h_tile(s)[:, c0 : c0 + columns, :], RUN),
-                    a_tiles[j0 // HALF, g][0][:, (j0 % HALF + c0) // RUN : (j0 % HALF + c0 + columns) // RUN, :, :],
-                    b_gained[s][:].rearrange("p b c t e -> p (b c) t e")[:, c0 // RUN : (c0 + columns) // RUN, :, :],
+                    runs_out(h_tile(s)[:, c0:c1, :], RUN),
+                    a_tiles[j0 // HALF, g][0][:, (a0 + c0) // RUN : (a0 + c1) // RUN, :, :],
+                    b_gained[s][:, c0 // RUN : c1 // RUN, :, :],
                     ALU.mult,
                 )
             for j in blocks:
-                if not on_gpsimd(j, g):
-                    join(h_tile(s)[:, j - j0 : j - j0 + BLOCK, :], a_gained[j, g], b_banks[j, g], ALU.mult)
+                c0 = gpsimd_columns(j, g)
+                if c0 < BLOCK:
+                    join(
+                        h_tile(s)[:, j - j0 + c0 : j - j0 + BLOCK, :],
+                        a_gained[j, g],
+                        b_banks[j, g][:, :, c0:BLOCK],
+                        ALU.mult,
+                    )
             for j in blocks:
                 if j < SUMMED_FROM[g]:
-                    join(d_tiles[s][:, j - j0 : j - j0 + BLOCK, :], a_plain[j, g], b_banks[j, g], ALU.add)
+                    join(d_tiles[s][:, j - j0 : j - j0 + BLOCK, :], a_plain[j, g], b_banks[j, g][:], ALU.add)
 
         y_banks = {}
 

@@ -28,14 +28,14 @@ BLOCK = BANK // PACK
 WIDE = 2 * BLOCK
 WIDE_END = S - 2 * BLOCK
 SUMMED_FROM = (S - BLOCK, S - 2 * BLOCK)
-EARLY_SLICES = 2
+EARLY_SLICES = 4
 SUM_BANKS = 4
 BLOCK_BANKS = 4
 RUN = 4
 SECOND_BLOCK = 64
-W2_ON_GPSIMD = 48
+W2_ON_GPSIMD = (96, 48)
 REGION = 4096
-HEAD_AT = 4 * REGION
+HEAD_AT = 5 * REGION
 ALIGN = 64
 
 
@@ -71,10 +71,8 @@ def tile_list_photo_redshift_features_kernel(
         gains = kept("gains", [P, R_PASSES, PACK], F32)
         planes = [kept("plane%d" % i, [P, T], F32) for i in range(PACK)]
         x_rows = xT.rearrange("(p i) t -> i p t", i=PACK)
-        early = PACK * W2_ON_GPSIMD
-        w2_early = kept("w2_early", [P, PACK, early], F32)
-        w2_raw = [placed("w2_raw0", [P, PACK, PASS - early], F32, 0), kept("w2_raw1", [P, PACK, PASS], F32)]
-        w3_raw = [kept("w3_raw%d" % g, [P, PACK, N], F32, tag=("w3_raw0", "tab_w")[g]) for g in range(R_PASSES)]
+        w2_raw = [kept("w2_raw%d" % g, [P, PACK, PASS], F32) for g in range(R_PASSES)]
+        w3_raw = [kept("w3_raw%d" % g, [P, PACK, N], F32, tag=("w2_raw0", "tab_w")[g]) for g in range(R_PASSES)]
 
         def entries(idx, j0, width):
             return idx[:, j0 // LIST_ROWS : (j0 + width) // LIST_ROWS]
@@ -95,15 +93,14 @@ def tile_list_photo_redshift_features_kernel(
         nc.sync.dma_start(out=planes[0][:], in_=x_rows[0])
         nc.sync.dma_start(idx2[:], offs2)
         nc.sync.dma_start(idx3[:], offs3)
-        load_w2(w2_early, 0, early)
-        for i in range(1, PACK):
-            nc.sync.dma_start(out=planes[i][:], in_=x_rows[i])
-        load_w2(w2_raw[0], early, PASS)
-        load_w2(w2_raw[1], PASS, H)
+        for g in range(R_PASSES):
+            load_w2(w2_raw[g], g * PASS, (g + 1) * PASS)
+            nc.sync.dma_start(out=planes[1 + g][:], in_=x_rows[1 + g])
+        nc.sync.dma_start(out=planes[PACK - 1][:], in_=x_rows[PACK - 1])
 
-        minus_gains = kept("minus_gains", [P, R_PASSES, PACK], F32)
         warm = kept("warm", [P, 1], F32)
         nc.scalar.activation(warm[:], gains[:, 0, 0:1], ACT.Gelu_apprx_tanh)
+        minus_gains = kept("minus_gains", [P, R_PASSES, PACK], F32)
         nc.scalar.activation(minus_gains[:], gains[:], ACT.Copy, scale=-1.0)
 
         w1_wo = kept("w1_wo", [P, 2 * H], U8)
@@ -124,8 +121,8 @@ def tile_list_photo_redshift_features_kernel(
         nc.vector.tensor_copy(v_w[1][:], tab_w[:].bitcast(U32).indirect(entries(idx1, HALF, HALF)))
 
         def gpsimd_columns(j, g):
-            if j < HALF and (j, g) != (HALF - BLOCK, R_PASSES - 1):
-                return BLOCK if j % WIDE == 0 else SECOND_BLOCK
+            if (j, g) == (BLOCK, 0):
+                return SECOND_BLOCK
             return BLOCK if j % WIDE == 0 and j < SUMMED_FROM[g] else 0
 
         def sum_bank(shape):
@@ -198,29 +195,32 @@ def tile_list_photo_redshift_features_kernel(
             nc.scalar.copy(runs_out(grouped, 2), runs_in(rows, 2))
 
         quarters = S // QUARTER
-        colours = [kept("colours%d" % q, [P, PACK, QUARTER], F32, tag="colours%d" % (q % 2)) for q in range(quarters)]
+        colours = [kept("colours%d" % half, [P, PACK, HALF], F32) for half in range(2)]
 
         def pick(i, j0, width, picked):
             nc.vector.tensor_copy(picked[:], planes[i][:].indirect(entries(idx2, j0, width)))
             return picked
 
-        def subtract(i, q, picked):
+        def subtract(i, j0, width, picked):
             nc.vector.tensor_tensor(
-                colours[q][:, i, :], planes[i][:].indirect(entries(idx3, q * QUARTER, QUARTER)), picked, ALU.subtract
+                colours[j0 // HALF][:, i, j0 % HALF : j0 % HALF + width],
+                planes[i][:].indirect(entries(idx3, j0, width)),
+                picked,
+                ALU.subtract,
             )
 
-        def subtract_late(i, picked):
-            for n in range(2):
-                subtract(i, 2 + n, picked[:, n * QUARTER : (n + 1) * QUARTER])
+        w2_grouped = [kept("w2_grouped%d" % g, [P, PASS, PACK], BF16, tag="pick%d" % g) for g in range(R_PASSES)]
+        w3_grouped = [placed("w3_grouped%d" % g, [P, N, PACK], BF16, REGION * (1 + 2 * g)) for g in range(R_PASSES)]
 
-        w2_grouped = [placed("w2_grouped%d" % g, [P, PASS, PACK], BF16, REGION * (3 - 2 * g)) for g in range(R_PASSES)]
-        w3_grouped = [placed("w3_grouped%d" % g, [P, N, PACK], BF16, REGION * (2 + g)) for g in range(R_PASSES)]
-
-        def round_w2(g, m0=0):
-            nc.scalar.copy(
-                w2_grouped[g][:].rearrange("p (t m) i -> p m t i", t=PACK)[:, m0:P],
-                w2_raw[g][:].rearrange("p i (m t) -> p m t i", t=PACK),
+        def w2_walks(g, m0, m1):
+            return (
+                w2_grouped[g][:].rearrange("p (t m) i -> p m t i", t=PACK)[:, m0:m1],
+                w2_raw[g][:].rearrange("p i (m t) -> p m t i", t=PACK)[:, m0:m1],
             )
+
+        def round_w2(g):
+            round_on_gpsimd(*w2_walks(g, 0, W2_ON_GPSIMD[g]))
+            nc.scalar.copy(*w2_walks(g, W2_ON_GPSIMD[g], P))
 
         def round_on_gpsimd(grouped, rows):
             nc.gpsimd.tensor_scalar(grouped, rows, 1.0, 0.0, ALU.mult, ALU.add)
@@ -229,52 +229,49 @@ def tile_list_photo_redshift_features_kernel(
             cols = slice(part * N // 2, (part + 1) * N // 2)
             interleave(w3_grouped[g][:, cols, :], w3_raw[g][:, :, cols])
 
-        x_grouped = [kept("x_grouped%d" % q, [P, QUARTER, PACK], BF16) for q in range(quarters)]
-        x_grouped[1] = placed("x_grouped1", [P, QUARTER, PACK], BF16, REGION // 4)
+        x_grouped = [kept("x_grouped0", [P, QUARTER, PACK], BF16)] + [
+            placed("x_grouped%d" % q, [P, QUARTER, PACK], BF16, at)
+            for q, at in ((1, REGION // 4), (2, 2 * REGION), (3, 4 * REGION))
+        ]
 
         def round_x(q):
-            interleave(x_grouped[q][:], colours[q][:])
+            interleave(x_grouped[q][:], colours[q // 2][:, :, q % 2 * QUARTER : (q % 2 + 1) * QUARTER])
 
         def quantize_x(q, tag=None):
             return quantize("xq%d" % q, x_grouped[q][:], QUARTER, tag=tag)
 
-        w2q = []
-        for i in range(PACK):
-            picks = [kept("pick%d%d" % (i, q), [P, QUARTER], F32, tag="pick%d%d" % (i % 2, q)) for q in range(2)]
-            if i == 0:
-                picks[0] = placed("first_pick", [P, QUARTER], F32, 3 * REGION)
-            for q in range(2):
-                pick(i, q * QUARTER, QUARTER, picks[q])
-            for q in range(2):
-                subtract(i, q, picks[q][:])
-            if i == 0:
-                round_on_gpsimd(
-                    w2_grouped[0][:].rearrange("p (t m) i -> p m t i", t=PACK)[:, 0:W2_ON_GPSIMD],
-                    w2_early[:].rearrange("p i (m t) -> p m t i", t=PACK),
-                )
-                template_product(0, 0)
-                template_product(0, 1)
-                template_product(1, 0)
-                template_product(1, 1, range(0, EARLY_SLICES))
+        def gather(i, j0, width, tags):
+            picks = [pick(i, j0 + n * width, width, kept("pick%d_%d" % (i, n), [P, width], F32, tag=tags[n])) for n in range(2)]
+            for n in range(2):
+                subtract(i, j0 + n * width, width, picks[n][:])
+
+        gather(0, 0, HALF, ("pick0", "pick2"))
+        template_product(0, 0)
+        round_w2(0)
+        gather(1, 0, HALF, ("pick1", "pick3"))
+        template_product(0, 1)
+        template_product(1, 0)
+        round_w2(1)
+        gather(2, 0, QUARTER, ("pick2", "pick4"))
+        template_product(1, 1, range(0, EARLY_SLICES))
         for g in range(R_PASSES):
             nc.sync.dma_start(
                 out=w3_raw[g][:], in_=w3[g * PASS : (g + 1) * PASS, :].rearrange("(p i) n -> p i n", i=PACK)
             )
         nc.sync.dma_start(out=w4_w[:], in_=w4_words.rearrange("a p c i -> p a (c i)").bitcast(I32))
         load_scale_rows(w4_s, w4_scales.rearrange("a q c -> q a c"))
-        picked = pick(0, HALF, HALF, kept("late_pick0", [P, HALF], F32, tag="pick10"))
-        round_on_gpsimd(x_grouped[0][:], colours[0][:].rearrange("p t c -> p c t"))
-        round_w2(0, W2_ON_GPSIMD)
+        gather(3, 0, QUARTER, ("pick3", "pick5"))
+        w2q = [quantize("w2q0", w2_grouped[0][:], PASS, tag="pick3")]
+        w2q.append(quantize("w2q1", w2_grouped[1][:], PASS, tag="pick5"))
+        round_x(0)
         round_x(1)
         xq = [quantize_x(0)]
-        w2q.append(quantize("w2q0", w2_grouped[0][:], PASS, tag=None))
-        subtract(0, 2, picked[:, 0:QUARTER])
+        picked = pick(2, HALF, HALF, kept("late_pick", [P, HALF], F32, tag="pick0"))
         xq.append(quantize_x(1))
-        subtract(0, 3, picked[:, QUARTER:HALF])
+        subtract(2, HALF, HALF, picked[:])
         w3q = []
 
-        steps = [(j0, WIDE, g) for g in range(R_PASSES) for j0 in (0, WIDE)]
-        steps += [(HALF, WIDE, g) for g in range(R_PASSES)]
+        steps = [(j0, WIDE, g) for j0 in range(0, WIDE_END, WIDE) for g in range(R_PASSES)]
         wide_steps = len(steps)
         steps += [(j0, BLOCK, g) for j0 in range(WIDE_END, S, BLOCK) for g in range(R_PASSES)]
 
@@ -297,7 +294,7 @@ def tile_list_photo_redshift_features_kernel(
                 colour_pass(bank, j, g, t, False)
             interleave(grouped, bank[:])
 
-        h_tiles = [placed("h%d" % s, [P, WIDE, PACK], BF16, REGION * min(s, 3)) for s in range(wide_steps + 1)]
+        h_tiles = [placed("h%d" % s, [P, WIDE, PACK], BF16, REGION * min(s, 4)) for s in range(wide_steps + 1)]
         h_last = [kept("h_last%d" % g, [P, BLOCK, PACK], BF16) for g in range(R_PASSES)]
         d_tiles = [kept("d%d" % s, [P, WIDE, PACK], BF16, tag="d%d" % (s % 2)) for s in range(wide_steps)]
         d_tiles.append(kept("d_end", [P, BLOCK, PACK], BF16))
@@ -420,45 +417,41 @@ def tile_list_photo_redshift_features_kernel(
                 y_passes(j0, BLOCK, weights[g], columns_of(both, g * BLOCK, BLOCK), closes and g == R_PASSES - 1)
 
         colour_product(0)
-        round_w2(1)
         colour_product(1)
         for s in range(wide_steps):
-            if s + 1 < PACK:
-                picked = pick(s + 1, HALF, HALF, placed("late_pick%d" % (s + 1), [P, HALF], F32, REGION * s + REGION // 2))
-            meet(s)
-            if s + 1 < PACK:
-                subtract_late(s + 1, picked)
             if s == 0:
-                quantize_h(s)
-                w2q.append(quantize("w2q1", w2_grouped[1][:], PASS, tag=last_gained(s)))
                 round_w3(0, 0)
                 round_w3(0, 1)
-                colour_product(2)
-                d_term(s)
-            if s == 1:
+                picked = pick(3, HALF, HALF, placed("last_pick", [P, HALF], F32, REGION // 2))
+            meet(s)
+            if s == 0:
+                for n in range(2):
+                    subtract(3, HALF + n * QUARTER, QUARTER, picked[:, n * QUARTER : (n + 1) * QUARTER])
                 quantize_h(s)
                 w3q.append(quantize("w3q0", w3_grouped[0][:], N, tag=last_gained(s)))
+                colour_product(2)
+                round_x(2)
+                d_term(s)
+                h_term(s)
+            if s == 1:
+                quantize_h(s)
+                xq.append(quantize_x(2, tag=last_gained(s)))
+                colour_product(3)
                 round_w3(1, 0)
                 round_w3(1, 1)
-                colour_product(3)
-                dq1 = quantize("dq1", d_tiles[s][:], WIDE)
-                h_term(0)
-            if s == 2:
-                round_x(2)
-                round_x(3)
-                quantize_h(s)
                 d_term(s)
+            if s == 2:
+                quantize_h(s)
                 w3q.append(quantize("w3q1", w3_grouped[1][:], N, tag=last_gained(s)))
-                xq.append(quantize_x(2))
                 colour_product(4)
-                h_term(s)
-                template_product(1, 1, range(EARLY_SLICES, PACK))
-                y_passes(WIDE, WIDE, w4q[0], columns_of(dq1, 0, WIDE), False)
+                round_x(3)
                 h_term(1)
+                d_term(s)
+                h_term(s)
             if s == 3:
+                quantize_h(s)
                 xq.append(quantize_x(3, tag=last_gained(s)))
                 colour_product(5)
-                quantize_h(s)
                 for g in range(R_PASSES):
                     residual_in_psum(S - BLOCK, g, d_last[:, g * BLOCK : (g + 1) * BLOCK, :])
                 d_term(s)

@@ -113,11 +113,11 @@ def tile_list_photo_redshift_features_kernel(
         nc.vector.tensor_copy(v_s[:], tab_s[:].indirect(idx1[:]))
         v_w = [kept("v_w0", [P, HALF], U32)]
         nc.vector.tensor_copy(v_w[0][:], tab_w[:].bitcast(U32).indirect(entries(idx1, 0, HALF)))
-        nc.vector.tensor_copy(
+        nc.gpsimd.tensor_copy(
             w1_so[:].rearrange("p (g t m) -> p g t m", g=R_PASSES, t=PACK),
             w1_s[:].rearrange("p (g m t) -> p g t m", g=R_PASSES, t=PACK),
         )
-        v_w.append(placed("v_w1", [P, HALF], U32, HEAD_AT))
+        v_w.append(kept("v_w1", [P, HALF], U32))
         nc.vector.tensor_copy(v_w[1][:], tab_w[:].bitcast(U32).indirect(entries(idx1, HALF, HALF)))
 
         def gpsimd_columns(j, g):
@@ -294,18 +294,17 @@ def tile_list_photo_redshift_features_kernel(
                 colour_pass(bank, j, g, t, False)
             interleave(grouped, bank[:])
 
-        h_tiles = [placed("h%d" % s, [P, WIDE, PACK], BF16, REGION * min(s, 4)) for s in range(wide_steps + 1)]
-        h_last = [kept("h_last%d" % g, [P, BLOCK, PACK], BF16) for g in range(R_PASSES)]
+        h_tiles = [placed("h%d" % s, [P, steps[s][1], PACK], BF16, REGION * min(s, 4)) for s in range(wide_steps + 1)]
+        h_tiles.append(kept("h_last", [P, BLOCK, PACK], BF16))
+        h_both = kept("h_both", [P, WIDE, PACK], BF16)
         d_tiles = [kept("d%d" % s, [P, WIDE, PACK], BF16, tag="d%d" % (s % 2)) for s in range(wide_steps)]
         d_tiles.append(kept("d_end", [P, BLOCK, PACK], BF16))
         d_last = kept("d_last", [P, 3 * BLOCK, PACK], BF16)
 
         def h_tile(s):
-            if s < wide_steps:
+            if s < len(h_tiles):
                 return h_tiles[s][:]
-            if s < wide_steps + R_PASSES:
-                return h_tiles[wide_steps][:, (s - wide_steps) * BLOCK : (s - wide_steps + 1) * BLOCK, :]
-            return h_last[s - wide_steps - R_PASSES][:]
+            return h_both[:, steps[s][2] * BLOCK : (steps[s][2] + 1) * BLOCK, :]
 
         b_banks, b_gained = {}, {}
 
@@ -366,7 +365,7 @@ def tile_list_photo_redshift_features_kernel(
         y_banks = {}
 
         def y_passes(j0, width, weights, operand, closes):
-            tiles_a_bank = BANK // width
+            tiles_a_bank = 2 if j0 == WIDE_END else BANK // width
             for n0 in range(0, N // P, tiles_a_bank):
                 opens = (j0, n0) not in y_banks
                 if opens:
@@ -384,12 +383,13 @@ def tile_list_photo_redshift_features_kernel(
                         stop=(closes and n == tiles_a_bank - 1),
                     )
                 if closes:
-                    tiles = tiles_a_bank // 2 if j0 + width == S else tiles_a_bank
+                    tiles = tiles_a_bank
                     for n in range(0, tiles_a_bank, tiles):
                         result = ring.tile([P, tiles, width], F32, name="result", tag="result", bufs=5)
                         nc.scalar.activation(result[:], bank[:, n : n + tiles, :], ACT.Gelu_apprx_tanh)
                         rows = slice((n0 + n) * P, (n0 + n + tiles) * P)
-                        nc.sync.dma_start(
+                        queue = nc.scalar if j0 == WIDE_END and n0 > 0 else nc.sync
+                        queue.dma_start(
                             out=out[rows, j0 : j0 + width].rearrange("(n p) j -> p n j", p=P), in_=result[:]
                         )
 
@@ -459,27 +459,27 @@ def tile_list_photo_redshift_features_kernel(
             if s == 4:
                 quantize_h(s)
                 colour_product(wide_steps)
-                colour_product(wide_steps + 1)
+                colour_product(wide_steps + 2)
                 residual_in_psum(WIDE_END, R_PASSES - 1, d_last[:, WIDE : WIDE + BLOCK, :])
                 d_term(s)
                 h_term(s)
             if s == 5:
-                colour_product(wide_steps + 2)
                 colour_product(wide_steps + 3)
+                colour_product(wide_steps + 1)
                 summed = quantize("dq_last", d_last[:], 3 * BLOCK, tag=last_gained(s))
                 quantize_h(s)
                 d_term(s)
                 h_term(s)
-                y_passes(WIDE_END, BLOCK, w4q[1], columns_of(summed, WIDE, BLOCK), False)
                 for g in range(R_PASSES):
                     y_passes(S - BLOCK, BLOCK, w4q[g], columns_of(summed, g * BLOCK, BLOCK), False)
+                y_passes(WIDE_END, BLOCK, w4q[1], columns_of(summed, WIDE, BLOCK), False)
 
-        for s in range(wide_steps, len(steps) - 1):
+        for s in (wide_steps + 2, wide_steps + 3, wide_steps):
             meet(s)
-        d_end = quantize("dq_end", d_tiles[wide_steps][:], BLOCK, tag=last_gained(wide_steps))
+        both_passes("hq_both", h_both[:], S - BLOCK, w3q, True, tag=last_gained(wide_steps))
+        d_end = quantize("dq_end", d_tiles[wide_steps][:], BLOCK)
         y_passes(WIDE_END, BLOCK, w4q[0], columns_of(d_end, 0, BLOCK), False)
-        both_passes("hq_end", h_tiles[wide_steps][:], WIDE_END, w3q, True)
-        meet(len(steps) - 1)
-        for s in range(len(steps) - R_PASSES, len(steps)):
+        meet(wide_steps + 1)
+        for s in range(wide_steps, wide_steps + R_PASSES):
             quantize_h(s)
             h_term(s)

@@ -25,17 +25,13 @@ R_PASSES = H // PASS
 HALF = S // 2
 QUARTER = S // 4
 BLOCK = BANK // PACK
-WIDE = 2 * BLOCK
-WIDE_END = S - 2 * BLOCK
-SUMMED_FROM = (S - BLOCK, S - 2 * BLOCK)
-EARLY_SLICES = 4
+TAIL = S - QUARTER
+GPSIMD_SHARE = (128, 64, 64)
 SUM_BANKS = 4
 BLOCK_BANKS = 4
 RUN = 4
-SECOND_BLOCK = 64
 W2_ON_GPSIMD = (96, 48)
-REGION = 4096
-HEAD_AT = 5 * REGION
+ROOM = 8192
 ALIGN = 64
 
 
@@ -52,33 +48,30 @@ def tile_list_photo_redshift_features_kernel(
         def kept(name, shape, dtype, tag=None):
             return keep.tile(shape, dtype, name=name, tag=tag or name, align_bytes=ALIGN)
 
+        def placed(name, shape, dtype, room, offset=0):
+            return laid.tile(shape, dtype, name=name, tag=name, align_bytes=ALIGN, offset=room * ROOM + offset)
+
         def load_scale_rows(tile, rows):
             for q in range(4):
                 nc.sync.dma_start(out=tile[32 * q : 32 * q + 4].bitcast(I32), in_=rows[4 * q : 4 * q + 4].bitcast(I32))
-
-        def placed(name, shape, dtype, offset):
-            return laid.tile(shape, dtype, name=name, tag=name, align_bytes=ALIGN, offset=offset)
 
         idx1 = kept("idx1", [P, S // LIST_ROWS], U16)
         idx2 = kept("idx2", [P, S // LIST_ROWS], U16)
         idx3 = kept("idx3", [P, S // LIST_ROWS], U16)
         tab_s = kept("tab_s", [P, T], U8)
-        tab_w = kept("tab_w", [P, T], I32)
-        w1_s = placed("w1_s", [P, H], U8, HEAD_AT)
+        tab_w = placed("tab_w", [P, T], I32, 5)
+        w1_s = kept("w1_s", [P, H], U8)
         w1_w = kept("w1_w", [P, 2 * H], U8)
         w4_s = kept("w4_s", [P, R_PASSES, N], U8)
         w4_w = kept("w4_w", [P, R_PASSES, N], I32)
         gains = kept("gains", [P, R_PASSES, PACK], F32)
-        planes = [kept("plane%d" % i, [P, T], F32) for i in range(PACK)]
+        planes = [placed("plane%d" % i, [P, T], F32, i) for i in range(PACK)]
         x_rows = xT.rearrange("(p i) t -> i p t", i=PACK)
-        w2_raw = [kept("w2_raw%d" % g, [P, PACK, PASS], F32) for g in range(R_PASSES)]
-        w3_raw = [kept("w3_raw%d" % g, [P, PACK, N], F32, tag=("w2_raw0", "tab_w")[g]) for g in range(R_PASSES)]
+        w2_raw = [placed("w2_raw%d" % g, [P, PACK, PASS], F32, (4, 6)[g]) for g in range(R_PASSES)]
+        w3_raw = [placed("w3_raw%d" % g, [P, PACK, N], F32, 4 + g) for g in range(R_PASSES)]
 
         def entries(idx, j0, width):
             return idx[:, j0 // LIST_ROWS : (j0 + width) // LIST_ROWS]
-
-        def load_w2(tile, r0, r1):
-            nc.sync.dma_start(out=tile[:], in_=w2[:, r0:r1].rearrange("(p i) r -> p i r", i=PACK))
 
         nc.gpsimd.memset(tab_s[:].bitcast(I32), 0)
         nc.vector.memset(w1_s[:].bitcast(I32), 0)
@@ -94,7 +87,9 @@ def tile_list_photo_redshift_features_kernel(
         nc.sync.dma_start(idx2[:], offs2)
         nc.sync.dma_start(idx3[:], offs3)
         for g in range(R_PASSES):
-            load_w2(w2_raw[g], g * PASS, (g + 1) * PASS)
+            nc.sync.dma_start(
+                out=w2_raw[g][:], in_=w2[:, g * PASS : (g + 1) * PASS].rearrange("(p i) r -> p i r", i=PACK)
+            )
             nc.sync.dma_start(out=planes[1 + g][:], in_=x_rows[1 + g])
         nc.sync.dma_start(out=planes[PACK - 1][:], in_=x_rows[PACK - 1])
 
@@ -120,11 +115,6 @@ def tile_list_photo_redshift_features_kernel(
         v_w.append(kept("v_w1", [P, HALF], U32))
         nc.vector.tensor_copy(v_w[1][:], tab_w[:].bitcast(U32).indirect(entries(idx1, HALF, HALF)))
 
-        def gpsimd_columns(j, g):
-            if (j, g) == (BLOCK, 0):
-                return SECOND_BLOCK
-            return BLOCK if j % WIDE == 0 and j < SUMMED_FROM[g] else 0
-
         def sum_bank(shape):
             return psum.tile(shape, F32, name="sum_bank", tag="sum_bank", bufs=SUM_BANKS)
 
@@ -141,44 +131,58 @@ def tile_list_photo_redshift_features_kernel(
                 stop=stop,
             )
 
-        a_tiles, a_plain, a_gained = {}, {}, {}
+        groups = QUARTER // RUN
+        a_first = kept("a_first", [P, 2, R_PASSES, groups, PACK, RUN], F32)
+        a_third = kept("a_third", [P, R_PASSES, groups, PACK, RUN], F32)
+        a_tail = kept("a_tail", [P, BLOCK // RUN, PACK, RUN], F32)
+        a_quarter = [a_first[:, 0], a_first[:, 1], a_third[:]]
 
-        def template_product(half, g, slices=range(PACK)):
-            needed = min(HALF, SUMMED_FROM[g] - half * HALF)
-            if (half, g) not in a_tiles:
-                plain = kept("a_plain%d%d" % (half, g), [P, needed // RUN, PACK, RUN], F32)
-                for j in range(half * HALF, half * HALF + needed, BLOCK):
-                    a_plain[j, g] = plain[:, j % HALF // RUN : (j % HALF + BLOCK) // RUN, :, :]
-                alike = {}
-                for j in range(half * HALF, (half + 1) * HALF, BLOCK):
-                    if gpsimd_columns(j, g) < BLOCK:
-                        alike.setdefault(gpsimd_columns(j, g), []).append(j)
-                gained = []
-                for c0, blocks in alike.items():
-                    tile = kept("a_gained%d%d_%d" % (half, g, c0), [P, len(blocks), (BLOCK - c0) // RUN, PACK, RUN], F32)
-                    gained.append((tile, c0, blocks))
-                    for n, j in enumerate(blocks):
-                        a_gained[j, g] = tile[:, n, :, :, :]
-                a_tiles[half, g] = plain, gained
-            plain, gained = a_tiles[half, g]
-            for t in slices:
+        def a_plain(j, width, g):
+            if j >= TAIL:
+                return a_tail[:]
+            q, c0 = divmod(j, QUARTER)
+            return a_quarter[q][:, g, c0 // RUN : (c0 + width) // RUN]
+
+        gained_ranges = {
+            (0, 0): [],
+            (0, 1): [(GPSIMD_SHARE[0], QUARTER), (QUARTER + GPSIMD_SHARE[1], HALF)],
+            (1, 0): [(S - BLOCK, S)],
+            (1, 1): [(HALF + GPSIMD_SHARE[2], S)],
+        }
+        gained_tiles = {
+            (g, j0): kept("a_gained%d_%d" % (g, j0), [P, (j1 - j0) // RUN, PACK, RUN], F32)
+            for (half, g), ranges in gained_ranges.items()
+            for j0, j1 in ranges
+        }
+
+        def a_gained(j, width, g):
+            j0 = max(first for first, end in gained_ranges[j // HALF, g] if first <= j)
+            return gained_tiles[g, j0][:, (j - j0) // RUN : (j - j0 + width) // RUN]
+
+        def in_runs(columns):
+            return columns.rearrange("p (c e) -> p c e", e=RUN)
+
+        def template_product(half, g):
+            for t in range(PACK):
                 bank = sum_bank([P, HALF])
                 template_pass(bank[:], half * HALF, HALF, g, t, True)
-                nc.scalar.copy(plain[:, :, t, :], bank[:, 0:needed].rearrange("p (c e) -> p c e", e=RUN))
-                for tile, c0, blocks in gained:
-                    first = blocks[0] % HALF // BLOCK
-                    stride = (blocks[1] - blocks[0]) // BLOCK if len(blocks) > 1 else 1
+                if half == 0:
+                    nc.scalar.copy(a_first[:, :, g, :, t, :], bank[:].rearrange("p (q c e) -> p q c e", q=2, e=RUN))
+                else:
+                    nc.scalar.copy(a_third[:, g, :, t, :], in_runs(bank[:, 0:QUARTER]))
+                    if g == 0:
+                        nc.scalar.copy(a_tail[:, :, t, :], in_runs(bank[:, QUARTER : QUARTER + BLOCK]))
+                for j0, j1 in gained_ranges[half, g]:
                     nc.scalar.activation(
-                        tile[:, :, :, t, :],
-                        bank[:].rearrange("p (b c e) -> p b c e", c=BLOCK // RUN, e=RUN)[
-                            :, first : first + stride * (len(blocks) - 1) + 1 : stride, c0 // RUN : BLOCK // RUN, :
-                        ],
+                        gained_tiles[g, j0][:, :, t, :],
+                        in_runs(bank[:, j0 - half * HALF : j1 - half * HALF]),
                         ACT.Copy,
                         scale=minus_gains[:, g, t : t + 1],
                     )
 
-        def quantize(name, grouped, width, tag=None):
-            codes = kept(name + "_w", [P, width], U32, tag=tag)
+        def quantize(name, grouped, width, codes=None):
+            if codes is None:
+                codes = kept(name + "_w", [P, width], U32)
             scales = kept(name + "_s", [P, width], U8)
             nc.vector.quantize_mx(
                 out=codes[:].bitcast(FP8X4), scales=scales[:], in_=grouped.rearrange("p c i -> p (c i)")
@@ -194,11 +198,10 @@ def tile_list_photo_redshift_features_kernel(
         def interleave(grouped, rows):
             nc.scalar.copy(runs_out(grouped, 2), runs_in(rows, 2))
 
-        quarters = S // QUARTER
         colours = [kept("colours%d" % half, [P, PACK, HALF], F32) for half in range(2)]
 
         def pick(i, j0, width, picked):
-            nc.vector.tensor_copy(picked[:], planes[i][:].indirect(entries(idx2, j0, width)))
+            nc.vector.tensor_copy(picked, planes[i][:].indirect(entries(idx2, j0, width)))
             return picked
 
         def subtract(i, j0, width, picked):
@@ -210,7 +213,7 @@ def tile_list_photo_redshift_features_kernel(
             )
 
         w2_grouped = [kept("w2_grouped%d" % g, [P, PASS, PACK], BF16, tag="pick%d" % g) for g in range(R_PASSES)]
-        w3_grouped = [placed("w3_grouped%d" % g, [P, N, PACK], BF16, REGION * (1 + 2 * g)) for g in range(R_PASSES)]
+        w3_grouped = [kept("w3_grouped0", [P, N, PACK], BF16), placed("w3_grouped1", [P, N, PACK], BF16, 8)]
 
         def w2_walks(g, m0, m1):
             return (
@@ -219,61 +222,56 @@ def tile_list_photo_redshift_features_kernel(
             )
 
         def round_w2(g):
-            round_on_gpsimd(*w2_walks(g, 0, W2_ON_GPSIMD[g]))
+            grouped, rows = w2_walks(g, 0, W2_ON_GPSIMD[g])
+            nc.gpsimd.tensor_scalar(grouped, rows, 1.0, 0.0, ALU.mult, ALU.add)
             nc.scalar.copy(*w2_walks(g, W2_ON_GPSIMD[g], P))
 
-        def round_on_gpsimd(grouped, rows):
-            nc.gpsimd.tensor_scalar(grouped, rows, 1.0, 0.0, ALU.mult, ALU.add)
+        def round_w3(g):
+            for part in range(2):
+                cols = slice(part * N // 2, (part + 1) * N // 2)
+                interleave(w3_grouped[g][:, cols, :], w3_raw[g][:, :, cols])
 
-        def round_w3(g, part):
-            cols = slice(part * N // 2, (part + 1) * N // 2)
-            interleave(w3_grouped[g][:, cols, :], w3_raw[g][:, :, cols])
-
-        x_grouped = [kept("x_grouped0", [P, QUARTER, PACK], BF16)] + [
-            placed("x_grouped%d" % q, [P, QUARTER, PACK], BF16, at)
-            for q, at in ((1, REGION // 4), (2, 2 * REGION), (3, 4 * REGION))
+        x_late = placed("x_late", [P, HALF, PACK], BF16, 4)
+        x_grouped = [
+            kept("x_grouped0", [P, QUARTER, PACK], BF16),
+            placed("x_grouped1", [P, QUARTER, PACK], BF16, 7),
+            x_late[:, 0:QUARTER, :],
+            x_late[:, QUARTER:HALF, :],
         ]
 
         def round_x(q):
             interleave(x_grouped[q][:], colours[q // 2][:, :, q % 2 * QUARTER : (q % 2 + 1) * QUARTER])
 
-        def quantize_x(q, tag=None):
-            return quantize("xq%d" % q, x_grouped[q][:], QUARTER, tag=tag)
-
-        def gather(i, j0, width, tags):
-            picks = [pick(i, j0 + n * width, width, kept("pick%d_%d" % (i, n), [P, width], F32, tag=tags[n])) for n in range(2)]
+        def gather(i, width, tags):
+            picks = [
+                pick(i, n * width, width, kept("pick%d_%d" % (i, n), [P, width], F32, tag=tags[n])[:]) for n in range(2)
+            ]
             for n in range(2):
-                subtract(i, j0 + n * width, width, picks[n][:])
+                subtract(i, n * width, width, picks[n])
 
-        gather(0, 0, HALF, ("pick0", "pick2"))
+        gather(0, HALF, ("pick0", "pick2"))
         template_product(0, 0)
         round_w2(0)
-        gather(1, 0, HALF, ("pick1", "pick3"))
+        gather(1, HALF, ("pick1", "pick3"))
         template_product(0, 1)
         template_product(1, 0)
         round_w2(1)
-        gather(2, 0, QUARTER, ("pick2", "pick4"))
-        template_product(1, 1, range(0, EARLY_SLICES))
+        gather(2, QUARTER, ("pick2", "pick4"))
+        template_product(1, 1)
         for g in range(R_PASSES):
             nc.sync.dma_start(
                 out=w3_raw[g][:], in_=w3[g * PASS : (g + 1) * PASS, :].rearrange("(p i) n -> p i n", i=PACK)
             )
         nc.sync.dma_start(out=w4_w[:], in_=w4_words.rearrange("a p c i -> p a (c i)").bitcast(I32))
         load_scale_rows(w4_s, w4_scales.rearrange("a q c -> q a c"))
-        gather(3, 0, QUARTER, ("pick3", "pick5"))
-        w2q = [quantize("w2q0", w2_grouped[0][:], PASS, tag="pick3")]
-        w2q.append(quantize("w2q1", w2_grouped[1][:], PASS, tag="pick5"))
+        gather(3, QUARTER, ("pick3", "pick5"))
+        w2q = [
+            quantize("w2q%d" % g, w2_grouped[g][:], PASS, kept("w2q%d_w" % g, [P, PASS], U32, tag=("pick3", "pick5")[g]))
+            for g in range(R_PASSES)
+        ]
         round_x(0)
         round_x(1)
-        xq = [quantize_x(0)]
-        picked = pick(2, HALF, HALF, kept("late_pick", [P, HALF], F32, tag="pick0"))
-        xq.append(quantize_x(1))
-        subtract(2, HALF, HALF, picked[:])
-        w3q = []
-
-        steps = [(j0, WIDE, g) for j0 in range(0, WIDE_END, WIDE) for g in range(R_PASSES)]
-        wide_steps = len(steps)
-        steps += [(j0, BLOCK, g) for j0 in range(WIDE_END, S, BLOCK) for g in range(R_PASSES)]
+        xq = [quantize("xq0", x_grouped[0][:], QUARTER)]
 
         def colour_pass(bank, j, g, t, start):
             quarter, c0 = divmod(j, QUARTER)
@@ -294,78 +292,79 @@ def tile_list_photo_redshift_features_kernel(
                 colour_pass(bank, j, g, t, False)
             interleave(grouped, bank[:])
 
-        h_tiles = [placed("h%d" % s, [P, steps[s][1], PACK], BF16, REGION * min(s, 4)) for s in range(wide_steps + 1)]
-        h_tiles.append(kept("h_last", [P, BLOCK, PACK], BF16))
-        h_both = kept("h_both", [P, WIDE, PACK], BF16)
-        d_tiles = [kept("d%d" % s, [P, WIDE, PACK], BF16, tag="d%d" % (s % 2)) for s in range(wide_steps)]
-        d_tiles.append(kept("d_end", [P, BLOCK, PACK], BF16))
-        d_last = kept("d_last", [P, 3 * BLOCK, PACK], BF16)
+        def gpsimd_columns(j, g):
+            if j >= TAIL:
+                return BLOCK if (j, g) == (TAIL, 0) else 0
+            if g == 0:
+                return BLOCK
+            return GPSIMD_SHARE[j // QUARTER] if j % QUARTER == 0 else 0
 
-        def h_tile(s):
-            if s < len(h_tiles):
-                return h_tiles[s][:]
-            return h_both[:, steps[s][2] * BLOCK : (steps[s][2] + 1) * BLOCK, :]
+        b_gained = [
+            placed("b_gained%d" % q, [P, (QUARTER + GPSIMD_SHARE[q]) // RUN, PACK, RUN], F32, (0, 1, 6)[q])
+            for q in range(3)
+        ]
+        b_gained.append(placed("b_gained3", [P, BLOCK // RUN, PACK, RUN], F32, 0, 3 * ROOM // 4))
+        b_banks = {}
 
-        b_banks, b_gained = {}, {}
-
-        def gpsimd_share(s):
-            j0, width, g = steps[s]
-            return sum(gpsimd_columns(j, g) for j in range(j0, j0 + width, BLOCK))
-
-        def colour_product(s):
-            j0, width, g = steps[s]
-            if gpsimd_share(s):
-                b_gained[s] = kept("b_gained%d" % s, [P, gpsimd_share(s) // RUN, PACK, RUN], F32)
-            for j in range(j0, j0 + width, BLOCK):
+        def colour_product(q, blocks):
+            for j, g in blocks:
                 bank = psum.tile([P, PACK, BLOCK], F32, name="block_bank", tag="block_bank", bufs=BLOCK_BANKS)
                 b_banks[j, g] = bank
                 for t in range(PACK):
                     colour_pass(bank, j, g, t, True)
                 columns = gpsimd_columns(j, g)
+                c0 = g * QUARTER + j % QUARTER
                 for t in range(PACK if columns else 0):
                     nc.scalar.activation(
-                        b_gained[s][:, (j - j0) // RUN : (j - j0 + columns) // RUN, t, :],
-                        bank[:, t, 0:columns].rearrange("p (c e) -> p c e", e=RUN),
+                        b_gained[q][:, c0 // RUN : (c0 + columns) // RUN, t, :],
+                        in_runs(bank[:, t, 0:columns]),
                         ACT.Copy,
                         scale=minus_gains[:, g, t : t + 1],
                     )
 
-        def last_gained(s):
-            return "b_gained%d" % s
+        def blocks_of(q):
+            return [(q * QUARTER + n * BLOCK, g) for g in range(R_PASSES) for n in range(2)]
 
         def join(grouped, a, minus_b, op):
             nc.vector.tensor_tensor(runs_out(grouped, RUN), a, runs_in(minus_b, RUN), op)
 
-        def meet(s):
-            j0, width, g = steps[s]
-            blocks = list(range(j0, j0 + width, BLOCK))
-            share = gpsimd_share(s)
-            cuts = [0, BLOCK, share] if s == 0 else [0, share]
-            for c0, c1 in zip(cuts, cuts[1:]) if share else ():
-                a0 = j0 % HALF
-                nc.gpsimd.tensor_tensor(
-                    runs_out(h_tile(s)[:, c0:c1, :], RUN),
-                    a_tiles[j0 // HALF, g][0][:, (a0 + c0) // RUN : (a0 + c1) // RUN, :, :],
-                    b_gained[s][:, c0 // RUN : c1 // RUN, :, :],
-                    ALU.mult,
+        def join_h(grouped, j, g):
+            c0 = gpsimd_columns(j, g)
+            join(grouped[:, c0:BLOCK, :], a_gained(j + c0, BLOCK - c0, g), b_banks[j, g][:, :, c0:BLOCK], ALU.mult)
+
+        def join_d(grouped, j, g):
+            join(grouped, a_plain(j, BLOCK, g), b_banks[j, g][:], ALU.add)
+
+        def product_on_gpsimd(grouped, a, minus_b):
+            nc.gpsimd.tensor_tensor(runs_out(grouped, RUN), a, minus_b, ALU.mult)
+
+        h_tiles = [placed("h0", [P, HALF, PACK], BF16, 2)]
+        d_tiles = [placed("d0", [P, HALF, PACK], BF16, 7)]
+        both_tiles = {}
+        for q in (1, 2):
+            both = placed("hd%d" % q, [P, 2, HALF, PACK], BF16, 4 * q)
+            both_tiles[q] = both
+            h_tiles.append(both[:, 0])
+            d_tiles.append(both[:, 1])
+
+        def meet(q):
+            share = QUARTER + GPSIMD_SHARE[q]
+            cuts = (0, QUARTER, share) if q == 0 else (0, share)
+            a = a_quarter[q].rearrange("p g c t e -> p (g c) t e")
+            for c0, c1 in zip(cuts, cuts[1:]):
+                product_on_gpsimd(
+                    h_tiles[q][:, c0:c1, :], a[:, c0 // RUN : c1 // RUN], b_gained[q][:, c0 // RUN : c1 // RUN]
                 )
-            for j in blocks:
-                c0 = gpsimd_columns(j, g)
-                if c0 < BLOCK:
-                    join(
-                        h_tile(s)[:, j - j0 + c0 : j - j0 + BLOCK, :],
-                        a_gained[j, g],
-                        b_banks[j, g][:, :, c0:BLOCK],
-                        ALU.mult,
-                    )
-            for j in blocks:
-                if j < SUMMED_FROM[g]:
-                    join(d_tiles[s][:, j - j0 : j - j0 + BLOCK, :], a_plain[j, g], b_banks[j, g][:], ALU.add)
+            for n, (j, g) in enumerate(blocks_of(q)):
+                cols = slice(n * BLOCK, (n + 1) * BLOCK)
+                if gpsimd_columns(j, g) < BLOCK:
+                    join_h(h_tiles[q][:, cols, :], j, g)
+                join_d(d_tiles[q][:, cols, :], j, g)
 
         y_banks = {}
 
         def y_passes(j0, width, weights, operand, closes):
-            tiles_a_bank = 2 if j0 == WIDE_END else BANK // width
+            tiles_a_bank = 2 if j0 == TAIL else BANK // width
             for n0 in range(0, N // P, tiles_a_bank):
                 opens = (j0, n0) not in y_banks
                 if opens:
@@ -383,103 +382,88 @@ def tile_list_photo_redshift_features_kernel(
                         stop=(closes and n == tiles_a_bank - 1),
                     )
                 if closes:
-                    tiles = tiles_a_bank
-                    for n in range(0, tiles_a_bank, tiles):
-                        result = ring.tile([P, tiles, width], F32, name="result", tag="result", bufs=5)
-                        nc.scalar.activation(result[:], bank[:, n : n + tiles, :], ACT.Gelu_apprx_tanh)
-                        rows = slice((n0 + n) * P, (n0 + n + tiles) * P)
-                        queue = nc.scalar if j0 == WIDE_END and n0 > 0 else nc.sync
-                        queue.dma_start(
-                            out=out[rows, j0 : j0 + width].rearrange("(n p) j -> p n j", p=P), in_=result[:]
-                        )
+                    result = ring.tile([P, tiles_a_bank, width], F32, name="result", tag="result", bufs=5)
+                    nc.scalar.activation(result[:], bank[:], ACT.Gelu_apprx_tanh)
+                    rows = slice(n0 * P, (n0 + tiles_a_bank) * P)
+                    queue = nc.scalar if j0 == TAIL and n0 > 0 else nc.sync
+                    queue.dma_start(out=out[rows, j0 : j0 + width].rearrange("(n p) j -> p n j", p=P), in_=result[:])
 
         def columns_of(quantized, c0, columns):
             return quantized[0][:, c0 : c0 + columns], quantized[1][:, c0 : c0 + columns]
 
         w4q = [(w4_w[:, g, :], w4_s[:, g, :]) for g in range(R_PASSES)]
+        w3q = []
 
-        hq = {}
+        def term(q, g, weights, quantized, closes=False):
+            y_passes(q * QUARTER, QUARTER, weights[g], columns_of(quantized, g * QUARTER, QUARTER), closes)
 
-        def quantize_h(s, tag=None):
-            hq[s] = quantize("hq%d" % s, h_tile(s), steps[s][1], tag=tag)
+        def behind(name, width, room, offset):
+            return placed(name, [P, width], U32, room, offset)
 
-        def h_term(s):
-            j0, width, g = steps[s]
-            y_passes(j0, width, w3q[g], columns_of(hq[s], 0, width), g == R_PASSES - 1)
+        colour_product(0, blocks_of(0))
+        late = [pick(2, HALF + n * QUARTER, QUARTER, colours[0][:, n, 0:QUARTER]) for n in range(2)]
+        xq.append(quantize("xq1", x_grouped[1][:], QUARTER))
+        for n in range(2):
+            subtract(2, HALF + n * QUARTER, QUARTER, late[n])
+        round_w3(0)
+        last = pick(3, HALF, HALF, colours[0][:, 2, :])
+        meet(0)
+        colour_product(1, blocks_of(1))
+        for n in range(2):
+            subtract(3, HALF + n * QUARTER, QUARTER, last[:, n * QUARTER : (n + 1) * QUARTER])
+        round_x(2)
+        round_x(3)
+        w3q.append(quantize("w3q0", w3_grouped[0][:], N, behind("w3q0_w", N, 0, 0)))
+        hq0 = quantize("hq0", h_tiles[0][:], HALF)
+        dq0 = quantize("dq0", d_tiles[0][:], HALF, behind("dq0_w", HALF, 0, 2048))
+        xq_late = quantize("xq_late", x_late[:], HALF, behind("xq_late_w", HALF, 0, 4096))
+        xq.extend(columns_of(xq_late, n * QUARTER, QUARTER) for n in range(2))
+        round_w3(1)
 
-        def d_term(s):
-            j0, width, g = steps[s]
-            y_passes(j0, width, w4q[g], columns_of(quantize("dq%d" % s, d_tiles[s][:], WIDE), 0, WIDE), False)
+        meet(1)
+        colour_product(2, blocks_of(2))
+        d_last = placed("d_last", [P, 3 * BLOCK, PACK], BF16, 3)
+        summed_blocks = [(S - BLOCK, 0), (S - BLOCK, 1), (TAIL, 1)]
+        for n, (j, g) in enumerate(summed_blocks):
+            if n == 2:
+                term(0, 0, w3q, hq0)
+                term(0, 0, w4q, dq0)
+                term(0, 1, w4q, dq0)
+            residual_in_psum(j, g, d_last[:, n * BLOCK : (n + 1) * BLOCK, :])
+        w3q.append(quantize("w3q1", w3_grouped[1][:], N, behind("w3q1_w", N, 1, 0)))
+        hdq1 = quantize("hdq1", both_tiles[1][:].rearrange("p s c i -> p (s c) i"), S)
+        hq1, dq1 = columns_of(hdq1, 0, HALF), columns_of(hdq1, HALF, HALF)
+        term(0, 1, w3q, hq0, True)
 
-        def both_passes(name, grouped, j0, weights, closes, tag=None):
-            both = quantize(name, grouped, WIDE, tag=tag)
-            for g in range(R_PASSES):
-                y_passes(j0, BLOCK, weights[g], columns_of(both, g * BLOCK, BLOCK), closes and g == R_PASSES - 1)
+        meet(2)
+        colour_product(3, [(TAIL, 0), (S - BLOCK, 0), (S - BLOCK, 1), (TAIL, 1)])
+        for g in range(R_PASSES):
+            term(1, g, w3q, hq1)
+        for g in range(R_PASSES):
+            term(1, g, w4q, dq1, g == R_PASSES - 1)
+        hq2 = quantize("hq2", h_tiles[2], HALF)
+        summed = quantize("dq_last", d_last[:], 3 * BLOCK, behind("dq_last_w", 3 * BLOCK, 6, 0))
+        dq2 = quantize("dq2", d_tiles[2], HALF, behind("dq2_w", HALF, 6, 2048))
+        for g in range(R_PASSES):
+            term(2, g, w3q, hq2)
+        for g in range(R_PASSES):
+            term(2, g, w4q, dq2, g == R_PASSES - 1)
+        for n, (j, g) in enumerate(summed_blocks):
+            y_passes(j, BLOCK, w4q[g], columns_of(summed, n * BLOCK, BLOCK), False)
 
-        colour_product(0)
-        colour_product(1)
-        for s in range(wide_steps):
-            if s == 0:
-                round_w3(0, 0)
-                round_w3(0, 1)
-                picked = pick(3, HALF, HALF, placed("last_pick", [P, HALF], F32, REGION // 2))
-            meet(s)
-            if s == 0:
-                for n in range(2):
-                    subtract(3, HALF + n * QUARTER, QUARTER, picked[:, n * QUARTER : (n + 1) * QUARTER])
-                quantize_h(s)
-                w3q.append(quantize("w3q0", w3_grouped[0][:], N, tag=last_gained(s)))
-                colour_product(2)
-                round_x(2)
-                d_term(s)
-                h_term(s)
-            if s == 1:
-                quantize_h(s)
-                xq.append(quantize_x(2, tag=last_gained(s)))
-                colour_product(3)
-                round_w3(1, 0)
-                round_w3(1, 1)
-                d_term(s)
-            if s == 2:
-                quantize_h(s)
-                w3q.append(quantize("w3q1", w3_grouped[1][:], N, tag=last_gained(s)))
-                colour_product(4)
-                round_x(3)
-                h_term(1)
-                d_term(s)
-                h_term(s)
-            if s == 3:
-                quantize_h(s)
-                xq.append(quantize_x(3, tag=last_gained(s)))
-                colour_product(5)
-                for g in range(R_PASSES):
-                    residual_in_psum(S - BLOCK, g, d_last[:, g * BLOCK : (g + 1) * BLOCK, :])
-                d_term(s)
-                h_term(s)
-            if s == 4:
-                quantize_h(s)
-                colour_product(wide_steps)
-                colour_product(wide_steps + 2)
-                residual_in_psum(WIDE_END, R_PASSES - 1, d_last[:, WIDE : WIDE + BLOCK, :])
-                d_term(s)
-                h_term(s)
-            if s == 5:
-                colour_product(wide_steps + 3)
-                colour_product(wide_steps + 1)
-                summed = quantize("dq_last", d_last[:], 3 * BLOCK, tag=last_gained(s))
-                quantize_h(s)
-                d_term(s)
-                h_term(s)
-                for g in range(R_PASSES):
-                    y_passes(S - BLOCK, BLOCK, w4q[g], columns_of(summed, g * BLOCK, BLOCK), False)
-                y_passes(WIDE_END, BLOCK, w4q[1], columns_of(summed, WIDE, BLOCK), False)
-
-        for s in (wide_steps + 2, wide_steps + 3, wide_steps):
-            meet(s)
-        both_passes("hq_both", h_both[:], S - BLOCK, w3q, True, tag=last_gained(wide_steps))
-        d_end = quantize("dq_end", d_tiles[wide_steps][:], BLOCK)
-        y_passes(WIDE_END, BLOCK, w4q[0], columns_of(d_end, 0, BLOCK), False)
-        meet(wide_steps + 1)
-        for s in range(wide_steps, wide_steps + R_PASSES):
-            quantize_h(s)
-            h_term(s)
+        tail = placed("tail", [P, 5, BLOCK, PACK], BF16, 3, 3 * BLOCK * PACK * 2 - ALIGN)
+        product_on_gpsimd(tail[:, 0], a_tail[:], b_gained[3][:])
+        for g in range(R_PASSES):
+            join_h(tail[:, 2 + g], S - BLOCK, g)
+        join_d(tail[:, 4], TAIL, 0)
+        h_both = quantize(
+            "hq_both", tail[:, 2:4].rearrange("p g c i -> p (g c) i"), QUARTER, behind("hq_both_w", QUARTER, 0, 3 * ROOM // 4)
+        )
+        for g in range(R_PASSES):
+            y_passes(S - BLOCK, BLOCK, w3q[g], columns_of(h_both, g * BLOCK, BLOCK), g == R_PASSES - 1)
+        d_end = quantize("dq_end", tail[:, 4], BLOCK)
+        y_passes(TAIL, BLOCK, w4q[0], columns_of(d_end, 0, BLOCK), False)
+        join_h(tail[:, 1], TAIL, 1)
+        for g in range(R_PASSES):
+            h_end = quantize("hq_end%d" % g, tail[:, g], BLOCK)
+            y_passes(TAIL, BLOCK, w3q[g], columns_of(h_end, 0, BLOCK), g == R_PASSES - 1)

@@ -143,6 +143,10 @@ def tile_list_photo_redshift_features_kernel(
             q, c0 = divmod(j, QUARTER)
             return a_quarter[q][:, g, c0 // RUN : (c0 + width) // RUN]
 
+        early_colours = kept("early_colours", [P, PACK, HALF], F32)
+        colours = [early_colours[:, :, 0:QUARTER], early_colours[:, :, QUARTER:HALF]]
+        colours += [kept("colours%d" % q, [P, PACK, QUARTER], F32)[:] for q in (2, 3)]
+
         gained_ranges = {
             (0, 0): [],
             (0, 1): [(GPSIMD_SHARE[0], QUARTER), (QUARTER + GPSIMD_SHARE[1], HALF)],
@@ -198,15 +202,13 @@ def tile_list_photo_redshift_features_kernel(
         def interleave(grouped, rows):
             nc.scalar.copy(runs_out(grouped, 2), runs_in(rows, 2))
 
-        colours = [kept("colours%d" % half, [P, PACK, HALF], F32) for half in range(2)]
-
         def pick(i, j0, width, picked):
             nc.vector.tensor_copy(picked, planes[i][:].indirect(entries(idx2, j0, width)))
             return picked
 
         def subtract(i, j0, width, picked):
             nc.vector.tensor_tensor(
-                colours[j0 // HALF][:, i, j0 % HALF : j0 % HALF + width],
+                early_colours[:, i, j0 : j0 + width] if j0 < HALF else colours[j0 // QUARTER][:, i, :],
                 planes[i][:].indirect(entries(idx3, j0, width)),
                 picked,
                 ALU.subtract,
@@ -233,21 +235,23 @@ def tile_list_photo_redshift_features_kernel(
 
         x_late = placed("x_late", [P, HALF, PACK], BF16, 4)
         x_grouped = [
-            kept("x_grouped0", [P, QUARTER, PACK], BF16),
+            placed("x_grouped0", [P, QUARTER, PACK], BF16, 9),
             placed("x_grouped1", [P, QUARTER, PACK], BF16, 7),
             x_late[:, 0:QUARTER, :],
             x_late[:, QUARTER:HALF, :],
         ]
 
         def round_x(q):
-            interleave(x_grouped[q][:], colours[q // 2][:, :, q % 2 * QUARTER : (q % 2 + 1) * QUARTER])
+            interleave(x_grouped[q][:], colours[q])
 
         def gather(i, width, tags):
+            starts = (HALF, 0) if width == HALF else (0, QUARTER)
             picks = [
-                pick(i, n * width, width, kept("pick%d_%d" % (i, n), [P, width], F32, tag=tags[n])[:]) for n in range(2)
+                pick(i, starts[n], width, kept("pick%d_%d" % (i, n), [P, width], F32, tag=tags[n])[:]) for n in range(2)
             ]
-            for n in range(2):
-                subtract(i, n * width, width, picks[n])
+            for c0 in range(0, width, QUARTER):
+                subtract(i, starts[0] + c0, QUARTER, picks[0][:, c0 : c0 + QUARTER])
+            subtract(i, starts[1], width, picks[1])
 
         gather(0, HALF, ("pick0", "pick2"))
         template_product(0, 0)
@@ -338,7 +342,7 @@ def tile_list_photo_redshift_features_kernel(
         def product_on_gpsimd(grouped, a, minus_b):
             nc.gpsimd.tensor_tensor(runs_out(grouped, RUN), a, minus_b, ALU.mult)
 
-        h_tiles = [placed("h0", [P, HALF, PACK], BF16, 2)]
+        h_tiles = [placed("h0", [P, HALF, PACK], BF16, 9)]
         d_tiles = [placed("d0", [P, HALF, PACK], BF16, 7)]
         both_tiles = {}
         for q in (1, 2):
@@ -401,22 +405,26 @@ def tile_list_photo_redshift_features_kernel(
             return placed(name, [P, width], U32, room, offset)
 
         colour_product(0, blocks_of(0))
-        late = [pick(2, HALF + n * QUARTER, QUARTER, colours[0][:, n, 0:QUARTER]) for n in range(2)]
+        late = [
+            pick(2, HALF, QUARTER, colours[0][:, 0, :]),
+            pick(3, HALF, QUARTER, placed("late_pick", [P, QUARTER], F32, 9)[:]),
+        ]
         xq.append(quantize("xq1", x_grouped[1][:], QUARTER))
         for n in range(2):
-            subtract(2, HALF + n * QUARTER, QUARTER, late[n])
+            subtract(2 + n, HALF, QUARTER, late[n])
         round_w3(0)
-        last = pick(3, HALF, HALF, colours[0][:, 2, :])
-        meet(0)
-        colour_product(1, blocks_of(1))
-        for n in range(2):
-            subtract(3, HALF + n * QUARTER, QUARTER, last[:, n * QUARTER : (n + 1) * QUARTER])
         round_x(2)
+        last = [pick(2 + n, TAIL, QUARTER, colours[1][:, n, :]) for n in range(2)]
+        meet(0)
+        colour_product(1, blocks_of(1)[0:2])
+        for n in range(2):
+            subtract(2 + n, TAIL, QUARTER, last[n])
         round_x(3)
+        colour_product(1, blocks_of(1)[2:4])
         w3q.append(quantize("w3q0", w3_grouped[0][:], N, behind("w3q0_w", N, 0, 0)))
         hq0 = quantize("hq0", h_tiles[0][:], HALF)
-        dq0 = quantize("dq0", d_tiles[0][:], HALF, behind("dq0_w", HALF, 0, 2048))
         xq_late = quantize("xq_late", x_late[:], HALF, behind("xq_late_w", HALF, 0, 4096))
+        dq0 = quantize("dq0", d_tiles[0][:], HALF, kept("dq0_w", [P, HALF], U32, tag="colours3"))
         xq.extend(columns_of(xq_late, n * QUARTER, QUARTER) for n in range(2))
         round_w3(1)
 

@@ -26,11 +26,11 @@ HALF = S // 2
 QUARTER = S // 4
 BLOCK = BANK // PACK
 TAIL = S - QUARTER
-GPSIMD_SHARE = (128, 64, 64)
+GPSIMD_SHARE = (168, 64, 64)
 SUM_BANKS = 4
 BLOCK_BANKS = 4
 RUN = 4
-W2_ON_GPSIMD = (96, 48)
+W2_ON_GPSIMD = (120, 60)
 ROOM = 8192
 ALIGN = 64
 
@@ -145,7 +145,8 @@ def tile_list_photo_redshift_features_kernel(
 
         early_colours = kept("early_colours", [P, PACK, HALF], F32)
         colours = [early_colours[:, :, 0:QUARTER], early_colours[:, :, QUARTER:HALF]]
-        colours += [kept("colours%d" % q, [P, PACK, QUARTER], F32)[:] for q in (2, 3)]
+        colours.append(kept("colours2", [P, PACK, QUARTER], F32)[:])
+        last_colours = [kept("last_colours0", [P, 2, QUARTER], F32)]
 
         gained_ranges = {
             (0, 0): [],
@@ -206,9 +207,14 @@ def tile_list_photo_redshift_features_kernel(
             nc.vector.tensor_copy(picked, planes[i][:].indirect(entries(idx2, j0, width)))
             return picked
 
+        def colour_rows(i, j0, width):
+            if j0 < HALF:
+                return early_colours[:, i, j0 : j0 + width]
+            return colours[2][:, i, :] if j0 < TAIL else last_colours[i // 2][:, i % 2, :]
+
         def subtract(i, j0, width, picked):
             nc.vector.tensor_tensor(
-                early_colours[:, i, j0 : j0 + width] if j0 < HALF else colours[j0 // QUARTER][:, i, :],
+                colour_rows(i, j0, width),
                 planes[i][:].indirect(entries(idx3, j0, width)),
                 picked,
                 ALU.subtract,
@@ -233,16 +239,18 @@ def tile_list_photo_redshift_features_kernel(
                 cols = slice(part * N // 2, (part + 1) * N // 2)
                 interleave(w3_grouped[g][:, cols, :], w3_raw[g][:, :, cols])
 
-        x_late = placed("x_late", [P, HALF, PACK], BF16, 4)
         x_grouped = [
             placed("x_grouped0", [P, QUARTER, PACK], BF16, 9),
             placed("x_grouped1", [P, QUARTER, PACK], BF16, 7),
-            x_late[:, 0:QUARTER, :],
-            x_late[:, QUARTER:HALF, :],
+            placed("x_grouped2", [P, QUARTER, PACK], BF16, 4),
+            placed("x_grouped3", [P, QUARTER, PACK], BF16, 10),
         ]
 
         def round_x(q):
             interleave(x_grouped[q][:], colours[q])
+
+        def round_last_x(pair):
+            interleave(x_grouped[3][:, :, 2 * pair : 2 * pair + 2], last_colours[pair][:])
 
         def gather(i, width, tags):
             starts = (HALF, 0) if width == HALF else (0, QUARTER)
@@ -261,6 +269,7 @@ def tile_list_photo_redshift_features_kernel(
         template_product(1, 0)
         round_w2(1)
         gather(2, QUARTER, ("pick2", "pick4"))
+        round_last_x(0)
         template_product(1, 1)
         for g in range(R_PASSES):
             nc.sync.dma_start(
@@ -301,7 +310,7 @@ def tile_list_photo_redshift_features_kernel(
                 return BLOCK if (j, g) == (TAIL, 0) else 0
             if g == 0:
                 return BLOCK
-            return GPSIMD_SHARE[j // QUARTER] if j % QUARTER == 0 else 0
+            return max(0, min(BLOCK, GPSIMD_SHARE[j // QUARTER] - j % QUARTER))
 
         b_gained = [
             placed("b_gained%d" % q, [P, (QUARTER + GPSIMD_SHARE[q]) // RUN, PACK, RUN], F32, (0, 1, 6)[q])
@@ -346,7 +355,7 @@ def tile_list_photo_redshift_features_kernel(
         d_tiles = [placed("d0", [P, HALF, PACK], BF16, 7)]
         both_tiles = {}
         for q in (1, 2):
-            both = placed("hd%d" % q, [P, 2, HALF, PACK], BF16, 4 * q)
+            both = placed("hd%d" % q, [P, 2, HALF, PACK], BF16, 12 - 2 * q)
             both_tiles[q] = both
             h_tiles.append(both[:, 0])
             d_tiles.append(both[:, 1])
@@ -417,15 +426,16 @@ def tile_list_photo_redshift_features_kernel(
         last = [pick(2 + n, TAIL, QUARTER, colours[1][:, n, :]) for n in range(2)]
         meet(0)
         colour_product(1, blocks_of(1)[0:2])
+        last_colours.append(kept("last_colours1", [P, 2, QUARTER], F32, tag="a_gained1_%d" % GPSIMD_SHARE[0]))
         for n in range(2):
             subtract(2 + n, TAIL, QUARTER, last[n])
-        round_x(3)
+        round_last_x(1)
         colour_product(1, blocks_of(1)[2:4])
         w3q.append(quantize("w3q0", w3_grouped[0][:], N, behind("w3q0_w", N, 0, 0)))
         hq0 = quantize("hq0", h_tiles[0][:], HALF)
-        xq_late = quantize("xq_late", x_late[:], HALF, behind("xq_late_w", HALF, 0, 4096))
-        dq0 = quantize("dq0", d_tiles[0][:], HALF, kept("dq0_w", [P, HALF], U32, tag="colours3"))
-        xq.extend(columns_of(xq_late, n * QUARTER, QUARTER) for n in range(2))
+        for q in (2, 3):
+            xq.append(quantize("xq%d" % q, x_grouped[q][:], QUARTER, behind("xq%d_w" % q, QUARTER, 0, 1024 * q)))
+        dq0 = quantize("dq0", d_tiles[0][:], HALF, kept("dq0_w", [P, HALF], U32, tag="a_gained1_%d" % GPSIMD_SHARE[0]))
         round_w3(1)
 
         meet(1)

@@ -145,8 +145,8 @@ def tile_list_photo_redshift_features_kernel(
 
         early_colours = kept("early_colours", [P, PACK, HALF], F32)
         colours = [early_colours[:, :, 0:QUARTER], early_colours[:, :, QUARTER:HALF]]
-        colours.append(kept("colours2", [P, PACK, QUARTER], F32)[:])
-        last_colours = [kept("last_colours0", [P, 2, QUARTER], F32)]
+        late_low = kept("late_low", [P, 2, HALF], F32)
+        late_high = [kept("late_high2", [P, 2, QUARTER], F32)]
 
         gained_ranges = {
             (0, 0): [],
@@ -210,7 +210,9 @@ def tile_list_photo_redshift_features_kernel(
         def colour_rows(i, j0, width):
             if j0 < HALF:
                 return early_colours[:, i, j0 : j0 + width]
-            return colours[2][:, i, :] if j0 < TAIL else last_colours[i // 2][:, i % 2, :]
+            if i < 2:
+                return late_low[:, i, :]
+            return late_high[j0 // TAIL][:, i - 2, :]
 
         def subtract(i, j0, width, picked):
             nc.vector.tensor_tensor(
@@ -242,24 +244,21 @@ def tile_list_photo_redshift_features_kernel(
         x_grouped = [
             placed("x_grouped0", [P, QUARTER, PACK], BF16, 9),
             placed("x_grouped1", [P, QUARTER, PACK], BF16, 7),
-            placed("x_grouped2", [P, QUARTER, PACK], BF16, 4),
-            placed("x_grouped3", [P, QUARTER, PACK], BF16, 10),
         ]
+        x_late = placed("x_late", [P, HALF, PACK], BF16, 10)
 
         def round_x(q):
             interleave(x_grouped[q][:], colours[q])
 
-        def round_last_x(pair):
-            interleave(x_grouped[3][:, :, 2 * pair : 2 * pair + 2], last_colours[pair][:])
+        def round_late_x(n):
+            interleave(x_late[:, n * QUARTER : (n + 1) * QUARTER, 2:4], late_high[n][:])
 
         def gather(i, width, tags):
-            starts = (HALF, 0) if width == HALF else (0, QUARTER)
             picks = [
-                pick(i, starts[n], width, kept("pick%d_%d" % (i, n), [P, width], F32, tag=tags[n])[:]) for n in range(2)
+                pick(i, n * width, width, kept("pick%d_%d" % (i, n), [P, width], F32, tag=tags[n])[:]) for n in range(2)
             ]
-            for c0 in range(0, width, QUARTER):
-                subtract(i, starts[0] + c0, QUARTER, picks[0][:, c0 : c0 + QUARTER])
-            subtract(i, starts[1], width, picks[1])
+            for n in range(2):
+                subtract(i, n * width, width, picks[n])
 
         gather(0, HALF, ("pick0", "pick2"))
         template_product(0, 0)
@@ -269,7 +268,7 @@ def tile_list_photo_redshift_features_kernel(
         template_product(1, 0)
         round_w2(1)
         gather(2, QUARTER, ("pick2", "pick4"))
-        round_last_x(0)
+        interleave(x_late[:, :, 0:2], late_low[:])
         template_product(1, 1)
         for g in range(R_PASSES):
             nc.sync.dma_start(
@@ -422,19 +421,19 @@ def tile_list_photo_redshift_features_kernel(
         for n in range(2):
             subtract(2 + n, HALF, QUARTER, late[n])
         round_w3(0)
-        round_x(2)
+        round_late_x(0)
         last = [pick(2 + n, TAIL, QUARTER, colours[1][:, n, :]) for n in range(2)]
         meet(0)
         colour_product(1, blocks_of(1)[0:2])
-        last_colours.append(kept("last_colours1", [P, 2, QUARTER], F32, tag="a_gained1_%d" % GPSIMD_SHARE[0]))
+        late_high.append(kept("late_high3", [P, 2, QUARTER], F32, tag="a_gained1_%d" % GPSIMD_SHARE[0]))
         for n in range(2):
             subtract(2 + n, TAIL, QUARTER, last[n])
-        round_last_x(1)
+        round_late_x(1)
         colour_product(1, blocks_of(1)[2:4])
         w3q.append(quantize("w3q0", w3_grouped[0][:], N, behind("w3q0_w", N, 0, 0)))
         hq0 = quantize("hq0", h_tiles[0][:], HALF)
-        for q in (2, 3):
-            xq.append(quantize("xq%d" % q, x_grouped[q][:], QUARTER, behind("xq%d_w" % q, QUARTER, 0, 1024 * q)))
+        xq_late = quantize("xq_late", x_late[:], HALF, behind("xq_late_w", HALF, 0, 2048))
+        xq.extend(columns_of(xq_late, n * QUARTER, QUARTER) for n in range(2))
         dq0 = quantize("dq0", d_tiles[0][:], HALF, kept("dq0_w", [P, HALF], U32, tag="a_gained1_%d" % GPSIMD_SHARE[0]))
         round_w3(1)
 

@@ -31,6 +31,7 @@ SUM_BANKS = 4
 BLOCK_BANKS = 4
 RUN = 4
 W2_ON_GPSIMD = (120, 60)
+W3_ON_GPSIMD = 160
 ROOM = 8192
 ALIGN = 64
 
@@ -236,13 +237,13 @@ def tile_list_photo_redshift_features_kernel(
             nc.gpsimd.tensor_scalar(grouped, rows, 1.0, 0.0, ALU.mult, ALU.add)
             nc.scalar.copy(*w2_walks(g, W2_ON_GPSIMD[g], P))
 
-        def round_w3(g):
-            for part in range(2):
-                cols = slice(part * N // 2, (part + 1) * N // 2)
+        def round_w3(g, first):
+            middle = (first + N) // 2
+            for cols in (slice(first, middle), slice(middle, N)):
                 interleave(w3_grouped[g][:, cols, :], w3_raw[g][:, :, cols])
 
         x_grouped = [
-            placed("x_grouped0", [P, QUARTER, PACK], BF16, 9),
+            placed("x_grouped0", [P, QUARTER, PACK], BF16, 8, 4096 - ALIGN),
             placed("x_grouped1", [P, QUARTER, PACK], BF16, 7),
         ]
         x_late = placed("x_late", [P, HALF, PACK], BF16, 10)
@@ -350,7 +351,7 @@ def tile_list_photo_redshift_features_kernel(
         def product_on_gpsimd(grouped, a, minus_b):
             nc.gpsimd.tensor_tensor(runs_out(grouped, RUN), a, minus_b, ALU.mult)
 
-        h_tiles = [placed("h0", [P, HALF, PACK], BF16, 9)]
+        h_tiles = [placed("h0", [P, HALF, PACK], BF16, 8, 4096)]
         d_tiles = [placed("d0", [P, HALF, PACK], BF16, 7)]
         both_tiles = {}
         for q in (1, 2):
@@ -412,15 +413,23 @@ def tile_list_photo_redshift_features_kernel(
         def behind(name, width, room, offset):
             return placed(name, [P, width], U32, room, offset)
 
+        nc.gpsimd.tensor_scalar(
+            w3_grouped[1][:, 0:W3_ON_GPSIMD, :],
+            w3_raw[1][:, :, 0:W3_ON_GPSIMD].rearrange("p i n -> p n i"),
+            1.0,
+            0.0,
+            ALU.mult,
+            ALU.add,
+        )
         colour_product(0, blocks_of(0))
         late = [
             pick(2, HALF, QUARTER, colours[0][:, 0, :]),
-            pick(3, HALF, QUARTER, placed("late_pick", [P, QUARTER], F32, 9)[:]),
+            pick(3, HALF, QUARTER, placed("late_pick", [P, QUARTER], F32, 8, 4096)[:]),
         ]
         xq.append(quantize("xq1", x_grouped[1][:], QUARTER))
         for n in range(2):
             subtract(2 + n, HALF, QUARTER, late[n])
-        round_w3(0)
+        round_w3(0, 0)
         round_late_x(0)
         last = [pick(2 + n, TAIL, QUARTER, colours[1][:, n, :]) for n in range(2)]
         meet(0)
@@ -435,7 +444,7 @@ def tile_list_photo_redshift_features_kernel(
         xq_late = quantize("xq_late", x_late[:], HALF, behind("xq_late_w", HALF, 0, 2048))
         xq.extend(columns_of(xq_late, n * QUARTER, QUARTER) for n in range(2))
         dq0 = quantize("dq0", d_tiles[0][:], HALF, kept("dq0_w", [P, HALF], U32, tag="a_gained1_%d" % GPSIMD_SHARE[0]))
-        round_w3(1)
+        round_w3(1, W3_ON_GPSIMD)
 
         meet(1)
         colour_product(2, blocks_of(2))

@@ -94,8 +94,9 @@ def tile_list_photo_redshift_features_kernel(
             nc.sync.dma_start(out=planes[1 + g][:], in_=x_rows[1 + g])
         nc.sync.dma_start(out=planes[PACK - 1][:], in_=x_rows[PACK - 1])
 
-        warm = kept("warm", [P, 1], F32)
-        nc.scalar.activation(warm[:], gains[:, 0, 0:1], ACT.Gelu_apprx_tanh)
+        warm = kept("warm", [P, 2], F32)
+        nc.gpsimd.memset(warm[:, 0:1], 0.0)
+        nc.scalar.activation(warm[:, 1:2], warm[:, 0:1], ACT.Gelu_apprx_tanh)
         minus_gains = kept("minus_gains", [P, R_PASSES, PACK], F32)
         nc.scalar.activation(minus_gains[:], gains[:], ACT.Copy, scale=-1.0)
 

from contextlib import ExitStack

import concourse.mybir as mybir

K, T, S, H, N = 512, 2048, 1024, 1024, 512
FLOPS = 2 * S * (2 * K * H + 2 * H * N)

F32 = mybir.dt.float32
BF16 = mybir.dt.bfloat16
I32 = mybir.dt.int32
U32 = mybir.dt.uint32
U16 = mybir.dt.uint16
U8 = mybir.dt.uint8
FP8X4 = mybir.dt.float8_e4m3fn_x4
FP4X4 = mybir.dt.float4_e2m1fn_x4
ALU = mybir.AluOpType
ACT = mybir.ActivationFunctionType

P = 128
PACK = 4
PASS = P * PACK
BANK = 512
LIST_ROWS = 16
R_PASSES = H // PASS
HALF = S // 2
QUARTER = S // 4
BLOCK = BANK // PACK
TAIL = S - QUARTER
GPSIMD_SHARE = (168, 64, 64)
SUM_BANKS = 4
BLOCK_BANKS = 4
RUN = 4
W2_ON_GPSIMD = (120, 60)
W3_ON_GPSIMD = 160
ROOM = 8192
ALIGN = 64


def tile_list_photo_redshift_features_kernel(
    tc, tab_words, tab_scales, offs, xT, offs2, offs3, w1_words, w1_scales, w2, gain, w3, w4_words, w4_scales, out
):
    nc = tc.nc
    with ExitStack() as ctx:
        keep = ctx.enter_context(tc.tile_pool(name="keep", bufs=1))
        ring = ctx.enter_context(tc.tile_pool(name="ring", bufs=2))
        laid = ctx.enter_context(tc.tile_pool(name="laid", bufs=1))
        psum = ctx.enter_context(tc.psum_pool(name="psum", bufs=1))

        def kept(name, shape, dtype, tag=None):
            return keep.tile(shape, dtype, name=name, tag=tag or name, align_bytes=ALIGN)

        def placed(name, shape, dtype, room, offset=0):
            return laid.tile(shape, dtype, name=name, tag=name, align_bytes=ALIGN, offset=room * ROOM + offset)

        def load_scale_rows(tile, rows):
            for q in range(4):
                nc.sync.dma_start(out=tile[32 * q : 32 * q + 4].bitcast(I32), in_=rows[4 * q : 4 * q + 4].bitcast(I32))

        idx1 = kept("idx1", [P, S // LIST_ROWS], U16)
        idx2 = kept("idx2", [P, S // LIST_ROWS], U16)
        idx3 = kept("idx3", [P, S // LIST_ROWS], U16)
        tab_s = kept("tab_s", [P, T], U8)
        tab_w = placed("tab_w", [P, T], I32, 5)
        w1_s = kept("w1_s", [P, H], U8)
        w1_w = kept("w1_w", [P, 2 * H], U8)
        w4_s = kept("w4_s", [P, R_PASSES, N], U8)
        w4_w = kept("w4_w", [P, R_PASSES, N], I32)
        gains = kept("gains", [P, R_PASSES, PACK], F32)
        planes = [placed("plane%d" % i, [P, T], F32, i) for i in range(PACK)]
        x_rows = xT.rearrange("(p i) t -> i p t", i=PACK)
        w2_raw = [placed("w2_raw%d" % g, [P, PACK, PASS], F32, (4, 6)[g]) for g in range(R_PASSES)]
        w3_raw = [placed("w3_raw%d" % g, [P, PACK, N], F32, 4 + g) for g in range(R_PASSES)]

        def entries(idx, j0, width):
            return idx[:, j0 // LIST_ROWS : (j0 + width) // LIST_ROWS]

        nc.gpsimd.memset(tab_s[:].bitcast(I32), 0)
        nc.vector.memset(w1_s[:].bitcast(I32), 0)
        nc.gpsimd.memset(w4_s[:].rearrange("p a c -> p (a c)").bitcast(I32), 0)

        nc.scalar.dma_start(out=gains[:], in_=gain.rearrange("(g p t) -> p g t", g=R_PASSES, t=PACK))
        nc.sync.dma_start(out=w1_w[:].bitcast(I32), in_=w1_words[0].bitcast(I32))
        nc.sync.dma_start(idx1[:], offs)
        load_scale_rows(tab_s, tab_scales[0])
        nc.sync.dma_start(out=tab_w[:], in_=tab_words[0].rearrange("p t i -> p (t i)").bitcast(I32))
        load_scale_rows(w1_s, w1_scales[0])
        nc.sync.dma_start(out=planes[0][:], in_=x_rows[0])
        nc.sync.dma_start(idx2[:], offs2)
        nc.sync.dma_start(idx3[:], offs3)
        for g in range(R_PASSES):
            nc.sync.dma_start(
                out=w2_raw[g][:], in_=w2[:, g * PASS : (g + 1) * PASS].rearrange("(p i) r -> p i r", i=PACK)
            )
            nc.sync.dma_start(out=planes[1 + g][:], in_=x_rows[1 + g])
        nc.sync.dma_start(out=planes[PACK - 1][:], in_=x_rows[PACK - 1])

        warm = kept("warm", [P, 2], F32)
        nc.gpsimd.memset(warm[:, 0:1], 0.0)
        nc.scalar.activation(warm[:, 1:2], warm[:, 0:1], ACT.Gelu_apprx_tanh)
        minus_gains = kept("minus_gains", [P, R_PASSES, PACK], F32)
        nc.scalar.activation(minus_gains[:], gains[:], ACT.Copy, scale=-1.0)

        w1_wo = kept("w1_wo", [P, 2 * H], U8)
        w1_so = kept("w1_so", [P, H], U8)
        nc.vector.tensor_copy(
            w1_wo[:].bitcast(U16).rearrange("p (g t m) -> p g t m", g=R_PASSES, t=PACK),
            w1_w[:].bitcast(U16).rearrange("p (g m t) -> p g t m", g=R_PASSES, t=PACK),
        )
        v_s = kept("v_s", [P, S], U8)
        nc.vector.tensor_copy(v_s[:], tab_s[:].indirect(idx1[:]))
        v_w = [kept("v_w0", [P, HALF], U32)]
        nc.vector.tensor_copy(v_w[0][:], tab_w[:].bitcast(U32).indirect(entries(idx1, 0, HALF)))
        nc.gpsimd.tensor_copy(
            w1_so[:].rearrange("p (g t m) -> p g t m", g=R_PASSES, t=PACK),
            w1_s[:].rearrange("p (g m t) -> p g t m", g=R_PASSES, t=PACK),
        )
        v_w.append(kept("v_w1", [P, HALF], U32))
        nc.vector.tensor_copy(v_w[1][:], tab_w[:].bitcast(U32).indirect(entries(idx1, HALF, HALF)))

        def sum_bank(shape):
            return psum.tile(shape, F32, name="sum_bank", tag="sum_bank", bufs=SUM_BANKS)

        def template_pass(bank, j0, width, g, t, stop):
            r0 = g * PASS + t * P
            half, c0 = divmod(j0, HALF)
            nc.tensor.matmul_mx(
                out=bank,
                lhsT=w1_wo[:, 2 * r0 : 2 * (r0 + P)].bitcast(FP4X4),
                lhsT_scale=w1_so[:, r0 : r0 + P],
                rhs=v_w[half][:, c0 : c0 + width].bitcast(FP8X4),
                rhs_scale=v_s[:, j0 : j0 + width],
                start=True,
                stop=stop,
            )

        groups = QUARTER // RUN
        a_first = kept("a_first", [P, 2, R_PASSES, groups, PACK, RUN], F32)
        a_third = kept("a_third", [P, R_PASSES, groups, PACK, RUN], F32)
        a_tail = kept("a_tail", [P, BLOCK // RUN, PACK, RUN], F32)
        a_quarter = [a_first[:, 0], a_first[:, 1], a_third[:]]

        def a_plain(j, width, g):
            if j >= TAIL:
                return a_tail[:]
            q, c0 = divmod(j, QUARTER)
            return a_quarter[q][:, g, c0 // RUN : (c0 + width) // RUN]

        early_colours = kept("early_colours", [P, PACK, HALF], F32)
        colours = [early_colours[:, :, 0:QUARTER], early_colours[:, :, QUARTER:HALF]]
        late_low = kept("late_low", [P, 2, HALF], F32)
        late_high = [kept("late_high2", [P, 2, QUARTER], F32)]

        gained_ranges = {
            (0, 0): [],
            (0, 1): [(GPSIMD_SHARE[0], QUARTER), (QUARTER + GPSIMD_SHARE[1], HALF)],
            (1, 0): [(S - BLOCK, S)],
            (1, 1): [(HALF + GPSIMD_SHARE[2], S)],
        }
        gained_tiles = {
            (g, j0): kept("a_gained%d_%d" % (g, j0), [P, (j1 - j0) // RUN, PACK, RUN], F32)
            for (half, g), ranges in gained_ranges.items()
            for j0, j1 in ranges
        }

        def a_gained(j, width, g):
            j0 = max(first for first, end in gained_ranges[j // HALF, g] if first <= j)
            return gained_tiles[g, j0][:, (j - j0) // RUN : (j - j0 + width) // RUN]

        def in_runs(columns):
            return columns.rearrange("p (c e) -> p c e", e=RUN)

        def template_product(half, g):
            for t in range(PACK):
                bank = sum_bank([P, HALF])
                template_pass(bank[:], half * HALF, HALF, g, t, True)
                if half == 0:
                    nc.scalar.copy(a_first[:, :, g, :, t, :], bank[:].rearrange("p (q c e) -> p q c e", q=2, e=RUN))
                else:
                    nc.scalar.copy(a_third[:, g, :, t, :], in_runs(bank[:, 0:QUARTER]))
                    if g == 0:
                        nc.scalar.copy(a_tail[:, :, t, :], in_runs(bank[:, QUARTER : QUARTER + BLOCK]))
                for j0, j1 in gained_ranges[half, g]:
                    nc.scalar.activation(
                        gained_tiles[g, j0][:, :, t, :],
                        in_runs(bank[:, j0 - half * HALF : j1 - half * HALF]),
                        ACT.Copy,
                        scale=minus_gains[:, g, t : t + 1],
                    )

        def quantize(name, grouped, width, codes=None):
            if codes is None:
                codes = kept(name + "_w", [P, width], U32)
            scales = kept(name + "_s", [P, width], U8)
            nc.vector.quantize_mx(
                out=codes[:].bitcast(FP8X4), scales=scales[:], in_=grouped.rearrange("p c i -> p (c i)")
            )
            return codes, scales

        def runs_in(rows, run):
            return rows.rearrange("p t (c e) -> p c t e", e=run)

        def runs_out(grouped, run):
            return grouped.rearrange("p (c e) t -> p c t e", e=run)

        def interleave(grouped, rows):
            nc.scalar.copy(runs_out(grouped, 2), runs_in(rows, 2))

        def pick(i, j0, width, picked):
            nc.vector.tensor_copy(picked, planes[i][:].indirect(entries(idx2, j0, width)))
            return picked

        def colour_rows(i, j0, width):
            if j0 < HALF:
                return early_colours[:, i, j0 : j0 + width]
            if i < 2:
                return late_low[:, i, :]
            return late_high[j0 // TAIL][:, i - 2, :]

        def subtract(i, j0, width, picked):
            nc.vector.tensor_tensor(
                colour_rows(i, j0, width),
                planes[i][:].indirect(entries(idx3, j0, width)),
                picked,
                ALU.subtract,
            )

        w2_grouped = [kept("w2_grouped%d" % g, [P, PASS, PACK], BF16, tag="pick%d" % g) for g in range(R_PASSES)]
        w3_grouped = [kept("w3_grouped0", [P, N, PACK], BF16), placed("w3_grouped1", [P, N, PACK], BF16, 8)]

        def w2_walks(g, m0, m1):
            return (
                w2_grouped[g][:].rearrange("p (t m) i -> p m t i", t=PACK)[:, m0:m1],
                w2_raw[g][:].rearrange("p i (m t) -> p m t i", t=PACK)[:, m0:m1],
            )

        def round_w2(g):
            grouped, rows = w2_walks(g, 0, W2_ON_GPSIMD[g])
            nc.gpsimd.tensor_scalar(grouped, rows, 1.0, 0.0, ALU.mult, ALU.add)
            nc.scalar.copy(*w2_walks(g, W2_ON_GPSIMD[g], P))

        def round_w3(g, first):
            middle = (first + N) // 2
            for cols in (slice(first, middle), slice(middle, N)):
                interleave(w3_grouped[g][:, cols, :], w3_raw[g][:, :, cols])

        x_grouped = [
            placed("x_grouped0", [P, QUARTER, PACK], BF16, 8, 4096 - ALIGN),
            placed("x_grouped1", [P, QUARTER, PACK], BF16, 7),
        ]
        x_late = placed("x_late", [P, HALF, PACK], BF16, 10)

        def round_x(q):
            interleave(x_grouped[q][:], colours[q])

        def round_late_x(n):
            interleave(x_late[:, n * QUARTER : (n + 1) * QUARTER, 2:4], late_high[n][:])

        def gather(i, width, tags):
            picks = [
                pick(i, n * width, width, kept("pick%d_%d" % (i, n), [P, width], F32, tag=tags[n])[:]) for n in range(2)
            ]
            for n in range(2):
                subtract(i, n * width, width, picks[n])

        gather(0, HALF, ("pick0", "pick2"))
        template_product(0, 0)
        round_w2(0)
        gather(1, HALF, ("pick1", "pick3"))
        template_product(0, 1)
        template_product(1, 0)
        round_w2(1)
        gather(2, QUARTER, ("pick2", "pick4"))
        interleave(x_late[:, :, 0:2], late_low[:])
        template_product(1, 1)
        for g in range(R_PASSES):
            nc.sync.dma_start(
                out=w3_raw[g][:], in_=w3[g * PASS : (g + 1) * PASS, :].rearrange("(p i) n -> p i n", i=PACK)
            )
        nc.sync.dma_start(out=w4_w[:], in_=w4_words.rearrange("a p c i -> p a (c i)").bitcast(I32))
        load_scale_rows(w4_s, w4_scales.rearrange("a q c -> q a c"))
        gather(3, QUARTER, ("pick3", "pick5"))
        w2q = [
            quantize("w2q%d" % g, w2_grouped[g][:], PASS, kept("w2q%d_w" % g, [P, PASS], U32, tag=("pick3", "pick5")[g]))
            for g in range(R_PASSES)
        ]
        round_x(0)
        round_x(1)
        xq = [quantize("xq0", x_grouped[0][:], QUARTER)]

        def colour_pass(bank, j, g, t, start):
            quarter, c0 = divmod(j, QUARTER)
            nc.tensor.matmul_mx(
                out=bank[:, t, :],
                lhsT=w2q[g][0][:, t * P : (t + 1) * P].bitcast(FP8X4),
                lhsT_scale=w2q[g][1][:, t * P : (t + 1) * P],
                rhs=xq[quarter][0][:, c0 : c0 + BLOCK].bitcast(FP8X4),
                rhs_scale=xq[quarter][1][:, c0 : c0 + BLOCK],
                start=start,
                stop=True,
            )

        def residual_in_psum(j, g, grouped):
            bank = sum_bank([P, PACK, BLOCK])
            for t in range(PACK):
                template_pass(bank[:, t, :], j, BLOCK, g, t, False)
                colour_pass(bank, j, g, t, False)
            interleave(grouped, bank[:])

        def gpsimd_columns(j, g):
            if j >= TAIL:
                return BLOCK if (j, g) == (TAIL, 0) else 0
            if g == 0:
                return BLOCK
            return max(0, min(BLOCK, GPSIMD_SHARE[j // QUARTER] - j % QUARTER))

        b_gained = [
            placed("b_gained%d" % q, [P, (QUARTER + GPSIMD_SHARE[q]) // RUN, PACK, RUN], F32, (0, 1, 6)[q])
            for q in range(3)
        ]
        b_gained.append(placed("b_gained3", [P, BLOCK // RUN, PACK, RUN], F32, 0, 3 * ROOM // 4))
        b_banks = {}

        def colour_product(q, blocks):
            for j, g in blocks:
                bank = psum.tile([P, PACK, BLOCK], F32, name="block_bank", tag="block_bank", bufs=BLOCK_BANKS)
                b_banks[j, g] = bank
                for t in range(PACK):
                    colour_pass(bank, j, g, t, True)
                columns = gpsimd_columns(j, g)
                c0 = g * QUARTER + j % QUARTER
                for t in range(PACK if columns else 0):
                    nc.scalar.activation(
                        b_gained[q][:, c0 // RUN : (c0 + columns) // RUN, t, :],
                        in_runs(bank[:, t, 0:columns]),
                        ACT.Copy,
                        scale=minus_gains[:, g, t : t + 1],
                    )

        def blocks_of(q):
            return [(q * QUARTER + n * BLOCK, g) for g in range(R_PASSES) for n in range(2)]

        def join(grouped, a, minus_b, op):
            nc.vector.tensor_tensor(runs_out(grouped, RUN), a, runs_in(minus_b, RUN), op)

        def join_h(grouped, j, g):
            c0 = gpsimd_columns(j, g)
            join(grouped[:, c0:BLOCK, :], a_gained(j + c0, BLOCK - c0, g), b_banks[j, g][:, :, c0:BLOCK], ALU.mult)

        def join_d(grouped, j, g):
            join(grouped, a_plain(j, BLOCK, g), b_banks[j, g][:], ALU.add)

        def product_on_gpsimd(grouped, a, minus_b):
            nc.gpsimd.tensor_tensor(runs_out(grouped, RUN), a, minus_b, ALU.mult)

        h_tiles = [placed("h0", [P, HALF, PACK], BF16, 8, 4096)]
        d_tiles = [placed("d0", [P, HALF, PACK], BF16, 7)]
        both_tiles = {}
        for q in (1, 2):
            both = placed("hd%d" % q, [P, 2, HALF, PACK], BF16, 12 - 2 * q)
            both_tiles[q] = both
            h_tiles.append(both[:, 0])
            d_tiles.append(both[:, 1])

        def meet(q):
            share = QUARTER + GPSIMD_SHARE[q]
            cuts = (0, QUARTER, share) if q == 0 else (0, share)
            a = a_quarter[q].rearrange("p g c t e -> p (g c) t e")
            for c0, c1 in zip(cuts, cuts[1:]):
                product_on_gpsimd(
                    h_tiles[q][:, c0:c1, :], a[:, c0 // RUN : c1 // RUN], b_gained[q][:, c0 // RUN : c1 // RUN]
                )
            for n, (j, g) in enumerate(blocks_of(q)):
                cols = slice(n * BLOCK, (n + 1) * BLOCK)
                if gpsimd_columns(j, g) < BLOCK:
                    join_h(h_tiles[q][:, cols, :], j, g)
                join_d(d_tiles[q][:, cols, :], j, g)

        y_banks = {}

        def y_passes(j0, width, weights, operand, closes):
            tiles_a_bank = 2 if j0 == TAIL else BANK // width
            for n0 in range(0, N // P, tiles_a_bank):
                opens = (j0, n0) not in y_banks
                if opens:
                    y_banks[j0, n0] = sum_bank([P, tiles_a_bank, width])
                bank = y_banks[j0, n0]
                for n in range(tiles_a_bank):
                    cols = slice((n0 + n) * P, (n0 + n + 1) * P)
                    nc.tensor.matmul_mx(
                        out=bank[:, n, :],
                        lhsT=weights[0][:, cols].bitcast(FP8X4),
                        lhsT_scale=weights[1][:, cols],
                        rhs=operand[0].bitcast(FP8X4),
                        rhs_scale=operand[1],
                        start=(opens and n == 0),
                        stop=(closes and n == tiles_a_bank - 1),
                    )
                if closes:
                    result = ring.tile([P, tiles_a_bank, width], F32, name="result", tag="result", bufs=5)
                    nc.scalar.activation(result[:], bank[:], ACT.Gelu_apprx_tanh)
                    rows = slice(n0 * P, (n0 + tiles_a_bank) * P)
                    queue = nc.scalar if j0 == TAIL and n0 > 0 else nc.sync
                    queue.dma_start(out=out[rows, j0 : j0 + width].rearrange("(n p) j -> p n j", p=P), in_=result[:])

        def columns_of(quantized, c0, columns):
            return quantized[0][:, c0 : c0 + columns], quantized[1][:, c0 : c0 + columns]

        w4q = [(w4_w[:, g, :], w4_s[:, g, :]) for g in range(R_PASSES)]
        w3q = []

        def term(q, g, weights, quantized, closes=False):
            y_passes(q * QUARTER, QUARTER, weights[g], columns_of(quantized, g * QUARTER, QUARTER), closes)

        def behind(name, width, room, offset):
            return placed(name, [P, width], U32, room, offset)

        nc.gpsimd.tensor_scalar(
            w3_grouped[1][:, 0:W3_ON_GPSIMD, :],
            w3_raw[1][:, :, 0:W3_ON_GPSIMD].rearrange("p i n -> p n i"),
            1.0,
            0.0,
            ALU.mult,
            ALU.add,
        )
        colour_product(0, blocks_of(0))
        late = [
            pick(2, HALF, QUARTER, colours[0][:, 0, :]),
            pick(3, HALF, QUARTER, placed("late_pick", [P, QUARTER], F32, 8, 4096)[:]),
        ]
        xq.append(quantize("xq1", x_grouped[1][:], QUARTER))
        for n in range(2):
            subtract(2 + n, HALF, QUARTER, late[n])
        round_w3(0, 0)
        round_late_x(0)
        last = [pick(2 + n, TAIL, QUARTER, colours[1][:, n, :]) for n in range(2)]
        meet(0)
        colour_product(1, blocks_of(1)[0:2])
        late_high.append(kept("late_high3", [P, 2, QUARTER], F32, tag="a_gained1_%d" % GPSIMD_SHARE[0]))
        for n in range(2):
            subtract(2 + n, TAIL, QUARTER, last[n])
        round_late_x(1)
        colour_product(1, blocks_of(1)[2:4])
        w3q.append(quantize("w3q0", w3_grouped[0][:], N, behind("w3q0_w", N, 0, 0)))
        hq0 = quantize("hq0", h_tiles[0][:], HALF)
        xq_late = quantize("xq_late", x_late[:], HALF, behind("xq_late_w", HALF, 0, 2048))
        xq.extend(columns_of(xq_late, n * QUARTER, QUARTER) for n in range(2))
        dq0 = quantize("dq0", d_tiles[0][:], HALF, kept("dq0_w", [P, HALF], U32, tag="a_gained1_%d" % GPSIMD_SHARE[0]))
        round_w3(1, W3_ON_GPSIMD)

        meet(1)
        colour_product(2, blocks_of(2))
        d_last = placed("d_last", [P, 3 * BLOCK, PACK], BF16, 3)
        summed_blocks = [(S - BLOCK, 0), (S - BLOCK, 1), (TAIL, 1)]
        for n, (j, g) in enumerate(summed_blocks):
            if n == 2:
                term(0, 0, w3q, hq0)
                term(0, 0, w4q, dq0)
                term(0, 1, w4q, dq0)
            residual_in_psum(j, g, d_last[:, n * BLOCK : (n + 1) * BLOCK, :])
        w3q.append(quantize("w3q1", w3_grouped[1][:], N, behind("w3q1_w", N, 1, 0)))
        hdq1 = quantize("hdq1", both_tiles[1][:].rearrange("p s c i -> p (s c) i"), S)
        hq1, dq1 = columns_of(hdq1, 0, HALF), columns_of(hdq1, HALF, HALF)
        term(0, 1, w3q, hq0, True)

        meet(2)
        colour_product(3, [(TAIL, 0), (S - BLOCK, 0), (S - BLOCK, 1), (TAIL, 1)])
        for g in range(R_PASSES):
            term(1, g, w3q, hq1)
        for g in range(R_PASSES):
            term(1, g, w4q, dq1, g == R_PASSES - 1)
        hq2 = quantize("hq2", h_tiles[2], HALF)
        summed = quantize("dq_last", d_last[:], 3 * BLOCK, behind("dq_last_w", 3 * BLOCK, 6, 0))
        dq2 = quantize("dq2", d_tiles[2], HALF, behind("dq2_w", HALF, 6, 2048))
        for g in range(R_PASSES):
            term(2, g, w3q, hq2)
        for g in range(R_PASSES):
            term(2, g, w4q, dq2, g == R_PASSES - 1)
        for n, (j, g) in enumerate(summed_blocks):
            y_passes(j, BLOCK, w4q[g], columns_of(summed, n * BLOCK, BLOCK), False)

        tail = placed("tail", [P, 5, BLOCK, PACK], BF16, 3, 3 * BLOCK * PACK * 2 - ALIGN)
        product_on_gpsimd(tail[:, 0], a_tail[:], b_gained[3][:])
        for g in range(R_PASSES):
            join_h(tail[:, 2 + g], S - BLOCK, g)
        join_d(tail[:, 4], TAIL, 0)
        h_both = quantize(
            "hq_both", tail[:, 2:4].rearrange("p g c i -> p (g c) i"), QUARTER, behind("hq_both_w", QUARTER, 0, 3 * ROOM // 4)
        )
        for g in range(R_PASSES):
            y_passes(S - BLOCK, BLOCK, w3q[g], columns_of(h_both, g * BLOCK, BLOCK), g == R_PASSES - 1)
        d_end = quantize("dq_end", tail[:, 4], BLOCK)
        y_passes(TAIL, BLOCK, w4q[0], columns_of(d_end, 0, BLOCK), False)
        join_h(tail[:, 1], TAIL, 1)
        for g in range(R_PASSES):
            h_end = quantize("hq_end%d" % g, tail[:, g], BLOCK)
            y_passes(TAIL, BLOCK, w3q[g], columns_of(h_end, 0, BLOCK), g == R_PASSES - 1)
